import numpy as np
import ml_dtypes


def mxq(x, axis, fmt="e4m3"):
    dtype, down = {"e4m3": (ml_dtypes.float8_e4m3fn, 7), "e5m2": (ml_dtypes.float8_e5m2, 14)}[fmt]
    v = np.moveaxis(np.asarray(x, np.float32).astype(ml_dtypes.bfloat16).astype(np.float64), axis, -1)
    blocks = v.reshape(v.shape[:-1] + (-1, 32))
    amax = np.abs(blocks).max(-1, keepdims=True)
    byte = np.maximum(np.where(amax > 0, np.frexp(amax)[1] - 1 + 127, 0) - down, 1)
    scale = np.exp2(byte - 127.0)
    codes = (blocks / scale).astype(np.float32).astype(dtype).astype(np.float64)
    return np.moveaxis((codes * scale).reshape(v.shape), -1, axis)


WIDE = False


def mx_kscale(k):
    if not WIDE:
        return np.ones(k)
    levels = np.array([10, -10, 5, -5, 0])
    if k % 512:
        return np.exp2(np.random.permutation(np.resize(levels, k // 32))).repeat(32)
    a = np.empty((k // 512, 16))
    for p in range(k // 512):
        a[p, :8] = np.random.permutation(np.resize(levels, 8))
        for g in range(8):
            far = levels[np.abs(levels - a[p, g]) >= 10]
            a[p, g + 8] = far[np.random.randint(len(far))]
    return np.exp2(a.ravel()).repeat(32)


def f64(x):
    return np.asarray(x).astype(np.float64)


def striped(idx):
    return np.tile(idx.reshape(-1, 16).T, (8, 1)).astype(np.uint16)


def unstriped(offs):
    return offs[:16].T.reshape(-1).astype(np.int64)


E2M1 = np.array([0.0, 0.5, 1.0, 1.5, 2.0, 3.0, 4.0, 6.0, -0.0, -0.5, -1.0, -1.5, -2.0, -3.0, -4.0, -6.0])


def pack_weight(w, fmt):
    k, n = w.shape
    w = f64(np.asarray(w, np.float32).astype(ml_dtypes.bfloat16)).reshape(k // 32, 32, n)
    amax = np.abs(w).max(1)
    if fmt == "e4m3":
        byte = np.frexp(amax)[1] - 1 + 127 - 7
    else:
        mant, ex = np.frexp(amax / 6.0)
        byte = np.where(mant > 0.5, ex, ex - 1) + 127
    byte = np.clip(np.where(amax > 0, byte, 1), 1, 254)
    scaled = (w * np.exp2(127.0 - byte)[:, None, :]).reshape(k, n).astype(np.float32)
    by_word = np.ascontiguousarray(scaled.reshape(k // 512, 128, 4, n).transpose(0, 1, 3, 2))
    if fmt == "e4m3":
        words = by_word.astype(ml_dtypes.float8_e4m3fn).view(np.uint8)
    else:
        c = by_word.astype(ml_dtypes.float4_e2m1fn).view(np.uint8) & 0xF
        words = (c[..., 0::2] | (c[..., 1::2] << 4)).reshape(k // 512, 128, 2 * n)
    return np.ascontiguousarray(words), np.ascontiguousarray(byte.astype(np.uint8).reshape(k // 512, 16, n))


def unpack_weight(words, scales, fmt):
    g, _, n = scales.shape
    words = np.ascontiguousarray(words).reshape(g, 128, n, -1)
    if fmt == "e4m3":
        vals = words.view(ml_dtypes.float8_e4m3fn).astype(np.float64)
    else:
        nib = np.empty((g, 128, n, 4), np.uint8)
        nib[..., 0::2] = words & 0xF
        nib[..., 1::2] = words >> 4
        vals = E2M1[nib]
    vals = vals * np.repeat(np.exp2(scales.astype(np.float64) - 127.0), 8, axis=1)[..., None]
    return vals.transpose(0, 1, 3, 2).reshape(g * 512, n)


def gelu(v):
    return 0.5 * v * (1.0 + np.tanh(np.sqrt(2.0 / np.pi) * (v + 0.044715 * v**3)))


def striped8(idx):
    return np.concatenate([v.reshape(-1, 16).T for v in idx]).astype(np.uint16)


def unstriped8(offs):
    return np.stack([offs[16 * g:16 * g + 16].T.reshape(-1) for g in range(8)]).astype(np.int64)


def runs(v, idx8):
    k = np.arange(v.shape[0])
    return v[k[:, None], idx8[k % 512 // 64]]


def put_heads(h, wgs, idx8, t2):
    r = np.arange(h.shape[0])
    page = np.zeros((h.shape[0], t2))
    page[r[:, None], idx8[r % 512 // 64]] = wgs[r // 4 % 128] * h
    return page


K, H, N, T, S, T2 = 512, 1024, 512, 2048, 1024, 2048

def setup_inputs():
    n = np.random.standard_normal
    s = mx_kscale(K)[:, None]
    u = mx_kscale(H)[:, None]
    tab_words, tab_scales = pack_weight(n((K, T)) * s, "e4m3")
    wa_words, wa_scales = pack_weight(n((K, H)) / np.sqrt(K) / s, "e2m1")
    wc_words, wc_scales = pack_weight(n((K, H)) / np.sqrt(K) / s * u.T, "e4m3")
    return {
        "tab_words": tab_words, "tab_scales": tab_scales,
        "offs": striped8(np.stack([np.random.permutation(T)[:S] for _ in range(8)])),
        "wa_words": wa_words, "wa_scales": wa_scales,
        "wb": (n((K, H)) / np.sqrt(K) / s).astype(np.float32),
        "wc_words": wc_words, "wc_scales": wc_scales,
        "gain": (np.exp(0.3 * n(H)) * u[:, 0]).astype(np.float32),
        "wd": (n((H, N)) / np.sqrt(H) / u).astype(np.float32),
        "wgo": np.repeat(np.random.uniform(0.5, 2.0, (8, S)), 16, axis=0).astype(np.float32),
        "offs2": striped8(np.stack([np.random.permutation(T2)[:S] for _ in range(8)])),
    }

def reference(tab_words, tab_scales, offs, wa_words, wa_scales, wb, wc_words, wc_scales, gain, wd, wgo, offs2):
    v = runs(unpack_weight(tab_words, tab_scales, "e4m3"), unstriped8(offs))
    a = unpack_weight(wa_words, wa_scales, "e2m1").T @ v
    b = mxq(f64(wb), 0, "e4m3").T @ v
    c = unpack_weight(wc_words, wc_scales, "e4m3").T @ v
    z = 1.0 / (1.0 + np.exp(-a))
    t = f64(gain)[:, None] * np.tanh(b)
    h = c + z * (t - c)
    y = mxq(f64(wd), 0, "e4m3").T @ mxq(h, 0, "e4m3")
    out = put_heads(y, f64(wgo), unstriped8(offs2), T2)
    return out

@@ -1,0 +1,288 @@
+from contextlib import ExitStack
+
+import concourse.mybir as mybir
+
+K, H, N, T, S, T2 = 512, 1024, 512, 2048, 1024, 2048
+FLOPS = 2 * S * (3 * K * H + H * N)
+
+F32 = mybir.dt.float32
+BF16 = mybir.dt.bfloat16
+I32 = mybir.dt.int32
+U32 = mybir.dt.uint32
+U16 = mybir.dt.uint16
+U8 = mybir.dt.uint8
+FP8X4 = mybir.dt.float8_e4m3fn_x4
+FP4X4 = mybir.dt.float4_e2m1fn_x4
+ALU = mybir.AluOpType
+ACT = mybir.ActivationFunctionType
+
+P = 128
+PACK = 4
+RUN = 8
+BLOCKS = P // RUN
+PASS = P * PACK
+PASSES = H // PASS
+HALF = 512
+HALVES = S // HALF
+GATE_N = 256
+LIN_N = 128
+LAG = 2
+
+
+def tile_list_motet_voice_completion_kernel(
+    tc, tab_words, tab_scales, offs, wa_words, wa_scales, wb, wc_words, wc_scales, gain, wd, wgo, offs2, out
+):
+    nc = tc.nc
+    with ExitStack() as ctx:
+        keep = ctx.enter_context(tc.tile_pool(name="keep", bufs=1))
+        ring = ctx.enter_context(tc.tile_pool(name="ring", bufs=2))
+        psum = ctx.enter_context(tc.psum_pool(name="psum", bufs=4))
+
+        offs_sb = keep.tile([P, S // 16], U16, name="offs_sb")
+        nc.sync.dma_start(offs_sb[:], offs)
+        tab_bytes = keep.tile([P, T], U8, name="tab_bytes", align_bytes=64)
+        nc.sync.dma_start(
+            tab_bytes[:].bitcast(I32),
+            tab_scales[0].bitcast(I32).unsqueeze(1).broadcast_to([BLOCKS, RUN, T // 4]),
+        )
+        raw_scales = keep.tile([P, 2, H], U8, name="raw_scales", align_bytes=64)
+        for slot, scales in enumerate((wa_scales, wc_scales)):
+            rows = scales[0].bitcast(I32).unsqueeze(1).broadcast_to([BLOCKS, RUN, H // 4])
+            nc.sync.dma_start(raw_scales[:, slot, :].bitcast(I32), rows)
+
+        wb_rows = wb.rearrange("(p j) c -> p j c", j=PACK)
+        wa_rows = wa_words[0].bitcast(I32)
+        wc_rows = wc_words[0].rearrange("p e i -> p (e i)").bitcast(I32)
+        wb_raw, wa_raw, wc_raw = {}, {}, {}
+
+        def load_first_weights(b, wb_tiles, wc_tile, wa_tile):
+            for u in range(2):
+                wb_raw[b, u] = wb_tiles[u]
+                c0 = b * PASS + u * PASS // 2
+                nc.sync.dma_start(wb_tiles[u], wb_rows[:, :, c0 : c0 + PASS // 2])
+            if b == 0:
+                nc.sync.dma_start(tab[:].bitcast(I32), tab_words[0].rearrange("p t i -> p (t i)").bitcast(I32))
+            wc_raw[b], wa_raw[b] = wc_tile, wa_tile
+            nc.sync.dma_start(wc_tile, wc_rows[:, b * PASS : (b + 1) * PASS])
+            nc.sync.dma_start(wa_tile, wa_rows[:, b * PASS // 2 : (b + 1) * PASS // 2])
+
+        tab = keep.tile([P, T], U32, name="tab", align_bytes=64)
+        wb_first = [keep.tile([P, PACK, PASS // 2], F32, name="wb_first%d" % u) for u in range(2)]
+        wc_first = keep.tile([P, PASS], I32, name="wc_first")
+        wa_first = keep.tile([P, PASS // 2], I32, name="wa_first")
+        load_first_weights(0, [w[:] for w in wb_first], wc_first[:], wa_first[:])
+        gains = {}
+        gain_rows = gain.rearrange("(b q t i) -> b t q i", b=PASSES, t=PACK, i=RUN)
+        for b in range(PASSES):
+            for t in range(PACK):
+                gains[b, t] = keep.tile([P, 1], F32, name="gain%d%d" % (b, t))
+                nc.gpsimd.dma_start(gains[b, t][:], gain_rows[b, t].unsqueeze(2))
+        offs2_sb = keep.tile([P, S // 16], U16, name="offs2_sb")
+        nc.sync.dma_start(offs2_sb[:], offs2)
+
+        warm_in = keep.tile([P, 1], F32, name="warm_in")
+        warm_out = keep.tile([P, 1], F32, name="warm_out")
+        nc.vector.memset(warm_in[:], 0.0)
+        nc.scalar.activation(warm_out[:], warm_in[:], ACT.Sigmoid)
+        pages = []
+        for i in range(2):
+            page = keep.tile([P, T2], F32, name="page%d" % i)
+            nc.vector.memset(page[:], 0.0)
+            pages.append(page)
+
+        v_bytes = keep.tile([P, S], U8, name="v_bytes", align_bytes=64)
+        nc.vector.tensor_copy(v_bytes[:], tab_bytes[:].indirect(offs_sb[:]))
+        planes = keep.tile([P, 2 * H + S], U8, name="planes", align_bytes=64)
+        w_scales = planes[:, : 2 * H].rearrange("p (s c) -> p s c", s=2)
+        v_plane = planes[:, 2 * H :]
+        nc.vector.tensor_copy(
+            planes[:, : 2 * H].bitcast(I32).rearrange("p (g t q w) -> p g t q w", t=PACK, q=BLOCKS, w=RUN // 4),
+            raw_scales[:].rearrange("p s c -> p (s c)").bitcast(I32).rearrange(
+                "p (g q t w) -> p g t q w", t=PACK, q=BLOCKS, w=RUN // 4
+            ),
+        )
+        nc.vector.tensor_copy(v_plane.bitcast(I32), v_bytes[:].bitcast(I32))
+        for r in range(1, 4):
+            nc.scalar.dma_start(planes[r:P:32, :].bitcast(I32), planes[RUN * r : P : 32, :].bitcast(I32))
+
+        wb_second = keep.tile([P, 2, PACK, PASS // 2], F32, name="wb_second", tag="raw_scales", align_bytes=64)
+        words_second = keep.tile([P, PASS + PASS // 2], I32, name="words_second", tag="tab_bytes", align_bytes=64)
+        load_first_weights(1, [wb_second[:, u] for u in range(2)], words_second[:, :PASS], words_second[:, PASS:])
+        second = keep.tile([P, PASSES * PACK * N + S], F32, name="second", tag="v_bytes", align_bytes=64)
+        wd_rows = wd.rearrange("(b q t i) n -> b t q i n", b=PASSES, t=PACK, i=RUN)
+        wd_raw = second[:, : PASSES * PACK * N].rearrange("p (b t n) -> p b t n", b=PASSES, t=PACK)
+        for b in range(PASSES):
+            for t in range(PACK):
+                nc.sync.dma_start(wd_raw[:, b, t, :], wd_rows[b, t])
+        wgo_sb = second[:, PASSES * PACK * N :]
+        nc.sync.dma_start(wgo_sb, wgo)
+
+        def reorder(raw, name):
+            codes = keep.tile(list(raw.shape), I32, name=name, align_bytes=64)
+            nc.vector.tensor_copy(
+                codes[:].rearrange("p (t q w) -> p t q w", t=PACK, q=BLOCKS),
+                raw.rearrange("p (q t w) -> p t q w", t=PACK, q=BLOCKS),
+            )
+            return codes
+
+        def gather_words(half):
+            words = keep.tile([P, HALF], U32, name="v_words%d" % half, align_bytes=64)
+            nc.vector.tensor_copy(words[:], tab[:].indirect(offs_sb[:, half * HALF // 16 : (half + 1) * HALF // 16]))
+            return words
+
+        def first_weights(b):
+            grouped = ring.tile([P, PACK, BLOCKS, RUN, PACK], BF16, name="wb_grouped", align_bytes=64)
+            qs = BLOCKS // 2
+            for u in range(2):
+                nc.scalar.copy(
+                    grouped[:, :, u * qs : (u + 1) * qs].rearrange("p t q i j -> p t q j i"),
+                    wb_raw[b, u].rearrange("p j (q t i) -> p t q j i", t=PACK, i=RUN),
+                )
+            wb_codes = keep.tile([P, PASS], U32, name="wb_codes%d" % b, align_bytes=64)
+            wb_plane = keep.tile([P, PASS], U8, name="wb_plane%d" % b, align_bytes=64)
+            nc.vector.quantize_mx(
+                out=wb_codes[:].bitcast(FP8X4),
+                scales=wb_plane[:],
+                in_=grouped[:].rearrange("p t q i j -> p (t q i j)"),
+            )
+            return wb_codes, wb_plane
+
+        h_bf = [keep.tile([P, PASSES, HALF, PACK], BF16, name="h_bf%d" % half, align_bytes=64) for half in range(HALVES)]
+
+        def gates(b, half, j0, words, wb_mx, wa_codes):
+            wb_codes, wb_plane = wb_mx
+            rhs = words[:, j0 : j0 + GATE_N].bitcast(FP8X4)
+            rhs_scale = v_plane[:, half * HALF + j0 : half * HALF + j0 + GATE_N]
+            tb = ring.tile([P, PACK, GATE_N], F32, name="tb")
+            z = ring.tile([P, PACK, GATE_N], F32, name="z")
+            for t0 in range(0, PACK, 2):
+                bank = psum.tile([P, 2, GATE_N], F32, name="bank_b", tag="scalar_bank")
+                for t in range(t0, t0 + 2):
+                    nc.tensor.matmul_mx(
+                        out=bank[:, t - t0, :],
+                        lhsT=wb_codes[:, t * P : (t + 1) * P].bitcast(FP8X4),
+                        lhsT_scale=wb_plane[:, t * P : (t + 1) * P],
+                        rhs=rhs, rhs_scale=rhs_scale, start=True, stop=True,
+                    )
+                nc.scalar.activation(tb[:, t0 : t0 + 2, :], bank[:], ACT.Tanh)
+            for t0 in range(0, PACK, 2):
+                bank = psum.tile([P, 2, GATE_N], F32, name="bank_a", tag="scalar_bank")
+                for t in range(t0, t0 + 2):
+                    c0 = b * PASS + t * P
+                    nc.tensor.matmul_mx(
+                        out=bank[:, t - t0, :],
+                        lhsT=wa_codes[:].bitcast(U8)[:, 2 * t * P : 2 * (t + 1) * P].bitcast(FP4X4),
+                        lhsT_scale=w_scales[:, 0, c0 : c0 + P],
+                        rhs=rhs, rhs_scale=rhs_scale, start=True, stop=True,
+                    )
+                nc.scalar.activation(z[:, t0 : t0 + 2, :], bank[:], ACT.Sigmoid)
+            return tb, z
+
+        def difference(b, half, j0, words, wc_codes, tb_cols, z_cols, last):
+            bank = psum.tile([P, PACK, LIN_N], F32, name="bank_c")
+            for t in range(PACK):
+                c0 = b * PASS + t * P
+                nc.tensor.matmul_mx(
+                    out=bank[:, t, :],
+                    lhsT=wc_codes[:, t * P : (t + 1) * P].bitcast(FP8X4),
+                    lhsT_scale=w_scales[:, 1, c0 : c0 + P],
+                    rhs=words[:, j0 : j0 + LIN_N].bitcast(FP8X4),
+                    rhs_scale=v_plane[:, half * HALF + j0 : half * HALF + j0 + LIN_N],
+                    start=True, stop=True,
+                )
+            d = ring.tile([P, PACK, LIN_N], F32, name="d", bufs=LAG + 1)
+            for t in range(PACK):
+                nc.vector.scalar_tensor_tensor(
+                    d[:, t, :], tb_cols[:, t, :], gains[b, t][:], bank[:, t, :], ALU.mult, ALU.subtract
+                )
+            if last:
+                e = keep.tile([P, PACK, LIN_N], F32, name="e_last", tag="last_e_then_planes", align_bytes=64)
+            else:
+                e = ring.tile([P, PACK, LIN_N], F32, name="e", bufs=LAG + 1)
+            nc.gpsimd.tensor_tensor(e[:], d[:], z_cols, ALU.mult)
+            return b, half, j0, e, bank
+
+        def interpolate(b, half, j0, e, bank):
+            nc.vector.tensor_tensor(
+                h_bf[half][:, b, j0 : j0 + LIN_N, :].rearrange("p (c i) t -> p c t i", i=2),
+                e[:].rearrange("p t (c i) -> p c t i", i=2),
+                bank[:].rearrange("p t (c i) -> p c t i", i=2),
+                ALU.add,
+            )
+
+        v_words = {}
+        waiting = []
+        for b in range(PASSES):
+            wb_mx = first_weights(b)
+            for half in range(HALVES):
+                if half not in v_words:
+                    v_words[half] = gather_words(half)
+                if half == 0:
+                    wc_codes = reorder(wc_raw[b], "wc_codes%d" % b)
+                    wa_codes = reorder(wa_raw[b], "wa_codes%d" % b)
+                for g0 in range(0, HALF, GATE_N):
+                    tb, z = gates(b, half, g0, v_words[half], wb_mx, wa_codes)
+                    for l0 in range(0, GATE_N, LIN_N):
+                        last = b == PASSES - 1 and half == HALVES - 1 and g0 + l0 == HALF - LIN_N
+                        cols = slice(l0, l0 + LIN_N)
+                        waiting.append(
+                            difference(b, half, g0 + l0, v_words[half], wc_codes, tb[:, :, cols], z[:, :, cols], last)
+                        )
+                        if len(waiting) > LAG:
+                            interpolate(*waiting.pop(0))
+        for step in waiting:
+            interpolate(*step)
+
+        wd_grouped = keep.tile([P, PASSES, PACK, P, PACK], BF16, name="wd_grouped", align_bytes=64)
+        ms = P // 4
+        for b in range(PASSES):
+            for m0 in range(0, P, ms):
+                nc.scalar.copy(
+                    wd_grouped[:, b, :, m0 : m0 + ms, :].rearrange("p i m t -> p m t i"),
+                    wd_raw[:, b, :, PACK * m0 : PACK * (m0 + ms)].rearrange("p t (m i) -> p m t i", i=PACK),
+                )
+        late_planes = keep.tile([P, 1 + HALVES, H], U8, name="late_planes", tag="last_e_then_planes", align_bytes=64)
+        wd_codes = keep.tile([P, PASSES * N], U32, name="wd_codes", align_bytes=64)
+        nc.vector.quantize_mx(
+            out=wd_codes[:].bitcast(FP8X4),
+            scales=late_planes[:, 0, :],
+            in_=wd_grouped[:].rearrange("p b i m t -> p (b i m t)"),
+        )
+        y = {}
+        for half in range(HALVES):
+            h_codes = keep.tile([P, PASSES * HALF], U32, name="h_codes%d" % half, align_bytes=64)
+            nc.vector.quantize_mx(
+                out=h_codes[:].bitcast(FP8X4),
+                scales=late_planes[:, 1 + half, :],
+                in_=h_bf[half][:].rearrange("p b j t -> p (b j t)"),
+            )
+            for i in range(PACK):
+                bank = psum.tile([P, HALF], F32, name="bank_y", tag="scalar_bank")
+                for b in range(PASSES):
+                    w_cols = slice(b * N + i * P, b * N + (i + 1) * P)
+                    h_cols = slice(b * HALF, (b + 1) * HALF)
+                    nc.tensor.matmul_mx(
+                        out=bank[:],
+                        lhsT=wd_codes[:, w_cols].bitcast(FP8X4),
+                        lhsT_scale=late_planes[:, 0, w_cols],
+                        rhs=h_codes[:, h_cols].bitcast(FP8X4),
+                        rhs_scale=late_planes[:, 1 + half, h_cols],
+                        start=(b == 0), stop=(b == PASSES - 1),
+                    )
+                y[half, i] = keep.tile([P, HALF], F32, name="y%d%d" % (half, i))
+                nc.scalar.copy(y[half, i][:], bank[:])
+
+        out_rows = out.rearrange("(p i) c -> p i c", i=PACK)
+        for i in range(PACK):
+            for half in range(HALVES):
+                nc.vector.tensor_tensor(
+                    pages[i][:].indirect(offs2_sb[:, half * HALF // 16 : (half + 1) * HALF // 16]),
+                    y[half, i][:],
+                    wgo_sb[:, half * HALF : (half + 1) * HALF],
+                    ALU.mult,
+                )
+                if i == 0:
+                    page = keep.tile([P, T2], F32, name="page%d" % (2 + half), tag="y%d0" % half)
+                    nc.gpsimd.memset(page[:], 0.0)
+                    pages.append(page)
+            nc.sync.dma_start(out_rows[:, i, :], pages[i][:])

@@ -1,6 +1,7 @@
 from contextlib import ExitStack
 
 import concourse.mybir as mybir
+from concourse.masks import make_identity
 
 K, H, N, T, S, T2 = 512, 1024, 512, 2048, 1024, 2048
 FLOPS = 2 * S * (3 * K * H + H * N)
@@ -45,6 +46,8 @@ def tile_list_motet_voice_completion_kernel(
             tab_bytes[:].bitcast(I32),
             tab_scales[0].bitcast(I32).unsqueeze(1).broadcast_to([BLOCKS, RUN, T // 4]),
         )
+        offs2_sb = keep.tile([P, S // 16], U16, name="offs2_sb")
+        nc.sync.dma_start(offs2_sb[:], offs2)
         raw_scales = keep.tile([P, 2, H], U8, name="raw_scales", align_bytes=64)
         for slot, scales in enumerate((wa_scales, wc_scales)):
             rows = scales[0].bitcast(I32).unsqueeze(1).broadcast_to([BLOCKS, RUN, H // 4])
@@ -55,66 +58,81 @@ def tile_list_motet_voice_completion_kernel(
         wc_rows = wc_words[0].rearrange("p e i -> p (e i)").bitcast(I32)
         wb_raw, wa_raw, wc_raw = {}, {}, {}
 
-        def load_first_weights(b, wb_tiles, wc_tile, wa_tile):
-            for u in range(2):
-                wb_raw[b, u] = wb_tiles[u]
-                c0 = b * PASS + u * PASS // 2
-                nc.sync.dma_start(wb_tiles[u], wb_rows[:, :, c0 : c0 + PASS // 2])
-            if b == 0:
-                nc.sync.dma_start(tab[:].bitcast(I32), tab_words[0].rearrange("p t i -> p (t i)").bitcast(I32))
+        def load_wb(b, tiles):
+            wb_raw[b] = tiles
+            width = PASS // len(tiles)
+            for u, piece in enumerate(tiles):
+                c0 = b * PASS + u * width
+                nc.sync.dma_start(piece, wb_rows[:, :, c0 : c0 + width])
+
+        def load_words(b, wc_tile, wa_tile):
             wc_raw[b], wa_raw[b] = wc_tile, wa_tile
             nc.sync.dma_start(wc_tile, wc_rows[:, b * PASS : (b + 1) * PASS])
             nc.sync.dma_start(wa_tile, wa_rows[:, b * PASS // 2 : (b + 1) * PASS // 2])
 
         tab = keep.tile([P, T], U32, name="tab", align_bytes=64)
-        wb_first = [keep.tile([P, PACK, PASS // 2], F32, name="wb_first%d" % u) for u in range(2)]
-        wc_first = keep.tile([P, PASS], I32, name="wc_first")
-        wa_first = keep.tile([P, PASS // 2], I32, name="wa_first")
-        load_first_weights(0, [w[:] for w in wb_first], wc_first[:], wa_first[:])
-        gains = {}
-        gain_rows = gain.rearrange("(b q t i) -> b t q i", b=PASSES, t=PACK, i=RUN)
+        nc.sync.dma_start(tab[:].bitcast(I32), tab_words[0].rearrange("p t i -> p (t i)").bitcast(I32))
+        wb_first = [keep.tile([P, PACK, PASS // 4], F32, name="wb_first%d" % u) for u in range(4)]
+        load_wb(0, [w[:] for w in wb_first])
+        planes = keep.tile([P, 2 * H + S], U8, name="planes", align_bytes=64)
+        nc.gpsimd.memset(planes[:].bitcast(I32), 0)
+        block_gains = keep.tile([P, PASSES, PACK * RUN], F32, name="block_gains")
+        gain_rows = gain.rearrange("(b q c) -> b q c", b=PASSES, q=BLOCKS)
         for b in range(PASSES):
-            for t in range(PACK):
-                gains[b, t] = keep.tile([P, 1], F32, name="gain%d%d" % (b, t))
-                nc.gpsimd.dma_start(gains[b, t][:], gain_rows[b, t].unsqueeze(2))
-        offs2_sb = keep.tile([P, S // 16], U16, name="offs2_sb")
-        nc.sync.dma_start(offs2_sb[:], offs2)
+            nc.gpsimd.dma_start(block_gains[:, b, :], gain_rows[b].unsqueeze(1).broadcast_to([BLOCKS, RUN, PACK * RUN]))
+        identity = keep.tile([P, P], F32, name="identity")
+        make_identity(nc, identity[:])
 
         warm_in = keep.tile([P, 1], F32, name="warm_in")
         warm_out = keep.tile([P, 1], F32, name="warm_out")
         nc.vector.memset(warm_in[:], 0.0)
         nc.scalar.activation(warm_out[:], warm_in[:], ACT.Sigmoid)
-        pages = []
-        for i in range(2):
-            page = keep.tile([P, T2], F32, name="page%d" % i)
-            nc.vector.memset(page[:], 0.0)
-            pages.append(page)
+        pages = [keep.tile([P, T2], F32, name="page0")]
+        nc.vector.memset(pages[0][:].bitcast(I32), 0)
+
+        w_scales = planes[:, : 2 * H].rearrange("p (s c) -> p s c", s=2)
+        v_plane = planes[:, 2 * H :]
 
         v_bytes = keep.tile([P, S], U8, name="v_bytes", align_bytes=64)
         nc.vector.tensor_copy(v_bytes[:], tab_bytes[:].indirect(offs_sb[:]))
-        planes = keep.tile([P, 2 * H + S], U8, name="planes", align_bytes=64)
-        w_scales = planes[:, : 2 * H].rearrange("p (s c) -> p s c", s=2)
-        v_plane = planes[:, 2 * H :]
+        staged = keep.tile([P, 2 * H + S], U8, name="staged", align_bytes=64)
         nc.vector.tensor_copy(
-            planes[:, : 2 * H].bitcast(I32).rearrange("p (g t q w) -> p g t q w", t=PACK, q=BLOCKS, w=RUN // 4),
+            staged[:, : 2 * H].bitcast(I32).rearrange("p (g t q w) -> p g t q w", t=PACK, q=BLOCKS, w=RUN // 4),
             raw_scales[:].rearrange("p s c -> p (s c)").bitcast(I32).rearrange(
                 "p (g q t w) -> p g t q w", t=PACK, q=BLOCKS, w=RUN // 4
             ),
         )
-        nc.vector.tensor_copy(v_plane.bitcast(I32), v_bytes[:].bitcast(I32))
-        for r in range(1, 4):
-            nc.scalar.dma_start(planes[r:P:32, :].bitcast(I32), planes[RUN * r : P : 32, :].bitcast(I32))
+        nc.vector.tensor_copy(staged[:, 2 * H :].bitcast(I32), v_bytes[:].bitcast(I32))
+        for r in range(4):
+            nc.sync.dma_start(planes[r:P:32, :].bitcast(I32), staged[RUN * r : P : 32, :].bitcast(I32))
+        words_first = keep.tile([P, PASS + PASS // 2], I32, name="words_first", tag="v_bytes", align_bytes=64)
+        load_words(0, words_first[:, :PASS], words_first[:, PASS:])
 
-        wb_second = keep.tile([P, 2, PACK, PASS // 2], F32, name="wb_second", tag="raw_scales", align_bytes=64)
-        words_second = keep.tile([P, PASS + PASS // 2], I32, name="words_second", tag="tab_bytes", align_bytes=64)
-        load_first_weights(1, [wb_second[:, u] for u in range(2)], words_second[:, :PASS], words_second[:, PASS:])
-        second = keep.tile([P, PASSES * PACK * N + S], F32, name="second", tag="v_bytes", align_bytes=64)
+        own_row = keep.tile([P, RUN], F32, name="own_row")
+        nc.vector.tensor_reduce(
+            own_row[:], identity[:].rearrange("p (q i) -> p i q", i=RUN), mybir.AxisListType.X, ALU.add
+        )
+        masked = keep.tile([P, PASSES * PACK, RUN], F32, name="masked")
+        nc.vector.tensor_tensor(
+            masked[:],
+            block_gains[:].rearrange("p b (t i) -> p (b t) i", i=RUN),
+            own_row[:].unsqueeze(1).broadcast_to([P, PASSES * PACK, RUN]),
+            ALU.mult,
+        )
+        gains = keep.tile([P, PASSES * PACK], F32, name="gains")
+        nc.vector.tensor_reduce(gains[:], masked[:], mybir.AxisListType.X, ALU.add)
+
+        widths = [PACK * PASS // 2, PACK * PASS // 2, PASSES * PACK * N, S]
+        late = keep.tile([P, sum(widths)], F32, name="late", tag="staged", align_bytes=64)
+        parts = [late[:, sum(widths[:n]) : sum(widths[: n + 1])] for n in range(len(widths))]
+        wb_second = [part.rearrange("p (j c) -> p j c", j=PACK) for part in parts[:2]]
+        load_wb(1, wb_second)
         wd_rows = wd.rearrange("(b q t i) n -> b t q i n", b=PASSES, t=PACK, i=RUN)
-        wd_raw = second[:, : PASSES * PACK * N].rearrange("p (b t n) -> p b t n", b=PASSES, t=PACK)
+        wd_raw = parts[2].rearrange("p (b t n) -> p b t n", b=PASSES, t=PACK)
         for b in range(PASSES):
             for t in range(PACK):
                 nc.sync.dma_start(wd_raw[:, b, t, :], wd_rows[b, t])
-        wgo_sb = second[:, PASSES * PACK * N :]
+        wgo_sb = parts[3]
         nc.sync.dma_start(wgo_sb, wgo)
 
         def reorder(raw, name):
@@ -125,18 +143,18 @@ def tile_list_motet_voice_completion_kernel(
             )
             return codes
 
-        def gather_words(half):
-            words = keep.tile([P, HALF], U32, name="v_words%d" % half, align_bytes=64)
-            nc.vector.tensor_copy(words[:], tab[:].indirect(offs_sb[:, half * HALF // 16 : (half + 1) * HALF // 16]))
+        def gather_words(j0):
+            words = keep.tile([P, GATE_N], U32, name="v_words%d" % j0, align_bytes=64)
+            nc.vector.tensor_copy(words[:], tab[:].indirect(offs_sb[:, j0 // 16 : (j0 + GATE_N) // 16]))
             return words
 
         def first_weights(b):
             grouped = ring.tile([P, PACK, BLOCKS, RUN, PACK], BF16, name="wb_grouped", align_bytes=64)
-            qs = BLOCKS // 2
-            for u in range(2):
+            qs = BLOCKS // len(wb_raw[b])
+            for u, piece in enumerate(wb_raw[b]):
                 nc.scalar.copy(
                     grouped[:, :, u * qs : (u + 1) * qs].rearrange("p t q i j -> p t q j i"),
-                    wb_raw[b, u].rearrange("p j (q t i) -> p t q j i", t=PACK, i=RUN),
+                    piece.rearrange("p j (q t i) -> p t q j i", t=PACK, i=RUN),
                 )
             wb_codes = keep.tile([P, PASS], U32, name="wb_codes%d" % b, align_bytes=64)
             wb_plane = keep.tile([P, PASS], U8, name="wb_plane%d" % b, align_bytes=64)
@@ -151,7 +169,7 @@ def tile_list_motet_voice_completion_kernel(
 
         def gates(b, half, j0, words, wb_mx, wa_codes):
             wb_codes, wb_plane = wb_mx
-            rhs = words[:, j0 : j0 + GATE_N].bitcast(FP8X4)
+            rhs = words[:].bitcast(FP8X4)
             rhs_scale = v_plane[:, half * HALF + j0 : half * HALF + j0 + GATE_N]
             tb = ring.tile([P, PACK, GATE_N], F32, name="tb")
             z = ring.tile([P, PACK, GATE_N], F32, name="z")
@@ -178,7 +196,7 @@ def tile_list_motet_voice_completion_kernel(
                 nc.scalar.activation(z[:, t0 : t0 + 2, :], bank[:], ACT.Sigmoid)
             return tb, z
 
-        def difference(b, half, j0, words, wc_codes, tb_cols, z_cols, last):
+        def difference(b, half, j0, words, wc_codes, tb_cols, z_cols, left):
             bank = psum.tile([P, PACK, LIN_N], F32, name="bank_c")
             for t in range(PACK):
                 c0 = b * PASS + t * P
@@ -186,62 +204,67 @@ def tile_list_motet_voice_completion_kernel(
                     out=bank[:, t, :],
                     lhsT=wc_codes[:, t * P : (t + 1) * P].bitcast(FP8X4),
                     lhsT_scale=w_scales[:, 1, c0 : c0 + P],
-                    rhs=words[:, j0 : j0 + LIN_N].bitcast(FP8X4),
+                    rhs=words[:, j0 % GATE_N : j0 % GATE_N + LIN_N].bitcast(FP8X4),
                     rhs_scale=v_plane[:, half * HALF + j0 : half * HALF + j0 + LIN_N],
                     start=True, stop=True,
                 )
-            d = ring.tile([P, PACK, LIN_N], F32, name="d", bufs=LAG + 1)
+            if left == 1:
+                d = keep.tile([P, PACK, LIN_N], F32, name="d_last_gpsimd", tag="d_then_planes", align_bytes=64)
+            else:
+                d = ring.tile([P, PACK, LIN_N], F32, name="d", bufs=LAG + 1)
             for t in range(PACK):
                 nc.vector.scalar_tensor_tensor(
-                    d[:, t, :], tb_cols[:, t, :], gains[b, t][:], bank[:, t, :], ALU.mult, ALU.subtract
+                    d[:, t, :], tb_cols[:, t, :], gains[:, b * PACK + t : b * PACK + t + 1], bank[:, t, :], ALU.mult, ALU.subtract
                 )
-            if last:
-                e = keep.tile([P, PACK, LIN_N], F32, name="e_last", tag="last_e_then_planes", align_bytes=64)
-            else:
-                e = ring.tile([P, PACK, LIN_N], F32, name="e", bufs=LAG + 1)
-            nc.gpsimd.tensor_tensor(e[:], d[:], z_cols, ALU.mult)
+            e = ring.tile([P, PACK, LIN_N], F32, name="e", bufs=LAG + 1)
+            (nc.vector if left == 0 else nc.gpsimd).tensor_tensor(e[:], d[:], z_cols, ALU.mult)
             return b, half, j0, e, bank
 
         def interpolate(b, half, j0, e, bank):
             nc.vector.tensor_tensor(
-                h_bf[half][:, b, j0 : j0 + LIN_N, :].rearrange("p (c i) t -> p c t i", i=2),
-                e[:].rearrange("p t (c i) -> p c t i", i=2),
-                bank[:].rearrange("p t (c i) -> p c t i", i=2),
+                h_bf[half][:, b, j0 : j0 + LIN_N, :].rearrange("p (c i) t -> p c t i", i=4),
+                e[:].rearrange("p t (c i) -> p c t i", i=4),
+                bank[:].rearrange("p t (c i) -> p c t i", i=4),
                 ALU.add,
             )
 
-        v_words = {}
+        v_words = {j0: gather_words(j0) for j0 in range(0, S, GATE_N)}
+        wb_mx = first_weights(0)
+        wc_codes = reorder(wc_raw[0], "wc_codes0")
+        wa_codes = reorder(wa_raw[0], "wa_codes0")
+        words_second = keep.tile([P, PASS + PASS // 2], I32, name="words_second", tag="tab", align_bytes=64)
+        load_words(1, words_second[:, :PASS], words_second[:, PASS:])
         waiting = []
         for b in range(PASSES):
-            wb_mx = first_weights(b)
+            if b > 0:
+                wb_mx = first_weights(b)
+                wc_codes = reorder(wc_raw[b], "wc_codes%d" % b)
+                wa_codes = reorder(wa_raw[b], "wa_codes%d" % b)
             for half in range(HALVES):
-                if half not in v_words:
-                    v_words[half] = gather_words(half)
-                if half == 0:
-                    wc_codes = reorder(wc_raw[b], "wc_codes%d" % b)
-                    wa_codes = reorder(wa_raw[b], "wa_codes%d" % b)
                 for g0 in range(0, HALF, GATE_N):
-                    tb, z = gates(b, half, g0, v_words[half], wb_mx, wa_codes)
+                    words = v_words[half * HALF + g0]
+                    tb, z = gates(b, half, g0, words, wb_mx, wa_codes)
                     for l0 in range(0, GATE_N, LIN_N):
-                        last = b == PASSES - 1 and half == HALVES - 1 and g0 + l0 == HALF - LIN_N
+                        left = ((PASSES - b) * S - half * HALF - g0 - l0) // LIN_N - 1
                         cols = slice(l0, l0 + LIN_N)
                         waiting.append(
-                            difference(b, half, g0 + l0, v_words[half], wc_codes, tb[:, :, cols], z[:, :, cols], last)
+                            difference(b, half, g0 + l0, words, wc_codes, tb[:, :, cols], z[:, :, cols], left)
                         )
                         if len(waiting) > LAG:
                             interpolate(*waiting.pop(0))
-        for step in waiting:
-            interpolate(*step)
 
         wd_grouped = keep.tile([P, PASSES, PACK, P, PACK], BF16, name="wd_grouped", align_bytes=64)
         ms = P // 4
-        for b in range(PASSES):
-            for m0 in range(0, P, ms):
-                nc.scalar.copy(
-                    wd_grouped[:, b, :, m0 : m0 + ms, :].rearrange("p i m t -> p m t i"),
-                    wd_raw[:, b, :, PACK * m0 : PACK * (m0 + ms)].rearrange("p t (m i) -> p m t i", i=PACK),
-                )
-        late_planes = keep.tile([P, 1 + HALVES, H], U8, name="late_planes", tag="last_e_then_planes", align_bytes=64)
+        for i in range(PACK):
+            nc.gpsimd.tensor_scalar(
+                wd_grouped[:, 0, i], wd_raw[:, 0].rearrange("p t (m i) -> p i m t", i=PACK)[:, i], 1.0, 0.0, ALU.mult, ALU.add
+            )
+        for m0 in range(0, P, ms):
+            nc.scalar.copy(
+                wd_grouped[:, 1, :, m0 : m0 + ms, :].rearrange("p i m t -> p m t i"),
+                wd_raw[:, 1, :, PACK * m0 : PACK * (m0 + ms)].rearrange("p t (m i) -> p m t i", i=PACK),
+            )
+        late_planes = keep.tile([P, 1 + HALVES, H], U8, name="late_planes", tag="d_then_planes", align_bytes=64)
         wd_codes = keep.tile([P, PASSES * N], U32, name="wd_codes", align_bytes=64)
         nc.vector.quantize_mx(
             out=wd_codes[:].bitcast(FP8X4),
@@ -249,7 +272,8 @@ def tile_list_motet_voice_completion_kernel(
             in_=wd_grouped[:].rearrange("p b i m t -> p (b i m t)"),
         )
         y = {}
-        for half in range(HALVES):
+
+        def projection(half):
             h_codes = keep.tile([P, PASSES * HALF], U32, name="h_codes%d" % half, align_bytes=64)
             nc.vector.quantize_mx(
                 out=h_codes[:].bitcast(FP8X4),
@@ -272,6 +296,11 @@ def tile_list_motet_voice_completion_kernel(
                 y[half, i] = keep.tile([P, HALF], F32, name="y%d%d" % (half, i))
                 nc.scalar.copy(y[half, i][:], bank[:])
 
+        projection(0)
+        for step in waiting:
+            interpolate(*step)
+        projection(1)
+
         out_rows = out.rearrange("(p i) c -> p i c", i=PACK)
         for i in range(PACK):
             for half in range(HALVES):
@@ -281,8 +310,8 @@ def tile_list_motet_voice_completion_kernel(
                     wgo_sb[:, half * HALF : (half + 1) * HALF],
                     ALU.mult,
                 )
-                if i == 0:
-                    page = keep.tile([P, T2], F32, name="page%d" % (2 + half), tag="y%d0" % half)
+                if len(pages) < PACK:
+                    page = keep.tile([P, T2], F32, name="page%d" % len(pages), tag="y%d%d" % (half, i))
                     nc.gpsimd.memset(page[:], 0.0)
                     pages.append(page)
             nc.sync.dma_start(out_rows[:, i, :], pages[i][:])

@@ -222,9 +222,9 @@ def tile_list_motet_voice_completion_kernel(
 
         def interpolate(b, half, j0, e, bank):
             nc.vector.tensor_tensor(
-                h_bf[half][:, b, j0 : j0 + LIN_N, :].rearrange("p (c i) t -> p c t i", i=4),
-                e[:].rearrange("p t (c i) -> p c t i", i=4),
-                bank[:].rearrange("p t (c i) -> p c t i", i=4),
+                h_bf[half][:, b, j0 : j0 + LIN_N, :].rearrange("p (c i) t -> p c t i", i=2),
+                e[:].rearrange("p t (c i) -> p c t i", i=2),
+                bank[:].rearrange("p t (c i) -> p c t i", i=2),
                 ALU.add,
             )
 
@@ -255,15 +255,12 @@ def tile_list_motet_voice_completion_kernel(
 
         wd_grouped = keep.tile([P, PASSES, PACK, P, PACK], BF16, name="wd_grouped", align_bytes=64)
         ms = P // 4
-        for i in range(PACK):
-            nc.gpsimd.tensor_scalar(
-                wd_grouped[:, 0, i], wd_raw[:, 0].rearrange("p t (m i) -> p i m t", i=PACK)[:, i], 1.0, 0.0, ALU.mult, ALU.add
-            )
-        for m0 in range(0, P, ms):
-            nc.scalar.copy(
-                wd_grouped[:, 1, :, m0 : m0 + ms, :].rearrange("p i m t -> p m t i"),
-                wd_raw[:, 1, :, PACK * m0 : PACK * (m0 + ms)].rearrange("p t (m i) -> p m t i", i=PACK),
-            )
+        for b in range(PASSES):
+            for m0 in range(0, P, ms):
+                nc.scalar.copy(
+                    wd_grouped[:, b, :, m0 : m0 + ms, :].rearrange("p i m t -> p m t i"),
+                    wd_raw[:, b, :, PACK * m0 : PACK * (m0 + ms)].rearrange("p t (m i) -> p m t i", i=PACK),
+                )
         late_planes = keep.tile([P, 1 + HALVES, H], U8, name="late_planes", tag="d_then_planes", align_bytes=64)
         wd_codes = keep.tile([P, PASSES * N], U32, name="wd_codes", align_bytes=64)
         nc.vector.quantize_mx(

@@ -87,8 +87,9 @@ def tile_list_motet_voice_completion_kernel(
         warm_out = keep.tile([P, 1], F32, name="warm_out")
         nc.vector.memset(warm_in[:], 0.0)
         nc.scalar.activation(warm_out[:], warm_in[:], ACT.Sigmoid)
-        pages = [keep.tile([P, T2], F32, name="page0")]
-        nc.vector.memset(pages[0][:].bitcast(I32), 0)
+        pages = [keep.tile([P, T2], F32, name="page%d" % n) for n in range(2)]
+        for page in pages:
+            nc.vector.memset(page[:].bitcast(I32), 0)
 
         w_scales = planes[:, : 2 * H].rearrange("p (s c) -> p s c", s=2)
         v_plane = planes[:, 2 * H :]
@@ -302,13 +303,9 @@ def tile_list_motet_voice_completion_kernel(
         for i in range(PACK):
             for half in range(HALVES):
                 nc.vector.tensor_tensor(
-                    pages[i][:].indirect(offs2_sb[:, half * HALF // 16 : (half + 1) * HALF // 16]),
+                    pages[i % 2][:].indirect(offs2_sb[:, half * HALF // 16 : (half + 1) * HALF // 16]),
                     y[half, i][:],
                     wgo_sb[:, half * HALF : (half + 1) * HALF],
                     ALU.mult,
                 )
-                if len(pages) < PACK:
-                    page = keep.tile([P, T2], F32, name="page%d" % len(pages), tag="y%d%d" % (half, i))
-                    nc.gpsimd.memset(page[:], 0.0)
-                    pages.append(page)
-            nc.sync.dma_start(out_rows[:, i, :], pages[i][:])
+            nc.sync.dma_start(out_rows[:, i, :], pages[i % 2][:])

@@ -46,17 +46,21 @@ def tile_list_motet_voice_completion_kernel(
             tab_bytes[:].bitcast(I32),
             tab_scales[0].bitcast(I32).unsqueeze(1).broadcast_to([BLOCKS, RUN, T // 4]),
         )
-        offs2_sb = keep.tile([P, S // 16], U16, name="offs2_sb")
-        nc.sync.dma_start(offs2_sb[:], offs2)
         raw_scales = keep.tile([P, 2, H], U8, name="raw_scales", align_bytes=64)
         for slot, scales in enumerate((wa_scales, wc_scales)):
             rows = scales[0].bitcast(I32).unsqueeze(1).broadcast_to([BLOCKS, RUN, H // 4])
             nc.sync.dma_start(raw_scales[:, slot, :].bitcast(I32), rows)
 
+        gain_rows = keep.tile([P, P], F32, name="gain_rows")
+        nc.gpsimd.memset(gain_rows[:], 0.0)
+        gain_src = gain.rearrange("(b q t i) -> b t q i", b=PASSES, t=PACK, i=RUN)
+        for b in range(PASSES):
+            nc.sync.dma_start(
+                gain_rows[b * PACK : (b + 1) * PACK, :].rearrange("t (q i) -> t q i", i=RUN), gain_src[b]
+            )
+
         wb_rows = wb.rearrange("(p j) c -> p j c", j=PACK)
-        wa_rows = wa_words[0].bitcast(I32)
-        wc_rows = wc_words[0].rearrange("p e i -> p (e i)").bitcast(I32)
-        wb_raw, wa_raw, wc_raw = {}, {}, {}
+        wb_raw = {}
 
         def load_wb(b, tiles):
             wb_raw[b] = tiles
@@ -65,21 +69,15 @@ def tile_list_motet_voice_completion_kernel(
                 c0 = b * PASS + u * width
                 nc.sync.dma_start(piece, wb_rows[:, :, c0 : c0 + width])
 
-        def load_words(b, wc_tile, wa_tile):
-            wc_raw[b], wa_raw[b] = wc_tile, wa_tile
-            nc.sync.dma_start(wc_tile, wc_rows[:, b * PASS : (b + 1) * PASS])
-            nc.sync.dma_start(wa_tile, wa_rows[:, b * PASS // 2 : (b + 1) * PASS // 2])
-
+        wb_first = [keep.tile([P, PACK, PASS // 2], F32, name="wb_first%d" % u) for u in range(2)]
+        load_wb(0, [w[:] for w in wb_first])
         tab = keep.tile([P, T], U32, name="tab", align_bytes=64)
         nc.sync.dma_start(tab[:].bitcast(I32), tab_words[0].rearrange("p t i -> p (t i)").bitcast(I32))
-        wb_first = [keep.tile([P, PACK, PASS // 4], F32, name="wb_first%d" % u) for u in range(4)]
-        load_wb(0, [w[:] for w in wb_first])
+
+        offs2_sb = keep.tile([P, S // 16], U16, name="offs2_sb")
+        nc.sync.dma_start(offs2_sb[:], offs2)
         planes = keep.tile([P, 2 * H + S], U8, name="planes", align_bytes=64)
         nc.gpsimd.memset(planes[:].bitcast(I32), 0)
-        block_gains = keep.tile([P, PASSES, PACK * RUN], F32, name="block_gains")
-        gain_rows = gain.rearrange("(b q c) -> b q c", b=PASSES, q=BLOCKS)
-        for b in range(PASSES):
-            nc.gpsimd.dma_start(block_gains[:, b, :], gain_rows[b].unsqueeze(1).broadcast_to([BLOCKS, RUN, PACK * RUN]))
         identity = keep.tile([P, P], F32, name="identity")
         make_identity(nc, identity[:])
 
@@ -91,43 +89,34 @@ def tile_list_motet_voice_completion_kernel(
         for page in pages:
             nc.vector.memset(page[:].bitcast(I32), 0)
 
+        gain_bank = psum.tile([P, P], F32, name="gain_bank", tag="scalar_bank")
+        nc.tensor.transpose(gain_bank[:], gain_rows[:], identity[:])
+        gains = keep.tile([P, PASSES * PACK], F32, name="gains")
+        nc.scalar.copy(gains[:], gain_bank[:, : PASSES * PACK])
+
         w_scales = planes[:, : 2 * H].rearrange("p (s c) -> p s c", s=2)
         v_plane = planes[:, 2 * H :]
 
         v_bytes = keep.tile([P, S], U8, name="v_bytes", align_bytes=64)
         nc.vector.tensor_copy(v_bytes[:], tab_bytes[:].indirect(offs_sb[:]))
         staged = keep.tile([P, 2 * H + S], U8, name="staged", align_bytes=64)
+        nc.vector.tensor_copy(staged[:, 2 * H :].bitcast(I32), v_bytes[:].bitcast(I32))
         nc.vector.tensor_copy(
             staged[:, : 2 * H].bitcast(I32).rearrange("p (g t q w) -> p g t q w", t=PACK, q=BLOCKS, w=RUN // 4),
             raw_scales[:].rearrange("p s c -> p (s c)").bitcast(I32).rearrange(
                 "p (g q t w) -> p g t q w", t=PACK, q=BLOCKS, w=RUN // 4
             ),
         )
-        nc.vector.tensor_copy(staged[:, 2 * H :].bitcast(I32), v_bytes[:].bitcast(I32))
         for r in range(4):
             nc.sync.dma_start(planes[r:P:32, :].bitcast(I32), staged[RUN * r : P : 32, :].bitcast(I32))
-        words_first = keep.tile([P, PASS + PASS // 2], I32, name="words_first", tag="v_bytes", align_bytes=64)
-        load_words(0, words_first[:, :PASS], words_first[:, PASS:])
 
-        own_row = keep.tile([P, RUN], F32, name="own_row")
-        nc.vector.tensor_reduce(
-            own_row[:], identity[:].rearrange("p (q i) -> p i q", i=RUN), mybir.AxisListType.X, ALU.add
-        )
-        masked = keep.tile([P, PASSES * PACK, RUN], F32, name="masked")
-        nc.vector.tensor_tensor(
-            masked[:],
-            block_gains[:].rearrange("p b (t i) -> p (b t) i", i=RUN),
-            own_row[:].unsqueeze(1).broadcast_to([P, PASSES * PACK, RUN]),
-            ALU.mult,
-        )
-        gains = keep.tile([P, PASSES * PACK], F32, name="gains")
-        nc.vector.tensor_reduce(gains[:], masked[:], mybir.AxisListType.X, ALU.add)
-
+        raw_words = keep.tile([P, H + H // 2], I32, name="raw_words", tag="v_bytes", align_bytes=64)
+        nc.sync.dma_start(raw_words[:, H:], wa_words[0].bitcast(I32))
+        nc.sync.dma_start(raw_words[:, :H], wc_words[0].rearrange("p e i -> p (e i)").bitcast(I32))
         widths = [PACK * PASS // 2, PACK * PASS // 2, PASSES * PACK * N, S]
-        late = keep.tile([P, sum(widths)], F32, name="late", tag="staged", align_bytes=64)
+        late = keep.tile([P, sum(widths)], F32, name="late", tag="raw_scales", align_bytes=64)
         parts = [late[:, sum(widths[:n]) : sum(widths[: n + 1])] for n in range(len(widths))]
-        wb_second = [part.rearrange("p (j c) -> p j c", j=PACK) for part in parts[:2]]
-        load_wb(1, wb_second)
+        load_wb(1, [part.rearrange("p (j c) -> p j c", j=PACK) for part in parts[:2]])
         wd_rows = wd.rearrange("(b q t i) n -> b t q i n", b=PASSES, t=PACK, i=RUN)
         wd_raw = parts[2].rearrange("p (b t n) -> p b t n", b=PASSES, t=PACK)
         for b in range(PASSES):
@@ -139,41 +128,47 @@ def tile_list_motet_voice_completion_kernel(
         def reorder(raw, name):
             codes = keep.tile(list(raw.shape), I32, name=name, align_bytes=64)
             nc.vector.tensor_copy(
-                codes[:].rearrange("p (t q w) -> p t q w", t=PACK, q=BLOCKS),
-                raw.rearrange("p (q t w) -> p t q w", t=PACK, q=BLOCKS),
+                codes[:].rearrange("p (b t q w) -> p b t q w", b=PASSES, t=PACK, q=BLOCKS),
+                raw.rearrange("p (b q t w) -> p b t q w", b=PASSES, t=PACK, q=BLOCKS),
             )
             return codes
 
-        def gather_words(j0):
-            words = keep.tile([P, GATE_N], U32, name="v_words%d" % j0, align_bytes=64)
-            nc.vector.tensor_copy(words[:], tab[:].indirect(offs_sb[:, j0 // 16 : (j0 + GATE_N) // 16]))
+        def gather_words(j0, width, tag):
+            words = keep.tile([P, width], U32, name="v_words%d" % j0, tag=tag, align_bytes=64)
+            nc.vector.tensor_copy(words[:], tab[:].indirect(offs_sb[:, j0 // 16 : (j0 + width) // 16]))
             return words
 
-        def first_weights(b):
-            grouped = ring.tile([P, PACK, BLOCKS, RUN, PACK], BF16, name="wb_grouped", align_bytes=64)
+        def round_wb(b):
+            grouped = keep.tile([P, PACK, BLOCKS, RUN, PACK], BF16, name="wb_grouped%d" % b, align_bytes=64)
             qs = BLOCKS // len(wb_raw[b])
             for u, piece in enumerate(wb_raw[b]):
-                nc.scalar.copy(
-                    grouped[:, :, u * qs : (u + 1) * qs].rearrange("p t q i j -> p t q j i"),
-                    piece.rearrange("p j (q t i) -> p t q j i", t=PACK, i=RUN),
-                )
-            wb_codes = keep.tile([P, PASS], U32, name="wb_codes%d" % b, align_bytes=64)
-            wb_plane = keep.tile([P, PASS], U8, name="wb_plane%d" % b, align_bytes=64)
-            nc.vector.quantize_mx(
-                out=wb_codes[:].bitcast(FP8X4),
-                scales=wb_plane[:],
-                in_=grouped[:].rearrange("p t q i j -> p (t q i j)"),
-            )
-            return wb_codes, wb_plane
+                for t0 in range(0, PACK, 2):
+                    nc.scalar.copy(
+                        grouped[:, t0 : t0 + 2, u * qs : (u + 1) * qs].rearrange("p t q i j -> p t q j i"),
+                        piece.rearrange("p j (q t i) -> p t q j i", t=PACK, i=RUN)[:, t0 : t0 + 2],
+                    )
+            return grouped
+
+        def quantise(grouped, width, name):
+            codes = keep.tile([P, width], U32, name=name + "_codes", align_bytes=64)
+            plane = keep.tile([P, width], U8, name=name + "_plane", align_bytes=64)
+            nc.vector.quantize_mx(out=codes[:].bitcast(FP8X4), scales=plane[:], in_=grouped)
+            return codes, plane
 
         h_bf = [keep.tile([P, PASSES, HALF, PACK], BF16, name="h_bf%d" % half, align_bytes=64) for half in range(HALVES)]
 
-        def gates(b, half, j0, words, wb_mx, wa_codes):
-            wb_codes, wb_plane = wb_mx
-            rhs = words[:].bitcast(FP8X4)
-            rhs_scale = v_plane[:, half * HALF + j0 : half * HALF + j0 + GATE_N]
-            tb = ring.tile([P, PACK, GATE_N], F32, name="tb")
-            z = ring.tile([P, PACK, GATE_N], F32, name="z")
+        def v_cols(j0, width):
+            if j0 < GATE_N:
+                words = v_first[:, j0 : j0 + width]
+            else:
+                words = v_rest[:, j0 - GATE_N : j0 - GATE_N + width]
+            return words.bitcast(FP8X4), v_plane[:, j0 : j0 + width]
+
+        def gates(b, j0):
+            wb_codes, wb_plane = wb_mx[b]
+            rhs, rhs_scale = v_cols(j0, GATE_N)
+            tb = ring.tile([P, PACK, GATE_N], F32, name="tb", bufs=3)
+            z = ring.tile([P, PACK, GATE_N], F32, name="z", bufs=3)
             for t0 in range(0, PACK, 2):
                 bank = psum.tile([P, 2, GATE_N], F32, name="bank_b", tag="scalar_bank")
                 for t in range(t0, t0 + 2):
@@ -190,122 +185,127 @@ def tile_list_motet_voice_completion_kernel(
                     c0 = b * PASS + t * P
                     nc.tensor.matmul_mx(
                         out=bank[:, t - t0, :],
-                        lhsT=wa_codes[:].bitcast(U8)[:, 2 * t * P : 2 * (t + 1) * P].bitcast(FP4X4),
+                        lhsT=wa_codes[:].bitcast(U8)[:, 2 * c0 : 2 * (c0 + P)].bitcast(FP4X4),
                         lhsT_scale=w_scales[:, 0, c0 : c0 + P],
                         rhs=rhs, rhs_scale=rhs_scale, start=True, stop=True,
                     )
                 nc.scalar.activation(z[:, t0 : t0 + 2, :], bank[:], ACT.Sigmoid)
             return tb, z
 
-        def difference(b, half, j0, words, wc_codes, tb_cols, z_cols, left):
+        def difference(b, j0, tb_cols, z_cols, last):
+            rhs, rhs_scale = v_cols(j0, LIN_N)
             bank = psum.tile([P, PACK, LIN_N], F32, name="bank_c")
             for t in range(PACK):
                 c0 = b * PASS + t * P
                 nc.tensor.matmul_mx(
                     out=bank[:, t, :],
-                    lhsT=wc_codes[:, t * P : (t + 1) * P].bitcast(FP8X4),
+                    lhsT=wc_codes[:, c0 : c0 + P].bitcast(FP8X4),
                     lhsT_scale=w_scales[:, 1, c0 : c0 + P],
-                    rhs=words[:, j0 % GATE_N : j0 % GATE_N + LIN_N].bitcast(FP8X4),
-                    rhs_scale=v_plane[:, half * HALF + j0 : half * HALF + j0 + LIN_N],
-                    start=True, stop=True,
+                    rhs=rhs, rhs_scale=rhs_scale, start=True, stop=True,
                 )
-            if left == 1:
-                d = keep.tile([P, PACK, LIN_N], F32, name="d_last_gpsimd", tag="d_then_planes", align_bytes=64)
-            else:
-                d = ring.tile([P, PACK, LIN_N], F32, name="d", bufs=LAG + 1)
+            d = ring.tile([P, PACK, LIN_N], F32, name="d", bufs=LAG + 1)
             for t in range(PACK):
                 nc.vector.scalar_tensor_tensor(
                     d[:, t, :], tb_cols[:, t, :], gains[:, b * PACK + t : b * PACK + t + 1], bank[:, t, :], ALU.mult, ALU.subtract
                 )
             e = ring.tile([P, PACK, LIN_N], F32, name="e", bufs=LAG + 1)
-            (nc.vector if left == 0 else nc.gpsimd).tensor_tensor(e[:], d[:], z_cols, ALU.mult)
-            return b, half, j0, e, bank
+            (nc.vector if last else nc.gpsimd).tensor_tensor(e[:], d[:], z_cols, ALU.mult)
+            return b, j0, e, bank
 
-        def interpolate(b, half, j0, e, bank):
+        def interpolate(b, j0, e, bank):
             nc.vector.tensor_tensor(
-                h_bf[half][:, b, j0 : j0 + LIN_N, :].rearrange("p (c i) t -> p c t i", i=2),
+                h_bf[j0 // HALF][:, b, j0 % HALF : j0 % HALF + LIN_N, :].rearrange("p (c i) t -> p c t i", i=2),
                 e[:].rearrange("p t (c i) -> p c t i", i=2),
                 bank[:].rearrange("p t (c i) -> p c t i", i=2),
                 ALU.add,
             )
 
-        v_words = {j0: gather_words(j0) for j0 in range(0, S, GATE_N)}
-        wb_mx = first_weights(0)
-        wc_codes = reorder(wc_raw[0], "wc_codes0")
-        wa_codes = reorder(wa_raw[0], "wa_codes0")
-        words_second = keep.tile([P, PASS + PASS // 2], I32, name="words_second", tag="tab", align_bytes=64)
-        load_words(1, words_second[:, :PASS], words_second[:, PASS:])
-        waiting = []
-        for b in range(PASSES):
-            if b > 0:
-                wb_mx = first_weights(b)
-                wc_codes = reorder(wc_raw[b], "wc_codes%d" % b)
-                wa_codes = reorder(wa_raw[b], "wa_codes%d" % b)
-            for half in range(HALVES):
-                for g0 in range(0, HALF, GATE_N):
-                    words = v_words[half * HALF + g0]
-                    tb, z = gates(b, half, g0, words, wb_mx, wa_codes)
-                    for l0 in range(0, GATE_N, LIN_N):
-                        left = ((PASSES - b) * S - half * HALF - g0 - l0) // LIN_N - 1
-                        cols = slice(l0, l0 + LIN_N)
-                        waiting.append(
-                            difference(b, half, g0 + l0, words, wc_codes, tb[:, :, cols], z[:, :, cols], left)
-                        )
-                        if len(waiting) > LAG:
-                            interpolate(*waiting.pop(0))
-
-        wd_grouped = keep.tile([P, PASSES, PACK, P, PACK], BF16, name="wd_grouped", align_bytes=64)
-        ms = P // 4
-        for b in range(PASSES):
-            for m0 in range(0, P, ms):
-                nc.scalar.copy(
-                    wd_grouped[:, b, :, m0 : m0 + ms, :].rearrange("p i m t -> p m t i"),
-                    wd_raw[:, b, :, PACK * m0 : PACK * (m0 + ms)].rearrange("p t (m i) -> p m t i", i=PACK),
-                )
-        late_planes = keep.tile([P, 1 + HALVES, H], U8, name="late_planes", tag="d_then_planes", align_bytes=64)
-        wd_codes = keep.tile([P, PASSES * N], U32, name="wd_codes", align_bytes=64)
-        nc.vector.quantize_mx(
-            out=wd_codes[:].bitcast(FP8X4),
-            scales=late_planes[:, 0, :],
-            in_=wd_grouped[:].rearrange("p b i m t -> p (b i m t)"),
-        )
-        y = {}
-
-        def projection(half):
-            h_codes = keep.tile([P, PASSES * HALF], U32, name="h_codes%d" % half, align_bytes=64)
-            nc.vector.quantize_mx(
-                out=h_codes[:].bitcast(FP8X4),
-                scales=late_planes[:, 1 + half, :],
-                in_=h_bf[half][:].rearrange("p b j t -> p (b j t)"),
-            )
-            for i in range(PACK):
-                bank = psum.tile([P, HALF], F32, name="bank_y", tag="scalar_bank")
-                for b in range(PASSES):
-                    w_cols = slice(b * N + i * P, b * N + (i + 1) * P)
-                    h_cols = slice(b * HALF, (b + 1) * HALF)
-                    nc.tensor.matmul_mx(
-                        out=bank[:],
-                        lhsT=wd_codes[:, w_cols].bitcast(FP8X4),
-                        lhsT_scale=late_planes[:, 0, w_cols],
-                        rhs=h_codes[:, h_cols].bitcast(FP8X4),
-                        rhs_scale=late_planes[:, 1 + half, h_cols],
-                        start=(b == 0), stop=(b == PASSES - 1),
+        def round_wd(u):
+            grouped = keep.tile([P, PASSES, 2, P, PACK], BF16, name="wd_grouped%d" % u, align_bytes=64)
+            for b in range(PASSES):
+                for m0 in range(0, P, P // 2):
+                    nc.scalar.copy(
+                        grouped[:, b, :, m0 : m0 + P // 2, :].rearrange("p i m t -> p m t i"),
+                        wd_raw[:, b, :, PACK * m0 : PACK * (m0 + P // 2)].rearrange("p t (m i) -> p m t i", i=PACK)[
+                            :, :, :, 2 * u : 2 * u + 2
+                        ],
                     )
-                y[half, i] = keep.tile([P, HALF], F32, name="y%d%d" % (half, i))
-                nc.scalar.copy(y[half, i][:], bank[:])
+            return grouped[:].rearrange("p b i m t -> p (b i m t)")
 
-        projection(0)
+        y = [keep.tile([P, S], F32, name="y%d" % i) for i in range(PACK)]
+
+        def projection(i, half):
+            wd_codes, wd_plane = wd_mx[i // 2]
+            h_codes, h_plane = h_mx[half]
+            bank = psum.tile([P, HALF], F32, name="bank_y", tag="scalar_bank")
+            for b in range(PASSES):
+                w_cols = slice((2 * b + i % 2) * P, (2 * b + i % 2 + 1) * P)
+                h_cols = slice(b * HALF, (b + 1) * HALF)
+                nc.tensor.matmul_mx(
+                    out=bank[:],
+                    lhsT=wd_codes[:, w_cols].bitcast(FP8X4),
+                    lhsT_scale=wd_plane[:, w_cols],
+                    rhs=h_codes[:, h_cols].bitcast(FP8X4),
+                    rhs_scale=h_plane[:, h_cols],
+                    start=(b == 0), stop=(b == PASSES - 1),
+                )
+            nc.scalar.copy(y[i][:, half * HALF : (half + 1) * HALF], bank[:])
+
+        def quantise_h(half):
+            h_mx[half] = quantise(h_bf[half][:].rearrange("p b j t -> p (b j t)"), PASSES * HALF, "h%d" % half)
+
+        wb_mx, wd_mx, h_mx = {}, {}, {}
+        wb_mx[0] = quantise(round_wb(0)[:].rearrange("p t q i j -> p (t q i j)"), PASS, "wb0")
+        v_first = gather_words(0, GATE_N, "wb_grouped0")
+        wa_codes = reorder(raw_words[:, H:], "wa_codes")
+        wc_codes = reorder(raw_words[:, :H], "wc_codes")
+        v_rest = gather_words(GATE_N, S - GATE_N, "tab_bytes")
+
+        groups = [(b, j0) for b in range(PASSES) for j0 in range(0, S, GATE_N)]
+        ready = [gates(*groups[0])]
+        waiting = []
+        for n, (b, g0) in enumerate(groups):
+            if n == 1:
+                wb_mx[1] = quantise(round_wb(1)[:].rearrange("p t q i j -> p (t q i j)"), PASS, "wb1")
+            if n == 5:
+                wd_mx[0] = quantise(round_wd(0), PASSES * 2 * P, "wd0")
+            if n + 1 < len(groups):
+                ready.append(gates(*groups[n + 1]))
+            tb, z = ready.pop(0)
+            for l0 in range(0, GATE_N, LIN_N):
+                last = n == len(groups) - 1 and l0 + LIN_N == GATE_N
+                cols = slice(l0, l0 + LIN_N)
+                waiting.append(difference(b, g0 + l0, tb[:, :, cols], z[:, :, cols], last))
+                if len(waiting) > LAG:
+                    step = waiting.pop(0)
+                    interpolate(*step)
+                    if step[0] == PASSES - 1 and step[1] + LIN_N == HALF:
+                        quantise_h(0)
+                        projection(0, 0)
+                        projection(1, 0)
         for step in waiting:
             interpolate(*step)
-        projection(1)
+        quantise_h(1)
+        projection(0, 1)
+        projection(1, 1)
 
         out_rows = out.rearrange("(p i) c -> p i c", i=PACK)
-        for i in range(PACK):
+
+        def scatter(i, j0, width):
+            nc.vector.tensor_tensor(
+                pages[i % 2][:].indirect(offs2_sb[:, j0 // 16 : (j0 + width) // 16]),
+                y[i][:, j0 : j0 + width],
+                wgo_sb[:, j0 : j0 + width],
+                ALU.mult,
+            )
+
+        scatter(0, 0, HALF)
+        wd_mx[1] = quantise(round_wd(1), PASSES * 2 * P, "wd1")
+        for i in range(2, PACK):
             for half in range(HALVES):
-                nc.vector.tensor_tensor(
-                    pages[i % 2][:].indirect(offs2_sb[:, half * HALF // 16 : (half + 1) * HALF // 16]),
-                    y[half, i][:],
-                    wgo_sb[:, half * HALF : (half + 1) * HALF],
-                    ALU.mult,
-                )
+                projection(i, half)
+        scatter(0, HALF, HALF)
+        nc.sync.dma_start(out_rows[:, 0, :], pages[0][:])
+        for i in range(1, PACK):
+            scatter(i, 0, S)
             nc.sync.dma_start(out_rows[:, i, :], pages[i % 2][:])

@@ -27,7 +27,7 @@ HALF = 512
 HALVES = S // HALF
 GATE_N = 256
 LIN_N = 128
-LAG = 2
+C_BANKS = 5
 
 
 def tile_list_motet_voice_completion_kernel(
@@ -37,7 +37,7 @@ def tile_list_motet_voice_completion_kernel(
     with ExitStack() as ctx:
         keep = ctx.enter_context(tc.tile_pool(name="keep", bufs=1))
         ring = ctx.enter_context(tc.tile_pool(name="ring", bufs=2))
-        psum = ctx.enter_context(tc.psum_pool(name="psum", bufs=4))
+        psum = ctx.enter_context(tc.psum_pool(name="psum", bufs=8 - C_BANKS))
 
         offs_sb = keep.tile([P, S // 16], U16, name="offs_sb")
         nc.sync.dma_start(offs_sb[:], offs)
@@ -62,22 +62,22 @@ def tile_list_motet_voice_completion_kernel(
         wb_rows = wb.rearrange("(p j) c -> p j c", j=PACK)
         wb_raw = {}
 
-        def load_wb(b, tiles):
-            wb_raw[b] = tiles
-            width = PASS // len(tiles)
-            for u, piece in enumerate(tiles):
-                c0 = b * PASS + u * width
-                nc.sync.dma_start(piece, wb_rows[:, :, c0 : c0 + width])
+        def load_wb(b, c0, tiles):
+            wb_raw.setdefault(b, []).extend(tiles)
+            c0 = c0 + b * PASS
+            for piece in tiles:
+                nc.sync.dma_start(piece, wb_rows[:, :, c0 : c0 + piece.shape[2]])
+                c0 = c0 + piece.shape[2]
 
-        wb_first = [keep.tile([P, PACK, PASS // 2], F32, name="wb_first%d" % u) for u in range(2)]
-        load_wb(0, [w[:] for w in wb_first])
         tab = keep.tile([P, T], U32, name="tab", align_bytes=64)
         nc.sync.dma_start(tab[:].bitcast(I32), tab_words[0].rearrange("p t i -> p (t i)").bitcast(I32))
+        wb_first = keep.tile([P, PACK, PASS // 2], F32, name="wb_first", align_bytes=64)
+        wb_next = keep.tile([P, 2, PACK, PASS // 4], F32, name="wb_next", align_bytes=64)
+        load_wb(0, 0, [wb_first[:], wb_next[:, 0], wb_next[:, 1]])
 
         offs2_sb = keep.tile([P, S // 16], U16, name="offs2_sb")
         nc.sync.dma_start(offs2_sb[:], offs2)
         planes = keep.tile([P, 2 * H + S], U8, name="planes", align_bytes=64)
-        nc.gpsimd.memset(planes[:].bitcast(I32), 0)
         identity = keep.tile([P, P], F32, name="identity")
         make_identity(nc, identity[:])
 
@@ -85,9 +85,8 @@ def tile_list_motet_voice_completion_kernel(
         warm_out = keep.tile([P, 1], F32, name="warm_out")
         nc.vector.memset(warm_in[:], 0.0)
         nc.scalar.activation(warm_out[:], warm_in[:], ACT.Sigmoid)
-        pages = [keep.tile([P, T2], F32, name="page%d" % n) for n in range(2)]
-        for page in pages:
-            nc.vector.memset(page[:].bitcast(I32), 0)
+        pages = [keep.tile([P, T2], F32, name="page0")]
+        nc.vector.memset(pages[0][:].bitcast(I32), 0)
 
         gain_bank = psum.tile([P, P], F32, name="gain_bank", tag="scalar_bank")
         nc.tensor.transpose(gain_bank[:], gain_rows[:], identity[:])
@@ -99,24 +98,23 @@ def tile_list_motet_voice_completion_kernel(
 
         v_bytes = keep.tile([P, S], U8, name="v_bytes", align_bytes=64)
         nc.vector.tensor_copy(v_bytes[:], tab_bytes[:].indirect(offs_sb[:]))
-        staged = keep.tile([P, 2 * H + S], U8, name="staged", align_bytes=64)
-        nc.vector.tensor_copy(staged[:, 2 * H :].bitcast(I32), v_bytes[:].bitcast(I32))
         nc.vector.tensor_copy(
-            staged[:, : 2 * H].bitcast(I32).rearrange("p (g t q w) -> p g t q w", t=PACK, q=BLOCKS, w=RUN // 4),
+            planes[:, : 2 * H].bitcast(I32).rearrange("p (g t q w) -> p g t q w", t=PACK, q=BLOCKS, w=RUN // 4),
             raw_scales[:].rearrange("p s c -> p (s c)").bitcast(I32).rearrange(
                 "p (g q t w) -> p g t q w", t=PACK, q=BLOCKS, w=RUN // 4
             ),
         )
-        for r in range(4):
-            nc.sync.dma_start(planes[r:P:32, :].bitcast(I32), staged[RUN * r : P : 32, :].bitcast(I32))
+        nc.vector.tensor_copy(planes[:, 2 * H :].bitcast(I32), v_bytes[:].bitcast(I32))
+        for r in range(1, 4):
+            nc.sync.dma_start(planes[r:P:32, :].bitcast(I32), planes[RUN * r : P : 32, :].bitcast(I32))
 
         raw_words = keep.tile([P, H + H // 2], I32, name="raw_words", tag="v_bytes", align_bytes=64)
-        nc.sync.dma_start(raw_words[:, H:], wa_words[0].bitcast(I32))
         nc.sync.dma_start(raw_words[:, :H], wc_words[0].rearrange("p e i -> p (e i)").bitcast(I32))
+        nc.sync.dma_start(raw_words[:, H:], wa_words[0].bitcast(I32))
         widths = [PACK * PASS // 2, PACK * PASS // 2, PASSES * PACK * N, S]
-        late = keep.tile([P, sum(widths)], F32, name="late", tag="raw_scales", align_bytes=64)
+        late = keep.tile([P, sum(widths)], F32, name="late", tag="wb_first", align_bytes=64)
         parts = [late[:, sum(widths[:n]) : sum(widths[: n + 1])] for n in range(len(widths))]
-        load_wb(1, [part.rearrange("p (j c) -> p j c", j=PACK) for part in parts[:2]])
+        load_wb(1, 0, [part.rearrange("p (j c) -> p j c", j=PACK) for part in parts[:2]])
         wd_rows = wd.rearrange("(b q t i) n -> b t q i n", b=PASSES, t=PACK, i=RUN)
         wd_raw = parts[2].rearrange("p (b t n) -> p b t n", b=PASSES, t=PACK)
         for b in range(PASSES):
@@ -140,13 +138,15 @@ def tile_list_motet_voice_completion_kernel(
 
         def round_wb(b):
             grouped = keep.tile([P, PACK, BLOCKS, RUN, PACK], BF16, name="wb_grouped%d" % b, align_bytes=64)
-            qs = BLOCKS // len(wb_raw[b])
-            for u, piece in enumerate(wb_raw[b]):
-                for t0 in range(0, PACK, 2):
+            q0 = 0
+            for piece in wb_raw[b]:
+                blocks = piece.rearrange("p j (q t i) -> p t q j i", t=PACK, i=RUN)
+                for q in range(0, blocks.shape[2], BLOCKS // 4):
                     nc.scalar.copy(
-                        grouped[:, t0 : t0 + 2, u * qs : (u + 1) * qs].rearrange("p t q i j -> p t q j i"),
-                        piece.rearrange("p j (q t i) -> p t q j i", t=PACK, i=RUN)[:, t0 : t0 + 2],
+                        grouped[:, :, q0 : q0 + BLOCKS // 4].rearrange("p t q i j -> p t q j i"),
+                        blocks[:, :, q : q + BLOCKS // 4],
                     )
+                    q0 = q0 + BLOCKS // 4
             return grouped
 
         def quantise(grouped, width, name):
@@ -192,9 +192,10 @@ def tile_list_motet_voice_completion_kernel(
                 nc.scalar.activation(z[:, t0 : t0 + 2, :], bank[:], ACT.Sigmoid)
             return tb, z
 
-        def difference(b, j0, tb_cols, z_cols, last):
+        def difference(b, j0, tb, d):
             rhs, rhs_scale = v_cols(j0, LIN_N)
-            bank = psum.tile([P, PACK, LIN_N], F32, name="bank_c")
+            cols = slice(j0 % GATE_N, j0 % GATE_N + LIN_N)
+            bank = psum.tile([P, PACK, LIN_N], F32, name="bank_c", bufs=C_BANKS)
             for t in range(PACK):
                 c0 = b * PASS + t * P
                 nc.tensor.matmul_mx(
@@ -203,25 +204,22 @@ def tile_list_motet_voice_completion_kernel(
                     lhsT_scale=w_scales[:, 1, c0 : c0 + P],
                     rhs=rhs, rhs_scale=rhs_scale, start=True, stop=True,
                 )
-            d = ring.tile([P, PACK, LIN_N], F32, name="d", bufs=LAG + 1)
             for t in range(PACK):
                 nc.vector.scalar_tensor_tensor(
-                    d[:, t, :], tb_cols[:, t, :], gains[:, b * PACK + t : b * PACK + t + 1], bank[:, t, :], ALU.mult, ALU.subtract
+                    d[:, t, cols], tb[:, t, cols], gains[:, b * PACK + t : b * PACK + t + 1], bank[:, t, :], ALU.mult, ALU.subtract
                 )
-            e = ring.tile([P, PACK, LIN_N], F32, name="e", bufs=LAG + 1)
-            (nc.vector if last else nc.gpsimd).tensor_tensor(e[:], d[:], z_cols, ALU.mult)
-            return b, j0, e, bank
+            return bank
 
         def interpolate(b, j0, e, bank):
             nc.vector.tensor_tensor(
                 h_bf[j0 // HALF][:, b, j0 % HALF : j0 % HALF + LIN_N, :].rearrange("p (c i) t -> p c t i", i=2),
-                e[:].rearrange("p t (c i) -> p c t i", i=2),
+                e.rearrange("p t (c i) -> p c t i", i=2),
                 bank[:].rearrange("p t (c i) -> p c t i", i=2),
                 ALU.add,
             )
 
-        def round_wd(u):
-            grouped = keep.tile([P, PASSES, 2, P, PACK], BF16, name="wd_grouped%d" % u, align_bytes=64)
+        def round_wd(u, tag):
+            grouped = keep.tile([P, PASSES, 2, P, PACK], BF16, name="wd_grouped%d" % u, tag=tag, align_bytes=64)
             for b in range(PASSES):
                 for m0 in range(0, P, P // 2):
                     nc.scalar.copy(
@@ -256,9 +254,9 @@ def tile_list_motet_voice_completion_kernel(
 
         wb_mx, wd_mx, h_mx = {}, {}, {}
         wb_mx[0] = quantise(round_wb(0)[:].rearrange("p t q i j -> p (t q i j)"), PASS, "wb0")
-        v_first = gather_words(0, GATE_N, "wb_grouped0")
-        wa_codes = reorder(raw_words[:, H:], "wa_codes")
+        v_first = gather_words(0, GATE_N, "v_first")
         wc_codes = reorder(raw_words[:, :H], "wc_codes")
+        wa_codes = reorder(raw_words[:, H:], "wa_codes")
         v_rest = gather_words(GATE_N, S - GATE_N, "tab_bytes")
 
         groups = [(b, j0) for b in range(PASSES) for j0 in range(0, S, GATE_N)]
@@ -267,28 +265,38 @@ def tile_list_motet_voice_completion_kernel(
         for n, (b, g0) in enumerate(groups):
             if n == 1:
                 wb_mx[1] = quantise(round_wb(1)[:].rearrange("p t q i j -> p (t q i j)"), PASS, "wb1")
-            if n == 5:
-                wd_mx[0] = quantise(round_wd(0), PASSES * 2 * P, "wd0")
             if n + 1 < len(groups):
                 ready.append(gates(*groups[n + 1]))
             tb, z = ready.pop(0)
-            for l0 in range(0, GATE_N, LIN_N):
-                last = n == len(groups) - 1 and l0 + LIN_N == GATE_N
-                cols = slice(l0, l0 + LIN_N)
-                waiting.append(difference(b, g0 + l0, tb[:, :, cols], z[:, :, cols], last))
-                if len(waiting) > LAG:
-                    step = waiting.pop(0)
-                    interpolate(*step)
-                    if step[0] == PASSES - 1 and step[1] + LIN_N == HALF:
-                        quantise_h(0)
-                        projection(0, 0)
-                        projection(1, 0)
+            d = ring.tile([P, PACK, GATE_N], F32, name="d")
+            e = ring.tile([P, PACK, GATE_N], F32, name="e")
+            halves = [slice(l0, l0 + LIN_N) for l0 in range(0, GATE_N, LIN_N)]
+            banks = []
+            for cols in halves:
+                banks.append(difference(b, g0 + cols.start, tb, d))
+                if n + 1 == len(groups) and cols.start == 0:
+                    nc.gpsimd.tensor_tensor(e[:, :, cols], d[:, :, cols], z[:, :, cols], ALU.mult)
+            if n + 1 < len(groups):
+                nc.gpsimd.tensor_tensor(e[:], d[:], z[:], ALU.mult)
+            for step in waiting:
+                interpolate(*step)
+            if waiting and waiting[-1][0] == PASSES - 1 and waiting[-1][1] + LIN_N == HALF:
+                quantise_h(0)
+            waiting = [(b, g0 + cols.start, e[:, :, cols], bank) for cols, bank in zip(halves, banks)]
+        nc.vector.tensor_tensor(e[:, :, halves[1]], d[:, :, halves[1]], z[:, :, halves[1]], ALU.mult)
         for step in waiting:
             interpolate(*step)
+        wd_mx[0] = quantise(round_wd(0, "wd_grouped0"), PASSES * 2 * P, "wd0")
+        projection(0, 0)
         quantise_h(1)
+        wd_mx[1] = quantise(round_wd(1, "h_bf0"), PASSES * 2 * P, "wd1")
         projection(0, 1)
+        projection(1, 0)
         projection(1, 1)
 
+        pages.append(keep.tile([P, T2], F32, name="page1", tag="v_bytes", align_bytes=64))
+        for c0 in range(0, T2, T2 // 4):
+            nc.gpsimd.memset(pages[1][:, c0 : c0 + T2 // 4], 0.0)
         out_rows = out.rearrange("(p i) c -> p i c", i=PACK)
 
         def scatter(i, j0, width):
@@ -300,7 +308,6 @@ def tile_list_motet_voice_completion_kernel(
             )
 
         scatter(0, 0, HALF)
-        wd_mx[1] = quantise(round_wd(1), PASSES * 2 * P, "wd1")
         for i in range(2, PACK):
             for half in range(HALVES):
                 projection(i, half)

@@ -55,7 +55,7 @@ def tile_list_motet_voice_completion_kernel(
         nc.gpsimd.memset(gain_rows[:], 0.0)
         gain_src = gain.rearrange("(b q t i) -> b t q i", b=PASSES, t=PACK, i=RUN)
         for b in range(PASSES):
-            nc.sync.dma_start(
+            nc.gpsimd.dma_start(
                 gain_rows[b * PACK : (b + 1) * PACK, :].rearrange("t (q i) -> t q i", i=RUN), gain_src[b]
             )
 
@@ -72,8 +72,8 @@ def tile_list_motet_voice_completion_kernel(
         tab = keep.tile([P, T], U32, name="tab", align_bytes=64)
         nc.sync.dma_start(tab[:].bitcast(I32), tab_words[0].rearrange("p t i -> p (t i)").bitcast(I32))
         wb_first = keep.tile([P, PACK, PASS // 2], F32, name="wb_first", align_bytes=64)
-        wb_next = keep.tile([P, 2, PACK, PASS // 4], F32, name="wb_next", align_bytes=64)
-        load_wb(0, 0, [wb_first[:], wb_next[:, 0], wb_next[:, 1]])
+        wb_next = keep.tile([P, PACK, PASS // 2], F32, name="wb_next", align_bytes=64)
+        load_wb(0, 0, [wb_first[:], wb_next[:]])
 
         offs2_sb = keep.tile([P, S // 16], U16, name="offs2_sb")
         nc.sync.dma_start(offs2_sb[:], offs2)
@@ -85,13 +85,9 @@ def tile_list_motet_voice_completion_kernel(
         warm_out = keep.tile([P, 1], F32, name="warm_out")
         nc.vector.memset(warm_in[:], 0.0)
         nc.scalar.activation(warm_out[:], warm_in[:], ACT.Sigmoid)
-        pages = [keep.tile([P, T2], F32, name="page0")]
-        nc.vector.memset(pages[0][:].bitcast(I32), 0)
-
-        gain_bank = psum.tile([P, P], F32, name="gain_bank", tag="scalar_bank")
-        nc.tensor.transpose(gain_bank[:], gain_rows[:], identity[:])
-        gains = keep.tile([P, PASSES * PACK], F32, name="gains")
-        nc.scalar.copy(gains[:], gain_bank[:, : PASSES * PACK])
+        pages = [keep.tile([P, T2], F32, name="page%d" % n) for n in range(2)]
+        for page in pages:
+            nc.vector.memset(page[:].bitcast(I32), 0)
 
         w_scales = planes[:, : 2 * H].rearrange("p (s c) -> p s c", s=2)
         v_plane = planes[:, 2 * H :]
@@ -111,16 +107,16 @@ def tile_list_motet_voice_completion_kernel(
         raw_words = keep.tile([P, H + H // 2], I32, name="raw_words", tag="v_bytes", align_bytes=64)
         nc.sync.dma_start(raw_words[:, :H], wc_words[0].rearrange("p e i -> p (e i)").bitcast(I32))
         nc.sync.dma_start(raw_words[:, H:], wa_words[0].bitcast(I32))
-        widths = [PACK * PASS // 2, PACK * PASS // 2, PASSES * PACK * N, S]
+        widths = [PACK * PASS, PASSES * PACK * N, S]
         late = keep.tile([P, sum(widths)], F32, name="late", tag="wb_first", align_bytes=64)
         parts = [late[:, sum(widths[:n]) : sum(widths[: n + 1])] for n in range(len(widths))]
-        load_wb(1, 0, [part.rearrange("p (j c) -> p j c", j=PACK) for part in parts[:2]])
+        load_wb(1, 0, [part.rearrange("p (j c) -> p j c", j=PACK) for part in parts[:1]])
         wd_rows = wd.rearrange("(b q t i) n -> b t q i n", b=PASSES, t=PACK, i=RUN)
-        wd_raw = parts[2].rearrange("p (b t n) -> p b t n", b=PASSES, t=PACK)
+        wd_raw = parts[1].rearrange("p (b t n) -> p b t n", b=PASSES, t=PACK)
         for b in range(PASSES):
             for t in range(PACK):
                 nc.sync.dma_start(wd_raw[:, b, t, :], wd_rows[b, t])
-        wgo_sb = parts[3]
+        wgo_sb = parts[2]
         nc.sync.dma_start(wgo_sb, wgo)
 
         def reorder(raw, name):
@@ -136,26 +132,29 @@ def tile_list_motet_voice_completion_kernel(
             nc.vector.tensor_copy(words[:], tab[:].indirect(offs_sb[:, j0 // 16 : (j0 + width) // 16]))
             return words
 
-        def round_wb(b):
-            grouped = keep.tile([P, PACK, BLOCKS, RUN, PACK], BF16, name="wb_grouped%d" % b, align_bytes=64)
+        def round_wb(b, tag, shares):
+            grouped = keep.tile([P, PACK, BLOCKS, RUN, PACK], BF16, name="wb_grouped%d" % b, tag=tag, align_bytes=64)
             q0 = 0
-            for piece in wb_raw[b]:
-                blocks = piece.rearrange("p j (q t i) -> p t q j i", t=PACK, i=RUN)
-                for q in range(0, blocks.shape[2], BLOCKS // 4):
-                    nc.scalar.copy(
-                        grouped[:, :, q0 : q0 + BLOCKS // 4].rearrange("p t q i j -> p t q j i"),
-                        blocks[:, :, q : q + BLOCKS // 4],
-                    )
-                    q0 = q0 + BLOCKS // 4
-            return grouped
+            for copy, piece, q, count in shares:
+                blocks = wb_raw[b][piece].rearrange("p j (q t i) -> p t q j i", t=PACK, i=RUN)
+                copy(
+                    grouped[:, :, q0 : q0 + count].rearrange("p t q i j -> p t q j i"),
+                    blocks[:, :, q : q + count],
+                )
+                q0 = q0 + count
+            return grouped[:].rearrange("p t q i j -> p (t q i j)")
 
-        def quantise(grouped, width, name):
-            codes = keep.tile([P, width], U32, name=name + "_codes", align_bytes=64)
+        def quantise(grouped, width, name, tag=None):
+            codes = keep.tile([P, width], U32, name=name + "_codes", tag=tag or name + "_codes", align_bytes=64)
             plane = keep.tile([P, width], U8, name=name + "_plane", align_bytes=64)
             nc.vector.quantize_mx(out=codes[:].bitcast(FP8X4), scales=plane[:], in_=grouped)
             return codes, plane
 
-        h_bf = [keep.tile([P, PASSES, HALF, PACK], BF16, name="h_bf%d" % half, align_bytes=64) for half in range(HALVES)]
+        h_bf = {
+            (b, half): keep.tile([P, HALF, PACK], BF16, name="h_bf%d%d" % (b, half), align_bytes=64)
+            for b in range(PASSES)
+            for half in range(HALVES)
+        }
 
         def v_cols(j0, width):
             if j0 < GATE_N:
@@ -167,7 +166,7 @@ def tile_list_motet_voice_completion_kernel(
         def gates(b, j0):
             wb_codes, wb_plane = wb_mx[b]
             rhs, rhs_scale = v_cols(j0, GATE_N)
-            tb = ring.tile([P, PACK, GATE_N], F32, name="tb", bufs=3)
+            tb = keep.tile([P, PACK, GATE_N], F32, name="tb%d_%d" % (b, j0), align_bytes=64)
             z = ring.tile([P, PACK, GATE_N], F32, name="z", bufs=3)
             for t0 in range(0, PACK, 2):
                 bank = psum.tile([P, 2, GATE_N], F32, name="bank_b", tag="scalar_bank")
@@ -212,7 +211,7 @@ def tile_list_motet_voice_completion_kernel(
 
         def interpolate(b, j0, e, bank):
             nc.vector.tensor_tensor(
-                h_bf[j0 // HALF][:, b, j0 % HALF : j0 % HALF + LIN_N, :].rearrange("p (c i) t -> p c t i", i=2),
+                h_bf[b, j0 // HALF][:, j0 % HALF : j0 % HALF + LIN_N, :].rearrange("p (c i) t -> p c t i", i=2),
                 e.rearrange("p t (c i) -> p c t i", i=2),
                 bank[:].rearrange("p t (c i) -> p c t i", i=2),
                 ALU.add,
@@ -234,26 +233,33 @@ def tile_list_motet_voice_completion_kernel(
 
         def projection(i, half):
             wd_codes, wd_plane = wd_mx[i // 2]
-            h_codes, h_plane = h_mx[half]
             bank = psum.tile([P, HALF], F32, name="bank_y", tag="scalar_bank")
             for b in range(PASSES):
                 w_cols = slice((2 * b + i % 2) * P, (2 * b + i % 2 + 1) * P)
-                h_cols = slice(b * HALF, (b + 1) * HALF)
+                h_codes, h_plane = h_mx[b, half]
                 nc.tensor.matmul_mx(
                     out=bank[:],
                     lhsT=wd_codes[:, w_cols].bitcast(FP8X4),
                     lhsT_scale=wd_plane[:, w_cols],
-                    rhs=h_codes[:, h_cols].bitcast(FP8X4),
-                    rhs_scale=h_plane[:, h_cols],
+                    rhs=h_codes[:].bitcast(FP8X4),
+                    rhs_scale=h_plane[:],
                     start=(b == 0), stop=(b == PASSES - 1),
                 )
             nc.scalar.copy(y[i][:, half * HALF : (half + 1) * HALF], bank[:])
 
-        def quantise_h(half):
-            h_mx[half] = quantise(h_bf[half][:].rearrange("p b j t -> p (b j t)"), PASSES * HALF, "h%d" % half)
+        def quantise_h(b, half, tag=None):
+            h_mx[b, half] = quantise(h_bf[b, half][:].rearrange("p j t -> p (j t)"), HALF, "h%d%d" % (b, half), tag)
 
         wb_mx, wd_mx, h_mx = {}, {}, {}
-        wb_mx[0] = quantise(round_wb(0)[:].rearrange("p t q i j -> p (t q i j)"), PASS, "wb0")
+        quarter = BLOCKS // 4
+        shares = [(nc.scalar.copy, 0, 0, quarter), (nc.scalar.copy, 0, quarter, quarter)]
+        shares = shares + [(nc.scalar.copy, 1, 0, quarter), (nc.vector.tensor_copy, 1, quarter, quarter)]
+        wb_mx[0] = quantise(round_wb(0, "wb_grouped0", shares), PASS, "wb0")
+        gain_bank = psum.tile([P, P], F32, name="gain_bank", tag="scalar_bank")
+        nc.tensor.transpose(gain_bank[:], gain_rows[:], identity[:])
+        gains = keep.tile([P, PASSES * PACK], F32, name="gains", tag="wb_next", align_bytes=64)
+        nc.scalar.copy(gains[:], gain_bank[:, : PASSES * PACK])
+
         v_first = gather_words(0, GATE_N, "v_first")
         wc_codes = reorder(raw_words[:, :H], "wc_codes")
         wa_codes = reorder(raw_words[:, H:], "wa_codes")
@@ -263,9 +269,8 @@ def tile_list_motet_voice_completion_kernel(
         ready = [gates(*groups[0])]
         waiting = []
         for n, (b, g0) in enumerate(groups):
-            if n == 1:
-                wb_mx[1] = quantise(round_wb(1)[:].rearrange("p t q i j -> p (t q i j)"), PASS, "wb1")
-            if n + 1 < len(groups):
+            last = n + 1 == len(groups)
+            if not last:
                 ready.append(gates(*groups[n + 1]))
             tb, z = ready.pop(0)
             d = ring.tile([P, PACK, GATE_N], F32, name="d")
@@ -274,29 +279,36 @@ def tile_list_motet_voice_completion_kernel(
             banks = []
             for cols in halves:
                 banks.append(difference(b, g0 + cols.start, tb, d))
-                if n + 1 == len(groups) and cols.start == 0:
+                if last and cols.start == 0:
                     nc.gpsimd.tensor_tensor(e[:, :, cols], d[:, :, cols], z[:, :, cols], ALU.mult)
-            if n + 1 < len(groups):
+            if not last:
                 nc.gpsimd.tensor_tensor(e[:], d[:], z[:], ALU.mult)
+            slot = "tb%d_%d" % (b, g0)
+            if n == 1:
+                wb_second = round_wb(1, slot, [(nc.vector.tensor_copy, 0, 0, BLOCKS)])
+            if n == 2:
+                wb_mx[1] = quantise(wb_second, PASS, "wb1", slot)
+            if n == 3:
+                quantise_h(0, 0, slot)
+            if n == 5:
+                quantise_h(0, 1, slot)
+            if n == 6:
+                wd_first = round_wd(0, "wd_grouped0")
             for step in waiting:
                 interpolate(*step)
-            if waiting and waiting[-1][0] == PASSES - 1 and waiting[-1][1] + LIN_N == HALF:
-                quantise_h(0)
             waiting = [(b, g0 + cols.start, e[:, :, cols], bank) for cols, bank in zip(halves, banks)]
         nc.vector.tensor_tensor(e[:, :, halves[1]], d[:, :, halves[1]], z[:, :, halves[1]], ALU.mult)
+        quantise_h(1, 0, slot)
+        wd_mx[0] = quantise(wd_first, PASSES * 2 * P, "wd0", "tb1_512")
+        projection(0, 0)
         for step in waiting:
             interpolate(*step)
-        wd_mx[0] = quantise(round_wd(0, "wd_grouped0"), PASSES * 2 * P, "wd0")
-        projection(0, 0)
-        quantise_h(1)
-        wd_mx[1] = quantise(round_wd(1, "h_bf0"), PASSES * 2 * P, "wd1")
+        quantise_h(1, 1)
+        wd_mx[1] = quantise(round_wd(1, "h_bf10"), PASSES * 2 * P, "wd1")
         projection(0, 1)
         projection(1, 0)
         projection(1, 1)
 
-        pages.append(keep.tile([P, T2], F32, name="page1", tag="v_bytes", align_bytes=64))
-        for c0 in range(0, T2, T2 // 4):
-            nc.gpsimd.memset(pages[1][:, c0 : c0 + T2 // 4], 0.0)
         out_rows = out.rearrange("(p i) c -> p i c", i=PACK)
 
         def scatter(i, j0, width):

@@ -55,7 +55,7 @@ def tile_list_motet_voice_completion_kernel(
         nc.gpsimd.memset(gain_rows[:], 0.0)
         gain_src = gain.rearrange("(b q t i) -> b t q i", b=PASSES, t=PACK, i=RUN)
         for b in range(PASSES):
-            nc.gpsimd.dma_start(
+            nc.sync.dma_start(
                 gain_rows[b * PACK : (b + 1) * PACK, :].rearrange("t (q i) -> t q i", i=RUN), gain_src[b]
             )
 
@@ -135,10 +135,10 @@ def tile_list_motet_voice_completion_kernel(
         def round_wb(b, tag, shares):
             grouped = keep.tile([P, PACK, BLOCKS, RUN, PACK], BF16, name="wb_grouped%d" % b, tag=tag, align_bytes=64)
             q0 = 0
-            for copy, piece, q, count in shares:
-                blocks = wb_raw[b][piece].rearrange("p j (q t i) -> p t q j i", t=PACK, i=RUN)
+            for copy, order, piece, q, count in shares:
+                blocks = wb_raw[b][piece].rearrange("p j (q t i) -> " + order, t=PACK, i=RUN)
                 copy(
-                    grouped[:, :, q0 : q0 + count].rearrange("p t q i j -> p t q j i"),
+                    grouped[:, :, q0 : q0 + count].rearrange("p t q i j -> " + order),
                     blocks[:, :, q : q + count],
                 )
                 q0 = q0 + count
@@ -252,12 +252,12 @@ def tile_list_motet_voice_completion_kernel(
 
         wb_mx, wd_mx, h_mx = {}, {}, {}
         quarter = BLOCKS // 4
-        shares = [(nc.scalar.copy, 0, 0, quarter), (nc.scalar.copy, 0, quarter, quarter)]
-        shares = shares + [(nc.scalar.copy, 1, 0, quarter), (nc.vector.tensor_copy, 1, quarter, quarter)]
+        shares = [(nc.scalar.copy, "p t q j i", 0, 0, quarter), (nc.scalar.copy, "p t q j i", 0, quarter, quarter)]
+        shares = shares + [(nc.scalar.copy, "p t q j i", 1, 0, quarter), (nc.vector.tensor_copy, "p t q i j", 1, quarter, quarter)]
         wb_mx[0] = quantise(round_wb(0, "wb_grouped0", shares), PASS, "wb0")
         gain_bank = psum.tile([P, P], F32, name="gain_bank", tag="scalar_bank")
         nc.tensor.transpose(gain_bank[:], gain_rows[:], identity[:])
-        gains = keep.tile([P, PASSES * PACK], F32, name="gains", tag="wb_next", align_bytes=64)
+        gains = keep.tile([P, PASSES * PACK], F32, name="gains")
         nc.scalar.copy(gains[:], gain_bank[:, : PASSES * PACK])
 
         v_first = gather_words(0, GATE_N, "v_first")
@@ -285,7 +285,7 @@ def tile_list_motet_voice_completion_kernel(
                 nc.gpsimd.tensor_tensor(e[:], d[:], z[:], ALU.mult)
             slot = "tb%d_%d" % (b, g0)
             if n == 1:
-                wb_second = round_wb(1, slot, [(nc.vector.tensor_copy, 0, 0, BLOCKS)])
+                wb_second = round_wb(1, slot, [(nc.vector.tensor_copy, "p t q i j", 0, 0, BLOCKS)])
             if n == 2:
                 wb_mx[1] = quantise(wb_second, PASS, "wb1", slot)
             if n == 3:

@@ -28,6 +28,7 @@ HALVES = S // HALF
 GATE_N = 256
 LIN_N = 128
 C_BANKS = 5
+BANK = 512
 
 
 def tile_list_motet_voice_completion_kernel(
@@ -74,6 +75,8 @@ def tile_list_motet_voice_completion_kernel(
         wb_first = keep.tile([P, PACK, PASS // 2], F32, name="wb_first", align_bytes=64)
         wb_next = keep.tile([P, PACK, PASS // 2], F32, name="wb_next", align_bytes=64)
         load_wb(0, 0, [wb_first[:], wb_next[:]])
+        wa_raw = keep.tile([P, H // 2], I32, name="wa_raw", align_bytes=64)
+        nc.sync.dma_start(wa_raw[:], wa_words[0].bitcast(I32))
 
         offs2_sb = keep.tile([P, S // 16], U16, name="offs2_sb")
         nc.sync.dma_start(offs2_sb[:], offs2)
@@ -81,10 +84,6 @@ def tile_list_motet_voice_completion_kernel(
         identity = keep.tile([P, P], F32, name="identity")
         make_identity(nc, identity[:])
 
-        warm_in = keep.tile([P, 1], F32, name="warm_in")
-        warm_out = keep.tile([P, 1], F32, name="warm_out")
-        nc.vector.memset(warm_in[:], 0.0)
-        nc.scalar.activation(warm_out[:], warm_in[:], ACT.Sigmoid)
         pages = [keep.tile([P, T2], F32, name="page%d" % n) for n in range(2)]
         for page in pages:
             nc.vector.memset(page[:].bitcast(I32), 0)
@@ -104,9 +103,10 @@ def tile_list_motet_voice_completion_kernel(
         for r in range(1, 4):
             nc.sync.dma_start(planes[r:P:32, :].bitcast(I32), planes[RUN * r : P : 32, :].bitcast(I32))
 
-        raw_words = keep.tile([P, H + H // 2], I32, name="raw_words", tag="v_bytes", align_bytes=64)
-        nc.sync.dma_start(raw_words[:, :H], wc_words[0].rearrange("p e i -> p (e i)").bitcast(I32))
-        nc.sync.dma_start(raw_words[:, H:], wa_words[0].bitcast(I32))
+        wc_raw = keep.tile([P, H], I32, name="wc_raw", tag="v_bytes", align_bytes=64)
+        wc_rows = wc_words[0].rearrange("p e i -> p (e i)").bitcast(I32)
+        for b in range(PASSES):
+            nc.sync.dma_start(wc_raw[:, b * PASS : (b + 1) * PASS], wc_rows[:, b * PASS : (b + 1) * PASS])
         widths = [PACK * PASS, PASSES * PACK * N, S]
         late = keep.tile([P, sum(widths)], F32, name="late", tag="wb_first", align_bytes=64)
         parts = [late[:, sum(widths[:n]) : sum(widths[: n + 1])] for n in range(len(widths))]
@@ -119,11 +119,11 @@ def tile_list_motet_voice_completion_kernel(
         wgo_sb = parts[2]
         nc.sync.dma_start(wgo_sb, wgo)
 
-        def reorder(raw, name):
+        def reorder(raw, passes, name):
             codes = keep.tile(list(raw.shape), I32, name=name, align_bytes=64)
             nc.vector.tensor_copy(
-                codes[:].rearrange("p (b t q w) -> p b t q w", b=PASSES, t=PACK, q=BLOCKS),
-                raw.rearrange("p (b q t w) -> p b t q w", b=PASSES, t=PACK, q=BLOCKS),
+                codes[:].rearrange("p (b t q w) -> p b t q w", b=passes, t=PACK, q=BLOCKS),
+                raw.rearrange("p (b q t w) -> p b t q w", b=passes, t=PACK, q=BLOCKS),
             )
             return codes
 
@@ -150,11 +150,7 @@ def tile_list_motet_voice_completion_kernel(
             nc.vector.quantize_mx(out=codes[:].bitcast(FP8X4), scales=plane[:], in_=grouped)
             return codes, plane
 
-        h_bf = {
-            (b, half): keep.tile([P, HALF, PACK], BF16, name="h_bf%d%d" % (b, half), align_bytes=64)
-            for b in range(PASSES)
-            for half in range(HALVES)
-        }
+        h_bf = [keep.tile([P, PASSES, HALF, PACK], BF16, name="h_bf%d" % half, align_bytes=64) for half in range(HALVES)]
 
         def v_cols(j0, width):
             if j0 < GATE_N:
@@ -163,24 +159,32 @@ def tile_list_motet_voice_completion_kernel(
                 words = v_rest[:, j0 - GATE_N : j0 - GATE_N + width]
             return words.bitcast(FP8X4), v_plane[:, j0 : j0 + width]
 
-        def gates(b, j0):
+        def tanh_branch(b, j0, width):
             wb_codes, wb_plane = wb_mx[b]
-            rhs, rhs_scale = v_cols(j0, GATE_N)
-            tb = keep.tile([P, PACK, GATE_N], F32, name="tb%d_%d" % (b, j0), align_bytes=64)
-            z = ring.tile([P, PACK, GATE_N], F32, name="z", bufs=3)
-            for t0 in range(0, PACK, 2):
-                bank = psum.tile([P, 2, GATE_N], F32, name="bank_b", tag="scalar_bank")
-                for t in range(t0, t0 + 2):
+            rhs, rhs_scale = v_cols(j0, width)
+            per_bank = BANK // width
+            tb = []
+            for t0 in range(0, PACK, per_bank):
+                bank = psum.tile([P, per_bank, width], F32, name="bank_b", tag="scalar_bank")
+                for t in range(t0, t0 + per_bank):
                     nc.tensor.matmul_mx(
                         out=bank[:, t - t0, :],
                         lhsT=wb_codes[:, t * P : (t + 1) * P].bitcast(FP8X4),
                         lhsT_scale=wb_plane[:, t * P : (t + 1) * P],
                         rhs=rhs, rhs_scale=rhs_scale, start=True, stop=True,
                     )
-                nc.scalar.activation(tb[:, t0 : t0 + 2, :], bank[:], ACT.Tanh)
-            for t0 in range(0, PACK, 2):
-                bank = psum.tile([P, 2, GATE_N], F32, name="bank_a", tag="scalar_bank")
-                for t in range(t0, t0 + 2):
+                part = keep.tile([P, per_bank, width], F32, name="tb%d_%d_%d" % (b, j0, t0), align_bytes=64)
+                nc.scalar.activation(part[:], bank[:], ACT.Tanh)
+                tb.extend(part[:, t, :] for t in range(per_bank))
+            return tb
+
+        def gate(b, j0, width):
+            rhs, rhs_scale = v_cols(j0, width)
+            per_bank = BANK // width
+            z = ring.tile([P, PACK, width], F32, name="z", bufs=3)
+            for t0 in range(0, PACK, per_bank):
+                bank = psum.tile([P, per_bank, width], F32, name="bank_a", tag="scalar_bank")
+                for t in range(t0, t0 + per_bank):
                     c0 = b * PASS + t * P
                     nc.tensor.matmul_mx(
                         out=bank[:, t - t0, :],
@@ -188,30 +192,34 @@ def tile_list_motet_voice_completion_kernel(
                         lhsT_scale=w_scales[:, 0, c0 : c0 + P],
                         rhs=rhs, rhs_scale=rhs_scale, start=True, stop=True,
                     )
-                nc.scalar.activation(z[:, t0 : t0 + 2, :], bank[:], ACT.Sigmoid)
-            return tb, z
+                nc.scalar.activation(z[:, t0 : t0 + per_bank, :], bank[:], ACT.Sigmoid)
+            return z
 
-        def difference(b, j0, tb, d):
+        def gates(b, j0, width):
+            return tanh_branch(b, j0, width), gate(b, j0, width)
+
+        def linear_branch(b, j0):
             rhs, rhs_scale = v_cols(j0, LIN_N)
-            cols = slice(j0 % GATE_N, j0 % GATE_N + LIN_N)
             bank = psum.tile([P, PACK, LIN_N], F32, name="bank_c", bufs=C_BANKS)
             for t in range(PACK):
                 c0 = b * PASS + t * P
                 nc.tensor.matmul_mx(
                     out=bank[:, t, :],
-                    lhsT=wc_codes[:, c0 : c0 + P].bitcast(FP8X4),
+                    lhsT=wc_codes[b][:, t * P : (t + 1) * P].bitcast(FP8X4),
                     lhsT_scale=w_scales[:, 1, c0 : c0 + P],
                     rhs=rhs, rhs_scale=rhs_scale, start=True, stop=True,
                 )
-            for t in range(PACK):
-                nc.vector.scalar_tensor_tensor(
-                    d[:, t, cols], tb[:, t, cols], gains[:, b * PACK + t : b * PACK + t + 1], bank[:, t, :], ALU.mult, ALU.subtract
-                )
             return bank
+
+        def difference(b, cols, slices, tb, bank, d):
+            for t in slices:
+                nc.vector.scalar_tensor_tensor(
+                    d[:, t, cols], tb[t][:, cols], gains[:, b * PACK + t : b * PACK + t + 1], bank[:, t, :], ALU.mult, ALU.subtract
+                )
 
         def interpolate(b, j0, e, bank):
             nc.vector.tensor_tensor(
-                h_bf[b, j0 // HALF][:, j0 % HALF : j0 % HALF + LIN_N, :].rearrange("p (c i) t -> p c t i", i=2),
+                h_bf[j0 // HALF][:, b, j0 % HALF : j0 % HALF + LIN_N, :].rearrange("p (c i) t -> p c t i", i=2),
                 e.rearrange("p t (c i) -> p c t i", i=2),
                 bank[:].rearrange("p t (c i) -> p c t i", i=2),
                 ALU.add,
@@ -233,22 +241,23 @@ def tile_list_motet_voice_completion_kernel(
 
         def projection(i, half):
             wd_codes, wd_plane = wd_mx[i // 2]
+            h_codes, h_plane = h_mx[half]
             bank = psum.tile([P, HALF], F32, name="bank_y", tag="scalar_bank")
             for b in range(PASSES):
                 w_cols = slice((2 * b + i % 2) * P, (2 * b + i % 2 + 1) * P)
-                h_codes, h_plane = h_mx[b, half]
+                h_cols = slice(b * HALF, (b + 1) * HALF)
                 nc.tensor.matmul_mx(
                     out=bank[:],
                     lhsT=wd_codes[:, w_cols].bitcast(FP8X4),
                     lhsT_scale=wd_plane[:, w_cols],
-                    rhs=h_codes[:].bitcast(FP8X4),
-                    rhs_scale=h_plane[:],
+                    rhs=h_codes[:, h_cols].bitcast(FP8X4),
+                    rhs_scale=h_plane[:, h_cols],
                     start=(b == 0), stop=(b == PASSES - 1),
                 )
             nc.scalar.copy(y[i][:, half * HALF : (half + 1) * HALF], bank[:])
 
-        def quantise_h(b, half, tag=None):
-            h_mx[b, half] = quantise(h_bf[b, half][:].rearrange("p j t -> p (j t)"), HALF, "h%d%d" % (b, half), tag)
+        def quantise_h(half, tag=None):
+            h_mx[half] = quantise(h_bf[half][:].rearrange("p b j t -> p (b j t)"), PASSES * HALF, "h%d" % half, tag)
 
         wb_mx, wd_mx, h_mx = {}, {}, {}
         quarter = BLOCKS // 4
@@ -261,50 +270,51 @@ def tile_list_motet_voice_completion_kernel(
         nc.scalar.copy(gains[:], gain_bank[:, : PASSES * PACK])
 
         v_first = gather_words(0, GATE_N, "v_first")
-        wc_codes = reorder(raw_words[:, :H], "wc_codes")
-        wa_codes = reorder(raw_words[:, H:], "wa_codes")
+        wa_codes = reorder(wa_raw[:], PASSES, "wa_codes")
+        wc_codes = [reorder(wc_raw[:, b * PASS : (b + 1) * PASS], 1, "wc_codes%d" % b) for b in range(PASSES)]
         v_rest = gather_words(GATE_N, S - GATE_N, "tab_bytes")
 
-        groups = [(b, j0) for b in range(PASSES) for j0 in range(0, S, GATE_N)]
-        ready = [gates(*groups[0])]
+        groups = [(0, j0, LIN_N) for j0 in range(0, GATE_N, LIN_N)]
+        groups = groups + [(b, j0, GATE_N) for b in range(PASSES) for j0 in range(0, S, GATE_N)][1:]
+        z_first = gate(*groups[0])
+        ready = [(tanh_branch(*groups[0]), z_first)]
         waiting = []
-        for n, (b, g0) in enumerate(groups):
+        for n, (b, g0, width) in enumerate(groups):
             last = n + 1 == len(groups)
+            halves = [slice(l0, l0 + LIN_N) for l0 in range(0, width, LIN_N)]
+            banks = [linear_branch(b, g0 + cols.start) for cols in halves]
             if not last:
                 ready.append(gates(*groups[n + 1]))
             tb, z = ready.pop(0)
-            d = ring.tile([P, PACK, GATE_N], F32, name="d")
-            e = ring.tile([P, PACK, GATE_N], F32, name="e")
-            halves = [slice(l0, l0 + LIN_N) for l0 in range(0, GATE_N, LIN_N)]
-            banks = []
-            for cols in halves:
-                banks.append(difference(b, g0 + cols.start, tb, d))
-                if last and cols.start == 0:
-                    nc.gpsimd.tensor_tensor(e[:, :, cols], d[:, :, cols], z[:, :, cols], ALU.mult)
-            if not last:
+            d = ring.tile([P, PACK, width], F32, name="d")
+            e = ring.tile([P, PACK, width], F32, name="e")
+            if last:
+                difference(b, halves[0], range(PACK), tb, banks[0], d)
+                nc.gpsimd.tensor_tensor(e[:, :, halves[0]], d[:, :, halves[0]], z[:, :, halves[0]], ALU.mult)
+                difference(b, halves[1], range(PACK), tb, banks[1], d)
+            else:
+                for t0 in range(0, PACK, 2):
+                    for cols, bank in zip(halves, banks):
+                        difference(b, cols, range(t0, t0 + 2), tb, bank, d)
                 nc.gpsimd.tensor_tensor(e[:], d[:], z[:], ALU.mult)
-            slot = "tb%d_%d" % (b, g0)
-            if n == 1:
-                wb_second = round_wb(1, slot, [(nc.vector.tensor_copy, "p t q i j", 0, 0, BLOCKS)])
+            slot = "tb%d_%d_0" % (b, g0)
             if n == 2:
-                wb_mx[1] = quantise(wb_second, PASS, "wb1", slot)
+                wb_second = round_wb(1, slot, [(nc.vector.tensor_copy, "p t q i j", 0, 0, BLOCKS)])
             if n == 3:
-                quantise_h(0, 0, slot)
-            if n == 5:
-                quantise_h(0, 1, slot)
-            if n == 6:
-                wd_first = round_wd(0, "wd_grouped0")
+                wb_mx[1] = quantise(wb_second, PASS, "wb1", slot)
+            if n == 7:
+                wd_first = round_wd(0, slot)
             for step in waiting:
                 interpolate(*step)
             waiting = [(b, g0 + cols.start, e[:, :, cols], bank) for cols, bank in zip(halves, banks)]
         nc.vector.tensor_tensor(e[:, :, halves[1]], d[:, :, halves[1]], z[:, :, halves[1]], ALU.mult)
-        quantise_h(1, 0, slot)
-        wd_mx[0] = quantise(wd_first, PASSES * 2 * P, "wd0", "tb1_512")
+        quantise_h(0, slot)
+        wd_mx[0] = quantise(wd_first, PASSES * 2 * P, "wd0", "tb1_768_2")
         projection(0, 0)
         for step in waiting:
             interpolate(*step)
-        quantise_h(1, 1)
-        wd_mx[1] = quantise(round_wd(1, "h_bf10"), PASSES * 2 * P, "wd1")
+        quantise_h(1)
+        wd_mx[1] = quantise(round_wd(1, "h_bf0"), PASSES * 2 * P, "wd1")
         projection(0, 1)
         projection(1, 0)
         projection(1, 1)

@@ -237,7 +237,8 @@ def tile_list_motet_voice_completion_kernel(
                     )
             return grouped[:].rearrange("p b i m t -> p (b i m t)")
 
-        y = [keep.tile([P, S], F32, name="y%d" % i) for i in range(PACK)]
+        y = {i: keep.tile([P, S], F32, name="y%d" % i) for i in range(1, PACK)}
+        weighted = [keep.tile([P, S], F32, name="weighted%d" % i) for i in range(PACK)]
 
         def projection(i, half):
             wd_codes, wd_plane = wd_mx[i // 2]
@@ -254,7 +255,12 @@ def tile_list_motet_voice_completion_kernel(
                     rhs_scale=h_plane[:, h_cols],
                     start=(b == 0), stop=(b == PASSES - 1),
                 )
-            nc.scalar.copy(y[i][:, half * HALF : (half + 1) * HALF], bank[:])
+            cols = slice(half * HALF, (half + 1) * HALF)
+            if i == 0:
+                nc.vector.tensor_tensor(weighted[i][:, cols], bank[:], wgo_sb[:, cols], ALU.mult)
+            else:
+                nc.scalar.copy(y[i][:, cols], bank[:])
+                nc.gpsimd.tensor_tensor(weighted[i][:, cols], y[i][:, cols], wgo_sb[:, cols], ALU.mult)
 
         def quantise_h(half, tag=None):
             h_mx[half] = quantise(h_bf[half][:].rearrange("p b j t -> p (b j t)"), PASSES * HALF, "h%d" % half, tag)
@@ -322,11 +328,9 @@ def tile_list_motet_voice_completion_kernel(
         out_rows = out.rearrange("(p i) c -> p i c", i=PACK)
 
         def scatter(i, j0, width):
-            nc.vector.tensor_tensor(
+            nc.vector.tensor_copy(
                 pages[i % 2][:].indirect(offs2_sb[:, j0 // 16 : (j0 + width) // 16]),
-                y[i][:, j0 : j0 + width],
-                wgo_sb[:, j0 : j0 + width],
-                ALU.mult,
+                weighted[i][:, j0 : j0 + width],
             )
 
         scatter(0, 0, HALF)

@@ -72,11 +72,11 @@ def tile_list_motet_voice_completion_kernel(
 
         tab = keep.tile([P, T], U32, name="tab", align_bytes=64)
         nc.sync.dma_start(tab[:].bitcast(I32), tab_words[0].rearrange("p t i -> p (t i)").bitcast(I32))
+        wa_raw = keep.tile([P, H // 2], I32, name="wa_raw", align_bytes=64)
+        nc.sync.dma_start(wa_raw[:], wa_words[0].bitcast(I32))
         wb_first = keep.tile([P, PACK, PASS // 2], F32, name="wb_first", align_bytes=64)
         wb_next = keep.tile([P, PACK, PASS // 2], F32, name="wb_next", align_bytes=64)
         load_wb(0, 0, [wb_first[:], wb_next[:]])
-        wa_raw = keep.tile([P, H // 2], I32, name="wa_raw", align_bytes=64)
-        nc.sync.dma_start(wa_raw[:], wa_words[0].bitcast(I32))
 
         offs2_sb = keep.tile([P, S // 16], U16, name="offs2_sb")
         nc.sync.dma_start(offs2_sb[:], offs2)
@@ -84,9 +84,11 @@ def tile_list_motet_voice_completion_kernel(
         identity = keep.tile([P, P], F32, name="identity")
         make_identity(nc, identity[:])
 
-        pages = [keep.tile([P, T2], F32, name="page%d" % n) for n in range(2)]
-        for page in pages:
-            nc.vector.memset(page[:].bitcast(I32), 0)
+        pages = [keep.tile([P, T2], F32, name="page%d" % n) for n in range(PACK - 1)]
+        for cols in (slice(0, T2 // 2 - 1), slice(T2 // 2 - 1, T2)):
+            nc.vector.memset(pages[0][:, cols].bitcast(I32), 0)
+        for page in pages[1:]:
+            nc.gpsimd.memset(page[:], 0.0)
 
         w_scales = planes[:, : 2 * H].rearrange("p (s c) -> p s c", s=2)
         v_plane = planes[:, 2 * H :]
@@ -102,6 +104,11 @@ def tile_list_motet_voice_completion_kernel(
         nc.vector.tensor_copy(planes[:, 2 * H :].bitcast(I32), v_bytes[:].bitcast(I32))
         for r in range(1, 4):
             nc.sync.dma_start(planes[r:P:32, :].bitcast(I32), planes[RUN * r : P : 32, :].bitcast(I32))
+
+        last_page = keep.tile([P, T2], F32, name="page3", tag="raw_scales", align_bytes=64)
+        pages.append(last_page)
+        for c0 in range(0, T2, BANK):
+            nc.gpsimd.memset(last_page[:, c0 : c0 + BANK], 0.0)
 
         wc_raw = keep.tile([P, H], I32, name="wc_raw", tag="v_bytes", align_bytes=64)
         wc_rows = wc_words[0].rearrange("p e i -> p (e i)").bitcast(I32)
@@ -119,8 +126,8 @@ def tile_list_motet_voice_completion_kernel(
         wgo_sb = parts[2]
         nc.sync.dma_start(wgo_sb, wgo)
 
-        def reorder(raw, passes, name):
-            codes = keep.tile(list(raw.shape), I32, name=name, align_bytes=64)
+        def reorder(raw, passes, name, tag=None):
+            codes = keep.tile(list(raw.shape), I32, name=name, tag=tag or name, align_bytes=64)
             nc.vector.tensor_copy(
                 codes[:].rearrange("p (b t q w) -> p b t q w", b=passes, t=PACK, q=BLOCKS),
                 raw.rearrange("p (b q t w) -> p b t q w", b=passes, t=PACK, q=BLOCKS),
@@ -225,27 +232,25 @@ def tile_list_motet_voice_completion_kernel(
                 ALU.add,
             )
 
-        def round_wd(u, tag):
-            grouped = keep.tile([P, PASSES, 2, P, PACK], BF16, name="wd_grouped%d" % u, tag=tag, align_bytes=64)
-            for b in range(PASSES):
-                for m0 in range(0, P, P // 2):
-                    nc.scalar.copy(
-                        grouped[:, b, :, m0 : m0 + P // 2, :].rearrange("p i m t -> p m t i"),
-                        wd_raw[:, b, :, PACK * m0 : PACK * (m0 + P // 2)].rearrange("p t (m i) -> p m t i", i=PACK)[
-                            :, :, :, 2 * u : 2 * u + 2
-                        ],
-                    )
-            return grouped[:].rearrange("p b i m t -> p (b i m t)")
+        def round_wd(tag):
+            grouped = keep.tile([P, 2, PASSES, 2, P, PACK], BF16, name="wd_grouped", tag=tag, align_bytes=64)
+            for u in range(2):
+                for b in range(PASSES):
+                    for m0 in range(0, P, P // 2):
+                        nc.scalar.copy(
+                            grouped[:, u, b, :, m0 : m0 + P // 2, :].rearrange("p i m t -> p m t i"),
+                            wd_raw[:, b, :, PACK * m0 : PACK * (m0 + P // 2)].rearrange("p t (m i) -> p m t i", i=PACK)[
+                                :, :, :, 2 * u : 2 * u + 2
+                            ],
+                        )
+            return grouped[:].rearrange("p u b i m t -> p (u b i m t)")
 
-        y = {i: keep.tile([P, S], F32, name="y%d" % i) for i in range(1, PACK)}
-        weighted = [keep.tile([P, S], F32, name="weighted%d" % i) for i in range(PACK)]
-
-        def projection(i, half):
-            wd_codes, wd_plane = wd_mx[i // 2]
+        def projection_bank(i, half):
+            wd_codes, wd_plane = wd_mx[0]
             h_codes, h_plane = h_mx[half]
             bank = psum.tile([P, HALF], F32, name="bank_y", tag="scalar_bank")
             for b in range(PASSES):
-                w_cols = slice((2 * b + i % 2) * P, (2 * b + i % 2 + 1) * P)
+                w_cols = slice((i // 2 * 4 + 2 * b + i % 2) * P, (i // 2 * 4 + 2 * b + i % 2 + 1) * P)
                 h_cols = slice(b * HALF, (b + 1) * HALF)
                 nc.tensor.matmul_mx(
                     out=bank[:],
@@ -255,17 +260,23 @@ def tile_list_motet_voice_completion_kernel(
                     rhs_scale=h_plane[:, h_cols],
                     start=(b == 0), stop=(b == PASSES - 1),
                 )
-            cols = slice(half * HALF, (half + 1) * HALF)
-            if i == 0:
-                nc.vector.tensor_tensor(weighted[i][:, cols], bank[:], wgo_sb[:, cols], ALU.mult)
-            else:
-                nc.scalar.copy(y[i][:, cols], bank[:])
-                nc.gpsimd.tensor_tensor(weighted[i][:, cols], y[i][:, cols], wgo_sb[:, cols], ALU.mult)
+            return bank
+
+        def projection(i, half, tag=None):
+            y = keep.tile([P, HALF], F32, name="y%d_%d" % (i, half), tag=tag or "y%d_%d" % (i, half), align_bytes=64)
+            nc.scalar.copy(y[:], projection_bank(i, half)[:])
+            return y
+
+        def window(i, half):
+            return pages[i][:].indirect(offs2_sb[:, half * HALF // 16 : (half + 1) * HALF // 16])
 
         def quantise_h(half, tag=None):
             h_mx[half] = quantise(h_bf[half][:].rearrange("p b j t -> p (b j t)"), PASSES * HALF, "h%d" % half, tag)
 
         wb_mx, wd_mx, h_mx = {}, {}, {}
+        v_first = gather_words(0, GATE_N, "v_first")
+        wa_codes = reorder(wa_raw[:], PASSES, "wa_codes")
+        v_rest = gather_words(GATE_N, S - GATE_N, "tab_bytes")
         quarter = BLOCKS // 4
         shares = [(nc.scalar.copy, "p t q j i", 0, 0, quarter), (nc.scalar.copy, "p t q j i", 0, quarter, quarter)]
         shares = shares + [(nc.scalar.copy, "p t q j i", 1, 0, quarter), (nc.vector.tensor_copy, "p t q i j", 1, quarter, quarter)]
@@ -275,70 +286,202 @@ def tile_list_motet_voice_completion_kernel(
         gains = keep.tile([P, PASSES * PACK], F32, name="gains")
         nc.scalar.copy(gains[:], gain_bank[:, : PASSES * PACK])
 
-        v_first = gather_words(0, GATE_N, "v_first")
-        wa_codes = reorder(wa_raw[:], PASSES, "wa_codes")
-        wc_codes = [reorder(wc_raw[:, b * PASS : (b + 1) * PASS], 1, "wc_codes%d" % b) for b in range(PASSES)]
-        v_rest = gather_words(GATE_N, S - GATE_N, "tab_bytes")
+        wc_codes = {0: reorder(wc_raw[:, :PASS], 1, "wc_codes0")}
+
+        def second_pass(tag):
+            grouped = keep.tile([P, PACK, BLOCKS, RUN, PACK], BF16, name="wb_grouped1", tag=tag, align_bytes=64)
+            codes = keep.tile([P, PASS], U32, name="wb1_codes", align_bytes=64)
+            plane = keep.tile([P, PASS], U8, name="wb1_plane", align_bytes=64)
+            blocks = wb_raw[1][0].rearrange("p j (q t i) -> p t q i j", t=PACK, i=RUN)
+            for t0 in range(0, PACK, 2):
+                nc.vector.tensor_copy(grouped[:, t0 : t0 + 2], blocks[:, t0 : t0 + 2])
+            for t0 in range(0, PACK, 2):
+                cols = slice(t0 * P, (t0 + 2) * P)
+                nc.vector.quantize_mx(
+                    out=codes[:, cols].bitcast(FP8X4), scales=plane[:, cols],
+                    in_=grouped[:, t0 : t0 + 2].rearrange("p t q i j -> p (t q i j)"),
+                )
+                if t0 == 0:
+                    wc_codes[1] = reorder(wc_raw[:, PASS:], 1, "wc_codes1", None)
+            wb_mx[1] = codes, plane
 
         groups = [(0, j0, LIN_N) for j0 in range(0, GATE_N, LIN_N)]
-        groups = groups + [(b, j0, GATE_N) for b in range(PASSES) for j0 in range(0, S, GATE_N)][1:]
-        z_first = gate(*groups[0])
-        ready = [(tanh_branch(*groups[0]), z_first)]
-        waiting = []
-        for n, (b, g0, width) in enumerate(groups):
-            last = n + 1 == len(groups)
-            halves = [slice(l0, l0 + LIN_N) for l0 in range(0, width, LIN_N)]
-            banks = [linear_branch(b, g0 + cols.start) for cols in halves]
-            if not last:
-                ready.append(gates(*groups[n + 1]))
-            tb, z = ready.pop(0)
-            d = ring.tile([P, PACK, width], F32, name="d")
-            e = ring.tile([P, PACK, width], F32, name="e")
-            if last:
-                difference(b, halves[0], range(PACK), tb, banks[0], d)
-                nc.gpsimd.tensor_tensor(e[:, :, halves[0]], d[:, :, halves[0]], z[:, :, halves[0]], ALU.mult)
-                difference(b, halves[1], range(PACK), tb, banks[1], d)
-            else:
-                for t0 in range(0, PACK, 2):
-                    for cols, bank in zip(halves, banks):
-                        difference(b, cols, range(t0, t0 + 2), tb, bank, d)
-                nc.gpsimd.tensor_tensor(e[:], d[:], z[:], ALU.mult)
-            slot = "tb%d_%d_0" % (b, g0)
-            if n == 2:
-                wb_second = round_wb(1, slot, [(nc.vector.tensor_copy, "p t q i j", 0, 0, BLOCKS)])
-            if n == 3:
-                wb_mx[1] = quantise(wb_second, PASS, "wb1", slot)
-            if n == 7:
-                wd_first = round_wd(0, slot)
-            for step in waiting:
-                interpolate(*step)
-            waiting = [(b, g0 + cols.start, e[:, :, cols], bank) for cols, bank in zip(halves, banks)]
-        nc.vector.tensor_tensor(e[:, :, halves[1]], d[:, :, halves[1]], z[:, :, halves[1]], ALU.mult)
-        quantise_h(0, slot)
-        wd_mx[0] = quantise(wd_first, PASSES * 2 * P, "wd0", "tb1_768_2")
-        projection(0, 0)
-        for step in waiting:
-            interpolate(*step)
+        groups = groups + [(b, q * GATE_N, GATE_N) for b, q in ((0, 1), (0, 2), (1, 0), (1, 1), (0, 3), (1, 2), (1, 3))]
+        tb, z, banks, d, e, y, weighted, scaled, copied = {}, {}, {}, {}, {}, {}, {}, {}, {}
+
+        def steps(n):
+            return [slice(l0, l0 + LIN_N) for l0 in range(0, groups[n][2], LIN_N)]
+
+        def tanh_of(n):
+            tb[n] = tanh_branch(*groups[n])
+
+        def gate_of(n):
+            z[n] = gate(*groups[n])
+
+        def gates_of(n):
+            tanh_of(n)
+            gate_of(n)
+
+        def linear_of(n):
+            b, g0, width = groups[n]
+            banks[n] = [linear_branch(b, g0 + cols.start) for cols in steps(n)]
+
+        def d_vector(n):
+            b, g0, width = groups[n]
+            d[n] = ring.tile([P, PACK, width], F32, name="d")
+            for t0 in range(0, PACK, 2):
+                for cols, bank in zip(steps(n), banks[n]):
+                    difference(b, cols, range(t0, t0 + 2), tb[n], bank, d[n])
+
+        def stage(n):
+            b, g0, width = groups[n]
+            scaled[n] = ring.tile([P, PACK, width], F32, name="scaled")
+            copied[n] = ring.tile([P, PACK, width], F32, name="copied")
+            for t in range(PACK):
+                nc.scalar.activation(scaled[n][:, t, :], tb[n][t], ACT.Copy, scale=gains[:, b * PACK + t : b * PACK + t + 1])
+            for cols, bank in zip(steps(n), banks[n]):
+                nc.scalar.copy(copied[n][:, :, cols], bank[:])
+
+        def woven_gate_of(n):
+            b, g0, width = groups[n]
+            z[n] = ring.tile([P, width, PACK], F32, name="z", bufs=3)
+            for cols in steps(n):
+                rhs, rhs_scale = v_cols(g0 + cols.start, LIN_N)
+                bank = psum.tile([P, PACK, LIN_N], F32, name="bank_a", tag="scalar_bank")
+                for t in range(PACK):
+                    c0 = b * PASS + t * P
+                    nc.tensor.matmul_mx(
+                        out=bank[:, t, :],
+                        lhsT=wa_codes[:].bitcast(U8)[:, 2 * c0 : 2 * (c0 + P)].bitcast(FP4X4),
+                        lhsT_scale=w_scales[:, 0, c0 : c0 + P],
+                        rhs=rhs, rhs_scale=rhs_scale, start=True, stop=True,
+                    )
+                nc.scalar.activation(z[n][:, cols, :], bank[:].rearrange("p t j -> p j t"), ACT.Sigmoid)
+
+        def scale_of(n):
+            b, g0, width = groups[n]
+            scaled[n] = ring.tile([P, PACK, width], F32, name="scaled")
+            for t in range(PACK):
+                nc.scalar.activation(scaled[n][:, t, :], tb[n][t], ACT.Copy, scale=gains[:, b * PACK + t : b * PACK + t + 1])
+
+        def linear_share(n):
+            d[n] = ring.tile([P, groups[n][2], PACK], F32, name="d")
+            for cols, bank in zip(steps(n), banks[n]):
+                nc.vector.scalar_tensor_tensor(
+                    d[n][:, cols, :], z[n][:, cols, :], 1.0, bank[:].rearrange("p t j -> p j t"), ALU.subtract, ALU.mult
+                )
+
+        def tanh_share(n):
+            e[n] = keep.tile([P, groups[n][2], PACK], F32, name="e%d" % n, tag="e%d" % (n if n == 5 else n % 3), align_bytes=64)
+            nc.gpsimd.tensor_tensor(e[n][:], z[n][:], scaled[n][:].rearrange("p t j -> p j t"), ALU.mult)
+
+        def join(n):
+            b, g0, width = groups[n]
+            nc.gpsimd.tensor_tensor(h_bf[g0 // HALF][:, b, g0 % HALF : g0 % HALF + width, :], e[n][:], d[n][:], ALU.subtract)
+
+        def weigh_from_bank(i):
+            weighted[i] = ring.tile([P, HALF], F32, name="weighted")
+            nc.vector.tensor_tensor(weighted[i][:], projection_bank(i, 0)[:], wgo_sb[:, :HALF], ALU.mult)
+
+        def place_fused(i):
+            nc.vector.tensor_tensor(window(i, 0), y[i][:], wgo_sb[:, :HALF], ALU.mult)
+
+        def d_gpsimd(n):
+            d[n] = ring.tile([P, PACK, groups[n][2]], F32, name="d")
+            nc.gpsimd.tensor_tensor(d[n][:], scaled[n][:], copied[n][:], ALU.subtract)
+
+        def product(n, split=None):
+            e[n] = keep.tile([P, PACK, groups[n][2]], F32, name="e%d" % n, tag="e%d" % (n if n == 5 else n % 3), align_bytes=64)
+            for cols in [slice(0, split), slice(split, groups[n][2])] if split else [slice(0, groups[n][2])]:
+                nc.gpsimd.tensor_tensor(e[n][:, :, cols], d[n][:, :, cols], z[n][:, :, cols], ALU.mult)
+
+        def h_of(n):
+            b, g0, width = groups[n]
+            for cols, bank in zip(steps(n), banks[n]):
+                interpolate(b, g0 + cols.start, e[n][:, :, cols], bank)
+
+        def slot(n):
+            return "tb%d_%d_0" % groups[n][:2]
+
+        def project(i, tag=None):
+            y[i] = projection(i, 0, tag)
+
+        def weigh(i, tag="weighted"):
+            weighted[i] = ring.tile([P, HALF], F32, name="weighted", tag=tag)
+            nc.gpsimd.tensor_tensor(weighted[i][:], y[i][:], wgo_sb[:, :HALF], ALU.mult)
+
+        def place(i):
+            nc.vector.tensor_copy(window(i, 0), weighted[i][:])
+
+        gate_of(0)
+        tanh_of(0)
+        linear_of(0)
+        tanh_of(1)
+        gate_of(1)
+        d_vector(0)
+        product(0)
+        linear_of(1)
+        gates_of(2)
+        d_vector(1)
+        product(1)
+        linear_of(2)
+        gates_of(3)
+        d_vector(2)
+        second_pass(slot(2))
+        product(2)
+        h_of(0)
+        h_of(1)
+        linear_of(3)
+        gates_of(4)
+        d_vector(3)
+        product(3)
+        h_of(2)
+        linear_of(4)
+        gates_of(5)
+        d_vector(4)
+        product(4)
+        h_of(3)
+        linear_of(5)
+        gates_of(6)
+        wd_first = round_wd(slot(3))
+        d_vector(5)
+        product(5)
+        h_of(4)
+        linear_of(6)
+        woven_gate_of(7)
+        tanh_of(7)
+        d_vector(6)
+        product(6, 160)
+        h_of(5)
+        quantise_h(0)
+        wd_mx[0] = quantise(wd_first, PASSES * PACK * P, "wd", "e5")
+        scale_of(7)
+        linear_of(7)
+        linear_share(7)
+        tanh_share(7)
+        weigh_from_bank(0)
+        project(1)
+        h_of(6)
+        weigh(1)
+        place(0)
+        woven_gate_of(8)
+        tanh_of(8)
+        scale_of(8)
+        linear_of(8)
+        join(7)
+        linear_share(8)
+        place(1)
+        project(2)
+        weigh(2)
+        tanh_share(8)
+        join(8)
+        project(3, "e2")
+        place(2)
         quantise_h(1)
-        wd_mx[1] = quantise(round_wd(1, "h_bf0"), PASSES * 2 * P, "wd1")
-        projection(0, 1)
-        projection(1, 0)
-        projection(1, 1)
+        place_fused(3)
 
         out_rows = out.rearrange("(p i) c -> p i c", i=PACK)
-
-        def scatter(i, j0, width):
-            nc.vector.tensor_copy(
-                pages[i % 2][:].indirect(offs2_sb[:, j0 // 16 : (j0 + width) // 16]),
-                weighted[i][:, j0 : j0 + width],
-            )
-
-        scatter(0, 0, HALF)
-        for i in range(2, PACK):
-            for half in range(HALVES):
-                projection(i, half)
-        scatter(0, HALF, HALF)
-        nc.sync.dma_start(out_rows[:, 0, :], pages[0][:])
-        for i in range(1, PACK):
-            scatter(i, 0, S)
-            nc.sync.dma_start(out_rows[:, i, :], pages[i % 2][:])
+        for i in range(PACK):
+            last = projection(i, 1)
+            nc.vector.tensor_tensor(window(i, 1), last[:], wgo_sb[:, HALF:], ALU.mult)
+            nc.sync.dma_start(out_rows[:, i, :], pages[i][:])

@@ -72,8 +72,9 @@ def tile_list_motet_voice_completion_kernel(
 
         tab = keep.tile([P, T], U32, name="tab", align_bytes=64)
         nc.sync.dma_start(tab[:].bitcast(I32), tab_words[0].rearrange("p t i -> p (t i)").bitcast(I32))
-        wa_raw = keep.tile([P, H // 2], I32, name="wa_raw", align_bytes=64)
-        nc.sync.dma_start(wa_raw[:], wa_words[0].bitcast(I32))
+        wa_rows = wa_words[0].bitcast(I32)
+        wa_first = keep.tile([P, PASS // 2], I32, name="wa_first", align_bytes=64)
+        nc.sync.dma_start(wa_first[:], wa_rows[:, : PASS // 2])
         wb_first = keep.tile([P, PACK, PASS // 2], F32, name="wb_first", align_bytes=64)
         wb_next = keep.tile([P, PACK, PASS // 2], F32, name="wb_next", align_bytes=64)
         load_wb(0, 0, [wb_first[:], wb_next[:]])
@@ -110,10 +111,12 @@ def tile_list_motet_voice_completion_kernel(
         for c0 in range(0, T2, BANK):
             nc.gpsimd.memset(last_page[:, c0 : c0 + BANK], 0.0)
 
-        wc_raw = keep.tile([P, H], I32, name="wc_raw", tag="v_bytes", align_bytes=64)
+        words_raw = keep.tile([P, H + PASS // 2], I32, name="words_raw", tag="v_bytes", align_bytes=64)
+        wc_raw = words_raw[:, :H]
         wc_rows = wc_words[0].rearrange("p e i -> p (e i)").bitcast(I32)
         for b in range(PASSES):
             nc.sync.dma_start(wc_raw[:, b * PASS : (b + 1) * PASS], wc_rows[:, b * PASS : (b + 1) * PASS])
+        nc.sync.dma_start(words_raw[:, H:], wa_rows[:, PASS // 2 :])
         widths = [PACK * PASS, PASSES * PACK * N, S]
         late = keep.tile([P, sum(widths)], F32, name="late", tag="wb_first", align_bytes=64)
         parts = [late[:, sum(widths[:n]) : sum(widths[: n + 1])] for n in range(len(widths))]
@@ -195,7 +198,7 @@ def tile_list_motet_voice_completion_kernel(
                     c0 = b * PASS + t * P
                     nc.tensor.matmul_mx(
                         out=bank[:, t - t0, :],
-                        lhsT=wa_codes[:].bitcast(U8)[:, 2 * c0 : 2 * (c0 + P)].bitcast(FP4X4),
+                        lhsT=wa_codes[b][:].bitcast(U8)[:, 2 * t * P : 2 * (t + 1) * P].bitcast(FP4X4),
                         lhsT_scale=w_scales[:, 0, c0 : c0 + P],
                         rhs=rhs, rhs_scale=rhs_scale, start=True, stop=True,
                     )
@@ -275,11 +278,11 @@ def tile_list_motet_voice_completion_kernel(
 
         wb_mx, wd_mx, h_mx = {}, {}, {}
         v_first = gather_words(0, GATE_N, "v_first")
-        wa_codes = reorder(wa_raw[:], PASSES, "wa_codes")
+        wa_codes = {0: reorder(wa_first[:], 1, "wa_codes0")}
         v_rest = gather_words(GATE_N, S - GATE_N, "tab_bytes")
         quarter = BLOCKS // 4
         shares = [(nc.scalar.copy, "p t q j i", 0, 0, quarter), (nc.scalar.copy, "p t q j i", 0, quarter, quarter)]
-        shares = shares + [(nc.scalar.copy, "p t q j i", 1, 0, quarter), (nc.vector.tensor_copy, "p t q i j", 1, quarter, quarter)]
+        shares = shares + [(nc.scalar.copy, "p t q j i", 1, 0, 2), (nc.vector.tensor_copy, "p t q i j", 1, 2, 6)]
         wb_mx[0] = quantise(round_wb(0, "wb_grouped0", shares), PASS, "wb0")
         gain_bank = psum.tile([P, P], F32, name="gain_bank", tag="scalar_bank")
         nc.tensor.transpose(gain_bank[:], gain_rows[:], identity[:])
@@ -302,7 +305,8 @@ def tile_list_motet_voice_completion_kernel(
                     in_=grouped[:, t0 : t0 + 2].rearrange("p t q i j -> p (t q i j)"),
                 )
                 if t0 == 0:
-                    wc_codes[1] = reorder(wc_raw[:, PASS:], 1, "wc_codes1", None)
+                    wc_codes[1] = reorder(wc_raw[:, PASS:], 1, "wc_codes1")
+                    wa_codes[1] = reorder(words_raw[:, H:], 1, "wa_codes1")
             wb_mx[1] = codes, plane
 
         groups = [(0, j0, LIN_N) for j0 in range(0, GATE_N, LIN_N)]
@@ -328,7 +332,7 @@ def tile_list_motet_voice_completion_kernel(
 
         def d_vector(n):
             b, g0, width = groups[n]
-            d[n] = ring.tile([P, PACK, width], F32, name="d")
+            d[n] = ring.tile([P, PACK, width], F32, name="d", bufs=3)
             for t0 in range(0, PACK, 2):
                 for cols, bank in zip(steps(n), banks[n]):
                     difference(b, cols, range(t0, t0 + 2), tb[n], bank, d[n])
@@ -342,22 +346,6 @@ def tile_list_motet_voice_completion_kernel(
             for cols, bank in zip(steps(n), banks[n]):
                 nc.scalar.copy(copied[n][:, :, cols], bank[:])
 
-        def woven_gate_of(n):
-            b, g0, width = groups[n]
-            z[n] = ring.tile([P, width, PACK], F32, name="z", bufs=3)
-            for cols in steps(n):
-                rhs, rhs_scale = v_cols(g0 + cols.start, LIN_N)
-                bank = psum.tile([P, PACK, LIN_N], F32, name="bank_a", tag="scalar_bank")
-                for t in range(PACK):
-                    c0 = b * PASS + t * P
-                    nc.tensor.matmul_mx(
-                        out=bank[:, t, :],
-                        lhsT=wa_codes[:].bitcast(U8)[:, 2 * c0 : 2 * (c0 + P)].bitcast(FP4X4),
-                        lhsT_scale=w_scales[:, 0, c0 : c0 + P],
-                        rhs=rhs, rhs_scale=rhs_scale, start=True, stop=True,
-                    )
-                nc.scalar.activation(z[n][:, cols, :], bank[:].rearrange("p t j -> p j t"), ACT.Sigmoid)
-
         def scale_of(n):
             b, g0, width = groups[n]
             scaled[n] = ring.tile([P, PACK, width], F32, name="scaled")
@@ -365,19 +353,22 @@ def tile_list_motet_voice_completion_kernel(
                 nc.scalar.activation(scaled[n][:, t, :], tb[n][t], ACT.Copy, scale=gains[:, b * PACK + t : b * PACK + t + 1])
 
         def linear_share(n):
-            d[n] = ring.tile([P, groups[n][2], PACK], F32, name="d")
+            d[n] = ring.tile([P, PACK, groups[n][2]], F32, name="d", bufs=3)
             for cols, bank in zip(steps(n), banks[n]):
-                nc.vector.scalar_tensor_tensor(
-                    d[n][:, cols, :], z[n][:, cols, :], 1.0, bank[:].rearrange("p t j -> p j t"), ALU.subtract, ALU.mult
-                )
+                nc.vector.scalar_tensor_tensor(d[n][:, :, cols], z[n][:, :, cols], 1.0, bank[:], ALU.subtract, ALU.mult)
 
         def tanh_share(n):
-            e[n] = keep.tile([P, groups[n][2], PACK], F32, name="e%d" % n, tag="e%d" % (n if n == 5 else n % 3), align_bytes=64)
-            nc.gpsimd.tensor_tensor(e[n][:], z[n][:], scaled[n][:].rearrange("p t j -> p j t"), ALU.mult)
+            e[n] = keep.tile([P, PACK, groups[n][2]], F32, name="e%d" % n, tag="e%d" % (n % 3), align_bytes=64)
+            nc.gpsimd.tensor_tensor(e[n][:], z[n][:], scaled[n][:], ALU.mult)
 
         def join(n):
             b, g0, width = groups[n]
-            nc.gpsimd.tensor_tensor(h_bf[g0 // HALF][:, b, g0 % HALF : g0 % HALF + width, :], e[n][:], d[n][:], ALU.subtract)
+            nc.gpsimd.tensor_tensor(
+                h_bf[g0 // HALF][:, b, g0 % HALF : g0 % HALF + width, :].rearrange("p (c i) t -> p c t i", i=2),
+                e[n][:].rearrange("p t (c i) -> p c t i", i=2),
+                d[n][:].rearrange("p t (c i) -> p c t i", i=2),
+                ALU.subtract,
+            )
 
         def weigh_from_bank(i):
             weighted[i] = ring.tile([P, HALF], F32, name="weighted")
@@ -387,18 +378,21 @@ def tile_list_motet_voice_completion_kernel(
             nc.vector.tensor_tensor(window(i, 0), y[i][:], wgo_sb[:, :HALF], ALU.mult)
 
         def d_gpsimd(n):
-            d[n] = ring.tile([P, PACK, groups[n][2]], F32, name="d")
+            d[n] = ring.tile([P, PACK, groups[n][2]], F32, name="d", bufs=3)
             nc.gpsimd.tensor_tensor(d[n][:], scaled[n][:], copied[n][:], ALU.subtract)
 
-        def product(n, split=None):
-            e[n] = keep.tile([P, PACK, groups[n][2]], F32, name="e%d" % n, tag="e%d" % (n if n == 5 else n % 3), align_bytes=64)
-            for cols in [slice(0, split), slice(split, groups[n][2])] if split else [slice(0, groups[n][2])]:
-                nc.gpsimd.tensor_tensor(e[n][:, :, cols], d[n][:, :, cols], z[n][:, :, cols], ALU.mult)
+        def product(n, step=None, tag=None):
+            cols = slice(0, groups[n][2]) if step is None else steps(n)[step]
+            part = keep.tile(
+                [P, PACK, cols.stop - cols.start], F32, name="e%d_%d" % (n, cols.start), tag=tag or "e%d" % (n % 3), align_bytes=64
+            )
+            nc.gpsimd.tensor_tensor(part[:], d[n][:, :, cols], z[n][:, :, cols], ALU.mult)
+            e.setdefault(n, []).extend(part[:, :, l0 : l0 + LIN_N] for l0 in range(0, cols.stop - cols.start, LIN_N))
 
         def h_of(n):
             b, g0, width = groups[n]
-            for cols, bank in zip(steps(n), banks[n]):
-                interpolate(b, g0 + cols.start, e[n][:, :, cols], bank)
+            for cols, part, bank in zip(steps(n), e[n], banks[n]):
+                interpolate(b, g0 + cols.start, part, bank)
 
         def slot(n):
             return "tb%d_%d_0" % groups[n][:2]
@@ -414,17 +408,17 @@ def tile_list_motet_voice_completion_kernel(
             nc.vector.tensor_copy(window(i, 0), weighted[i][:])
 
         gate_of(0)
-        tanh_of(0)
-        linear_of(0)
-        tanh_of(1)
         gate_of(1)
+        linear_of(0)
+        linear_of(1)
+        tanh_of(0)
+        tanh_of(1)
+        linear_of(2)
+        gates_of(2)
         d_vector(0)
         product(0)
-        linear_of(1)
-        gates_of(2)
         d_vector(1)
         product(1)
-        linear_of(2)
         gates_of(3)
         d_vector(2)
         second_pass(slot(2))
@@ -445,16 +439,17 @@ def tile_list_motet_voice_completion_kernel(
         gates_of(6)
         wd_first = round_wd(slot(3))
         d_vector(5)
-        product(5)
+        product(5, None, "e5")
         h_of(4)
         linear_of(6)
-        woven_gate_of(7)
+        gate_of(7)
         tanh_of(7)
         d_vector(6)
-        product(6, 160)
+        product(6, 0)
         h_of(5)
         quantise_h(0)
         wd_mx[0] = quantise(wd_first, PASSES * PACK * P, "wd", "e5")
+        product(6, 1, slot(3))
         scale_of(7)
         linear_of(7)
         linear_share(7)
@@ -464,15 +459,14 @@ def tile_list_motet_voice_completion_kernel(
         h_of(6)
         weigh(1)
         place(0)
-        woven_gate_of(8)
+        gate_of(8)
         tanh_of(8)
         scale_of(8)
         linear_of(8)
         join(7)
         linear_share(8)
         place(1)
-        project(2)
-        weigh(2)
+        weigh_from_bank(2)
         tanh_share(8)
         join(8)
         project(3, "e2")

@@ -108,8 +108,7 @@ def tile_list_motet_voice_completion_kernel(
 
         last_page = keep.tile([P, T2], F32, name="page3", tag="raw_scales", align_bytes=64)
         pages.append(last_page)
-        for c0 in range(0, T2, BANK):
-            nc.gpsimd.memset(last_page[:, c0 : c0 + BANK], 0.0)
+        nc.gpsimd.memset(last_page[:], 0.0)
 
         words_raw = keep.tile([P, H + PASS // 2], I32, name="words_raw", tag="v_bytes", align_bytes=64)
         wc_raw = words_raw[:, :H]
@@ -248,10 +247,13 @@ def tile_list_motet_voice_completion_kernel(
                         )
             return grouped[:].rearrange("p u b i m t -> p (u b i m t)")
 
-        def projection_bank(i, half):
+        def projection_bank(i, half, for_vector=False):
             wd_codes, wd_plane = wd_mx[0]
             h_codes, h_plane = h_mx[half]
-            bank = psum.tile([P, HALF], F32, name="bank_y", tag="scalar_bank")
+            if for_vector:
+                bank = psum.tile([P, HALF], F32, name="bank_y", tag="bank_c", bufs=C_BANKS)
+            else:
+                bank = psum.tile([P, HALF], F32, name="bank_y", tag="scalar_bank")
             for b in range(PASSES):
                 w_cols = slice((i // 2 * 4 + 2 * b + i % 2) * P, (i // 2 * 4 + 2 * b + i % 2 + 1) * P)
                 h_cols = slice(b * HALF, (b + 1) * HALF)
@@ -326,13 +328,18 @@ def tile_list_motet_voice_completion_kernel(
             tanh_of(n)
             gate_of(n)
 
-        def linear_of(n):
+        def linear_of(n, step=None):
             b, g0, width = groups[n]
-            banks[n] = [linear_branch(b, g0 + cols.start) for cols in steps(n)]
+            for cols in steps(n) if step is None else [steps(n)[step]]:
+                banks.setdefault(n, []).append(linear_branch(b, g0 + cols.start))
 
-        def d_vector(n):
+        def d_vector(n, step=None):
             b, g0, width = groups[n]
-            d[n] = ring.tile([P, PACK, width], F32, name="d", bufs=3)
+            if n not in d:
+                d[n] = ring.tile([P, PACK, width], F32, name="d", bufs=3)
+            if step is not None:
+                difference(b, steps(n)[step], range(PACK), tb[n], banks[n][step], d[n])
+                return
             for t0 in range(0, PACK, 2):
                 for cols, bank in zip(steps(n), banks[n]):
                     difference(b, cols, range(t0, t0 + 2), tb[n], bank, d[n])
@@ -357,8 +364,8 @@ def tile_list_motet_voice_completion_kernel(
             for cols, bank in zip(steps(n), banks[n]):
                 nc.vector.scalar_tensor_tensor(d[n][:, :, cols], z[n][:, :, cols], 1.0, bank[:], ALU.subtract, ALU.mult)
 
-        def tanh_share(n):
-            e[n] = keep.tile([P, PACK, groups[n][2]], F32, name="e%d" % n, tag="e%d" % (n % 3), align_bytes=64)
+        def tanh_share(n, tag=None):
+            e[n] = keep.tile([P, PACK, groups[n][2]], F32, name="e%d" % n, tag=tag or "e%d" % (n % 3), align_bytes=64)
             nc.gpsimd.tensor_tensor(e[n][:], z[n][:], scaled[n][:], ALU.mult)
 
         def join(n):
@@ -372,7 +379,7 @@ def tile_list_motet_voice_completion_kernel(
 
         def weigh_from_bank(i):
             weighted[i] = ring.tile([P, HALF], F32, name="weighted")
-            nc.vector.tensor_tensor(weighted[i][:], projection_bank(i, 0)[:], wgo_sb[:, :HALF], ALU.mult)
+            nc.vector.tensor_tensor(weighted[i][:], projection_bank(i, 0, True)[:], wgo_sb[:, :HALF], ALU.mult)
 
         def place_fused(i):
             nc.vector.tensor_tensor(window(i, 0), y[i][:], wgo_sb[:, :HALF], ALU.mult)
@@ -409,43 +416,56 @@ def tile_list_motet_voice_completion_kernel(
 
         gate_of(0)
         gate_of(1)
-        linear_of(0)
-        linear_of(1)
         tanh_of(0)
         tanh_of(1)
+        linear_of(0)
+        linear_of(1)
+        tanh_of(2)
         linear_of(2)
-        gates_of(2)
+        gate_of(2)
         d_vector(0)
         product(0)
         d_vector(1)
         product(1)
-        gates_of(3)
+        tanh_of(3)
+        linear_of(3, 0)
+        gate_of(3)
         d_vector(2)
-        second_pass(slot(2))
-        product(2)
         h_of(0)
+        second_pass(slot(2))
+        product(2, None, slot(2))
+        d_vector(3, 0)
         h_of(1)
-        linear_of(3)
-        gates_of(4)
-        d_vector(3)
+        linear_of(3, 1)
+        tanh_of(4)
+        linear_of(4, 0)
+        gate_of(4)
+        d_vector(3, 1)
         product(3)
+        d_vector(4, 0)
         h_of(2)
-        linear_of(4)
-        gates_of(5)
-        d_vector(4)
+        linear_of(4, 1)
+        tanh_of(5)
+        linear_of(5, 0)
+        gate_of(5)
+        d_vector(4, 1)
         product(4)
+        d_vector(5, 0)
         h_of(3)
-        linear_of(5)
-        gates_of(6)
+        linear_of(5, 1)
+        tanh_of(6)
+        linear_of(6, 0)
+        gate_of(6)
         wd_first = round_wd(slot(3))
-        d_vector(5)
+        d_vector(5, 1)
         product(5, None, "e5")
+        d_vector(6, 0)
         h_of(4)
-        linear_of(6)
+        linear_of(6, 1)
         gate_of(7)
         tanh_of(7)
-        d_vector(6)
         product(6, 0)
+        d_vector(6, 1)
         h_of(5)
         quantise_h(0)
         wd_mx[0] = quantise(wd_first, PASSES * PACK * P, "wd", "e5")

@@ -40,6 +40,8 @@ def tile_list_motet_voice_completion_kernel(
         ring = ctx.enter_context(tc.tile_pool(name="ring", bufs=2))
         psum = ctx.enter_context(tc.psum_pool(name="psum", bufs=8 - C_BANKS))
 
+        shared = ctx.enter_context(tc.tile_pool(name="shared", bufs=1))
+
         offs_sb = keep.tile([P, S // 16], U16, name="offs_sb")
         nc.sync.dma_start(offs_sb[:], offs)
         tab_bytes = keep.tile([P, T], U8, name="tab_bytes", align_bytes=64)
@@ -182,7 +184,9 @@ def tile_list_motet_voice_completion_kernel(
                         lhsT_scale=wb_plane[:, t * P : (t + 1) * P],
                         rhs=rhs, rhs_scale=rhs_scale, start=True, stop=True,
                     )
-                part = keep.tile([P, per_bank, width], F32, name="tb%d_%d_%d" % (b, j0, t0), align_bytes=64)
+                name = "tb%d_%d_%d" % (b, j0, t0)
+                tag = "tb%d_%d_%d" % (b, j0 - HALF, t0) if b == 1 and j0 >= HALF else name
+                part = keep.tile([P, per_bank, width], F32, name=name, tag=tag, align_bytes=64)
                 nc.scalar.activation(part[:], bank[:], ACT.Tanh)
                 tb.extend(part[:, t, :] for t in range(per_bank))
             return tb
@@ -190,7 +194,7 @@ def tile_list_motet_voice_completion_kernel(
         def gate(b, j0, width):
             rhs, rhs_scale = v_cols(j0, width)
             per_bank = BANK // width
-            z = ring.tile([P, PACK, width], F32, name="z", bufs=3)
+            z = ring.tile([P, PACK, width], F32, name="z", bufs=4)
             for t0 in range(0, PACK, per_bank):
                 bank = psum.tile([P, per_bank, width], F32, name="bank_a", tag="scalar_bank")
                 for t in range(t0, t0 + per_bank):
@@ -248,14 +252,14 @@ def tile_list_motet_voice_completion_kernel(
             return grouped[:].rearrange("p u b i m t -> p (u b i m t)")
 
         def projection_bank(i, half, for_vector=False):
-            wd_codes, wd_plane = wd_mx[0]
+            wd_codes, wd_plane = wd_mx[i // 2]
             h_codes, h_plane = h_mx[half]
             if for_vector:
                 bank = psum.tile([P, HALF], F32, name="bank_y", tag="bank_c", bufs=C_BANKS)
             else:
                 bank = psum.tile([P, HALF], F32, name="bank_y", tag="scalar_bank")
             for b in range(PASSES):
-                w_cols = slice((i // 2 * 4 + 2 * b + i % 2) * P, (i // 2 * 4 + 2 * b + i % 2 + 1) * P)
+                w_cols = slice((2 * b + i % 2) * P, (2 * b + i % 2 + 1) * P)
                 h_cols = slice(b * HALF, (b + 1) * HALF)
                 nc.tensor.matmul_mx(
                     out=bank[:],
@@ -268,8 +272,11 @@ def tile_list_motet_voice_completion_kernel(
             return bank
 
         def projection(i, half, tag=None):
-            y = keep.tile([P, HALF], F32, name="y%d_%d" % (i, half), tag=tag or "y%d_%d" % (i, half), align_bytes=64)
-            nc.scalar.copy(y[:], projection_bank(i, half)[:])
+            if tag is None:
+                y = keep.tile([P, HALF], F32, name="y%d_%d" % (i, half), tag="y%d" % i, align_bytes=64)
+            else:
+                y = shared.tile([P, 2 * HALF], F32, name="y%d_%d" % (i, half), offset=tag)[:, :HALF]
+            nc.scalar.copy(y[:], projection_bank(i, half, tag is not None)[:])
             return y
 
         def window(i, half):
@@ -290,6 +297,8 @@ def tile_list_motet_voice_completion_kernel(
         nc.tensor.transpose(gain_bank[:], gain_rows[:], identity[:])
         gains = keep.tile([P, PASSES * PACK], F32, name="gains")
         nc.scalar.copy(gains[:], gain_bank[:, : PASSES * PACK])
+        negated = keep.tile([P, PASSES * PACK], F32, name="negated")
+        nc.gpsimd.tensor_scalar(negated[:], gains[:], -1.0, 0.0, ALU.mult, ALU.add)
 
         wc_codes = {0: reorder(wc_raw[:, :PASS], 1, "wc_codes0")}
 
@@ -335,6 +344,8 @@ def tile_list_motet_voice_completion_kernel(
 
         def d_vector(n, step=None):
             b, g0, width = groups[n]
+            if n not in d and n == 5:
+                d[n] = keep.tile([P, PACK, width], F32, name="d5", align_bytes=64)
             if n not in d:
                 d[n] = ring.tile([P, PACK, width], F32, name="d", bufs=3)
             if step is not None:
@@ -353,19 +364,23 @@ def tile_list_motet_voice_completion_kernel(
             for cols, bank in zip(steps(n), banks[n]):
                 nc.scalar.copy(copied[n][:, :, cols], bank[:])
 
-        def scale_of(n):
+        def scale_of(n, gains=gains):
             b, g0, width = groups[n]
             scaled[n] = ring.tile([P, PACK, width], F32, name="scaled")
             for t in range(PACK):
                 nc.scalar.activation(scaled[n][:, t, :], tb[n][t], ACT.Copy, scale=gains[:, b * PACK + t : b * PACK + t + 1])
 
-        def linear_share(n):
-            d[n] = ring.tile([P, PACK, groups[n][2]], F32, name="d", bufs=3)
-            for cols, bank in zip(steps(n), banks[n]):
+        def linear_share(n, step=None):
+            if n not in d:
+                d[n] = ring.tile([P, PACK, groups[n][2]], F32, name="d", bufs=3)
+            for cols, bank in zip(steps(n), banks[n]) if step is None else [(steps(n)[step], banks[n][step])]:
                 nc.vector.scalar_tensor_tensor(d[n][:, :, cols], z[n][:, :, cols], 1.0, bank[:], ALU.subtract, ALU.mult)
 
         def tanh_share(n, tag=None):
-            e[n] = keep.tile([P, PACK, groups[n][2]], F32, name="e%d" % n, tag=tag or "e%d" % (n % 3), align_bytes=64)
+            if tag == 0:
+                e[n] = shared.tile([P, PACK, groups[n][2]], F32, name="e%d" % n, offset=0)
+            else:
+                e[n] = keep.tile([P, PACK, groups[n][2]], F32, name="e%d" % n, tag=tag or "e%d" % (n % 3), align_bytes=64)
             nc.gpsimd.tensor_tensor(e[n][:], z[n][:], scaled[n][:], ALU.mult)
 
         def join(n):
@@ -377,8 +392,41 @@ def tile_list_motet_voice_completion_kernel(
                 ALU.subtract,
             )
 
-        def weigh_from_bank(i):
-            weighted[i] = ring.tile([P, HALF], F32, name="weighted")
+        rows = {}
+
+        def join_on_tensor(n, offset, scalar_banks, step=None):
+            rows.setdefault(n, [])
+            for cols in steps(n) if step is None else [steps(n)[step]]:
+                if not scalar_banks:
+                    turned = psum.tile([P, PACK, P], F32, name="bank_turned", tag="bank_c", bufs=C_BANKS)
+                else:
+                    turned = psum.tile([P, PACK, P], F32, name="bank_turned", tag="scalar_bank")
+                for t in range(PACK):
+                    for k, share in enumerate((e[n], d[n])):
+                        nc.tensor.matmul(
+                            out=turned[:, t, :], lhsT=share[:, t, cols], rhs=identity[:], is_transpose=True, start=(k == 0), stop=(k == 1)
+                        )
+                if offset is not None and cols.start:
+                    row = shared.tile([P, P, PACK], BF16, name="last_rows%d" % n, offset=offset)
+                else:
+                    row = ring.tile([P, P, PACK], BF16, name="h_rows", bufs=2)
+                nc.scalar.activation(row[:], turned[:].rearrange("j t p -> j p t"), ACT.Copy, scale=-1.0)
+                rows[n].append(row)
+
+        def turn_back(n):
+            b, g0, width = groups[n]
+            pairs = psum.tile([P, len(steps(n)), 2, LIN_N], F32, name="bank_pairs", tag="bank_c", bufs=C_BANKS)
+            for s, row in enumerate(rows[n]):
+                words = row[:].rearrange("j p t -> j (p t)").bitcast(F32).rearrange("j (p u) -> j u p", u=2)
+                for u in range(2):
+                    nc.tensor.transpose(pairs[:, s, u, :], words[:, u, :], identity[:])
+            nc.scalar.copy(
+                h_bf[g0 // HALF][:, b, g0 % HALF : g0 % HALF + width, :].rearrange("p j t -> p (j t)").bitcast(F32).rearrange("p (s j u) -> p s j u", s=len(rows[n]), u=2),
+                pairs[:].rearrange("p s u j -> p s j u"),
+            )
+
+        def weigh_from_bank(i, tag):
+            weighted[i] = keep.tile([P, HALF], F32, name="weighted%d" % i, tag=tag, align_bytes=64)
             nc.vector.tensor_tensor(weighted[i][:], projection_bank(i, 0, True)[:], wgo_sb[:, :HALF], ALU.mult)
 
         def place_fused(i):
@@ -408,7 +456,7 @@ def tile_list_motet_voice_completion_kernel(
             y[i] = projection(i, 0, tag)
 
         def weigh(i, tag="weighted"):
-            weighted[i] = ring.tile([P, HALF], F32, name="weighted", tag=tag)
+            weighted[i] = ring.tile([P, HALF], F32, name="weighted", tag=tag, bufs=1)
             nc.gpsimd.tensor_tensor(weighted[i][:], y[i][:], wgo_sb[:, :HALF], ALU.mult)
 
         def place(i):
@@ -453,44 +501,47 @@ def tile_list_motet_voice_completion_kernel(
         d_vector(5, 0)
         h_of(3)
         linear_of(5, 1)
-        tanh_of(6)
-        linear_of(6, 0)
         gate_of(6)
+        gate_of(7)
         wd_first = round_wd(slot(3))
         d_vector(5, 1)
-        product(5, None, "e5")
-        d_vector(6, 0)
+        product(5, None, "e2")
         h_of(4)
-        linear_of(6, 1)
-        gate_of(7)
-        tanh_of(7)
-        product(6, 0)
-        d_vector(6, 1)
+        linear_of(6)
+        linear_share(6)
+        linear_of(7, 0)
+        linear_share(7, 0)
+        tanh_of(6)
+        scale_of(6, negated)
         h_of(5)
+        wd_mx[0] = quantise(wd_first[:, : PASS * PACK], PASS, "wd0", "d5")
         quantise_h(0)
-        wd_mx[0] = quantise(wd_first, PASSES * PACK * P, "wd", "e5")
-        product(6, 1, slot(3))
-        scale_of(7)
-        linear_of(7)
-        linear_share(7)
+        wd_mx[1] = quantise(wd_first[:, PASS * PACK :], PASS, "wd1", "e2")
+        tanh_share(6, slot(3))
+        tanh_of(7)
+        linear_of(7, 1)
+        linear_share(7, 1)
+        weigh_from_bank(0, "weighted0")
+        scale_of(7, negated)
         tanh_share(7)
-        weigh_from_bank(0)
-        project(1)
-        h_of(6)
-        weigh(1)
         place(0)
         gate_of(8)
-        tanh_of(8)
-        scale_of(8)
+        project(1)
+        weigh(1)
         linear_of(8)
-        join(7)
         linear_share(8)
-        place(1)
-        weigh_from_bank(2)
-        tanh_share(8)
-        join(8)
-        project(3, "e2")
+        tanh_of(8)
+        weigh_from_bank(2, "wb1_codes")
         place(2)
+        scale_of(8)
+        tanh_share(8, 0)
+        place(1)
+        join_on_tensor(6, 4096, False)
+        join_on_tensor(7, 5120, True)
+        turn_back(6)
+        turn_back(7)
+        join(8)
+        project(3, 2048)
         quantise_h(1)
         place_fused(3)
 

@@ -23,12 +23,28 @@ RUN = 8
 BLOCKS = P // RUN
 PASS = P * PACK
 PASSES = H // PASS
-HALF = 512
-HALVES = S // HALF
-GATE_N = 256
-LIN_N = 128
-C_BANKS = 5
+LIST_ROWS = 16
+QUADRANT = 32
 BANK = 512
+HALF = S // 2
+QUARTER = S // 4
+STEP = BANK // PACK
+SLOW_BANKS = 5
+SCALAR_BANKS = 8 - SLOW_BANKS
+SCALAR_BLOCKS = 2
+
+GROUPS = [(0, 0, STEP), (0, STEP, STEP), (0, QUARTER, QUARTER), (0, 2 * QUARTER, QUARTER)]
+GROUPS = GROUPS + [(1, 0, QUARTER), (1, QUARTER, QUARTER)]
+LAST_OF_HALF = len(GROUPS) - 1
+GROUPS = GROUPS + [(0, 3 * QUARTER, QUARTER), (1, 2 * QUARTER, QUARTER), (1, 3 * QUARTER, QUARTER)]
+LATE_A, LATE_B, LAST = range(LAST_OF_HALF + 1, len(GROUPS))
+
+GROUP_BYTES = PACK * QUARTER * 4
+ROW_BYTES = P * PACK * 2
+LAST_SHARE_AT = 0
+LAST_ROWS_AT = {LATE_A: GROUP_BYTES, LATE_B: GROUP_BYTES + ROW_BYTES}
+LAST_Y_AT = GROUP_BYTES // 2
+HALF_DIFFERENCE_AT = GROUP_BYTES + 2 * ROW_BYTES
 
 
 def tile_list_motet_voice_completion_kernel(
@@ -38,11 +54,10 @@ def tile_list_motet_voice_completion_kernel(
     with ExitStack() as ctx:
         keep = ctx.enter_context(tc.tile_pool(name="keep", bufs=1))
         ring = ctx.enter_context(tc.tile_pool(name="ring", bufs=2))
-        psum = ctx.enter_context(tc.psum_pool(name="psum", bufs=8 - C_BANKS))
+        psum = ctx.enter_context(tc.psum_pool(name="psum", bufs=SCALAR_BANKS))
+        placed = ctx.enter_context(tc.tile_pool(name="placed", bufs=1))
 
-        shared = ctx.enter_context(tc.tile_pool(name="shared", bufs=1))
-
-        offs_sb = keep.tile([P, S // 16], U16, name="offs_sb")
+        offs_sb = keep.tile([P, S // LIST_ROWS], U16, name="offs_sb")
         nc.sync.dma_start(offs_sb[:], offs)
         tab_bytes = keep.tile([P, T], U8, name="tab_bytes", align_bytes=64)
         nc.sync.dma_start(
@@ -50,9 +65,9 @@ def tile_list_motet_voice_completion_kernel(
             tab_scales[0].bitcast(I32).unsqueeze(1).broadcast_to([BLOCKS, RUN, T // 4]),
         )
         raw_scales = keep.tile([P, 2, H], U8, name="raw_scales", align_bytes=64)
-        for slot, scales in enumerate((wa_scales, wc_scales)):
-            rows = scales[0].bitcast(I32).unsqueeze(1).broadcast_to([BLOCKS, RUN, H // 4])
-            nc.sync.dma_start(raw_scales[:, slot, :].bitcast(I32), rows)
+        for which, scales in enumerate((wa_scales, wc_scales)):
+            repeated = scales[0].bitcast(I32).unsqueeze(1).broadcast_to([BLOCKS, RUN, H // 4])
+            nc.sync.dma_start(raw_scales[:, which, :].bitcast(I32), repeated)
 
         gain_rows = keep.tile([P, P], F32, name="gain_rows")
         nc.gpsimd.memset(gain_rows[:], 0.0)
@@ -62,32 +77,23 @@ def tile_list_motet_voice_completion_kernel(
                 gain_rows[b * PACK : (b + 1) * PACK, :].rearrange("t (q i) -> t q i", i=RUN), gain_src[b]
             )
 
-        wb_rows = wb.rearrange("(p j) c -> p j c", j=PACK)
-        wb_raw = {}
-
-        def load_wb(b, c0, tiles):
-            wb_raw.setdefault(b, []).extend(tiles)
-            c0 = c0 + b * PASS
-            for piece in tiles:
-                nc.sync.dma_start(piece, wb_rows[:, :, c0 : c0 + piece.shape[2]])
-                c0 = c0 + piece.shape[2]
-
         tab = keep.tile([P, T], U32, name="tab", align_bytes=64)
         nc.sync.dma_start(tab[:].bitcast(I32), tab_words[0].rearrange("p t i -> p (t i)").bitcast(I32))
         wa_rows = wa_words[0].bitcast(I32)
         wa_first = keep.tile([P, PASS // 2], I32, name="wa_first", align_bytes=64)
         nc.sync.dma_start(wa_first[:], wa_rows[:, : PASS // 2])
-        wb_first = keep.tile([P, PACK, PASS // 2], F32, name="wb_first", align_bytes=64)
-        wb_next = keep.tile([P, PACK, PASS // 2], F32, name="wb_next", align_bytes=64)
-        load_wb(0, 0, [wb_first[:], wb_next[:]])
+        wb_rows = wb.rearrange("(p row) c -> p row c", row=PACK)
+        wb_pieces = [keep.tile([P, PACK, PASS // 2], F32, name="wb_piece%d" % piece, align_bytes=64) for piece in range(2)]
+        for piece in range(2):
+            nc.sync.dma_start(wb_pieces[piece][:], wb_rows[:, :, piece * PASS // 2 : (piece + 1) * PASS // 2])
 
-        offs2_sb = keep.tile([P, S // 16], U16, name="offs2_sb")
+        offs2_sb = keep.tile([P, S // LIST_ROWS], U16, name="offs2_sb")
         nc.sync.dma_start(offs2_sb[:], offs2)
         planes = keep.tile([P, 2 * H + S], U8, name="planes", align_bytes=64)
         identity = keep.tile([P, P], F32, name="identity")
         make_identity(nc, identity[:])
 
-        pages = [keep.tile([P, T2], F32, name="page%d" % n) for n in range(PACK - 1)]
+        pages = [keep.tile([P, T2], F32, name="page%d" % pg) for pg in range(PACK - 1)]
         for cols in (slice(0, T2 // 2 - 1), slice(T2 // 2 - 1, T2)):
             nc.vector.memset(pages[0][:, cols].bitcast(I32), 0)
         for page in pages[1:]:
@@ -95,7 +101,6 @@ def tile_list_motet_voice_completion_kernel(
 
         w_scales = planes[:, : 2 * H].rearrange("p (s c) -> p s c", s=2)
         v_plane = planes[:, 2 * H :]
-
         v_bytes = keep.tile([P, S], U8, name="v_bytes", align_bytes=64)
         nc.vector.tensor_copy(v_bytes[:], tab_bytes[:].indirect(offs_sb[:]))
         nc.vector.tensor_copy(
@@ -104,24 +109,23 @@ def tile_list_motet_voice_completion_kernel(
                 "p (g q t w) -> p g t q w", t=PACK, q=BLOCKS, w=RUN // 4
             ),
         )
-        nc.vector.tensor_copy(planes[:, 2 * H :].bitcast(I32), v_bytes[:].bitcast(I32))
-        for r in range(1, 4):
-            nc.sync.dma_start(planes[r:P:32, :].bitcast(I32), planes[RUN * r : P : 32, :].bitcast(I32))
+        nc.vector.tensor_copy(v_plane.bitcast(I32), v_bytes[:].bitcast(I32))
+        for x in range(1, PACK):
+            nc.sync.dma_start(planes[x:P:QUADRANT, :].bitcast(I32), planes[RUN * x : P : QUADRANT, :].bitcast(I32))
 
-        last_page = keep.tile([P, T2], F32, name="page3", tag="raw_scales", align_bytes=64)
-        pages.append(last_page)
-        nc.gpsimd.memset(last_page[:], 0.0)
+        pages.append(keep.tile([P, T2], F32, name="page3", tag="raw_scales", align_bytes=64))
+        nc.gpsimd.memset(pages[-1][:], 0.0)
 
         words_raw = keep.tile([P, H + PASS // 2], I32, name="words_raw", tag="v_bytes", align_bytes=64)
-        wc_raw = words_raw[:, :H]
         wc_rows = wc_words[0].rearrange("p e i -> p (e i)").bitcast(I32)
         for b in range(PASSES):
-            nc.sync.dma_start(wc_raw[:, b * PASS : (b + 1) * PASS], wc_rows[:, b * PASS : (b + 1) * PASS])
+            nc.sync.dma_start(words_raw[:, b * PASS : (b + 1) * PASS], wc_rows[:, b * PASS : (b + 1) * PASS])
         nc.sync.dma_start(words_raw[:, H:], wa_rows[:, PASS // 2 :])
         widths = [PACK * PASS, PASSES * PACK * N, S]
-        late = keep.tile([P, sum(widths)], F32, name="late", tag="wb_first", align_bytes=64)
-        parts = [late[:, sum(widths[:n]) : sum(widths[: n + 1])] for n in range(len(widths))]
-        load_wb(1, 0, [part.rearrange("p (j c) -> p j c", j=PACK) for part in parts[:1]])
+        late = keep.tile([P, sum(widths)], F32, name="late", tag="wb_piece0", align_bytes=64)
+        parts = [late[:, sum(widths[:part]) : sum(widths[: part + 1])] for part in range(len(widths))]
+        wb_second = parts[0].rearrange("p (row c) -> p row c", row=PACK)
+        nc.sync.dma_start(wb_second, wb_rows[:, :, PASS:])
         wd_rows = wd.rearrange("(b q t i) n -> b t q i n", b=PASSES, t=PACK, i=RUN)
         wd_raw = parts[1].rearrange("p (b t n) -> p b t n", b=PASSES, t=PACK)
         for b in range(PASSES):
@@ -130,423 +134,350 @@ def tile_list_motet_voice_completion_kernel(
         wgo_sb = parts[2]
         nc.sync.dma_start(wgo_sb, wgo)
 
-        def reorder(raw, passes, name, tag=None):
-            codes = keep.tile(list(raw.shape), I32, name=name, tag=tag or name, align_bytes=64)
+        h_bf = [keep.tile([P, PASSES, HALF, PACK], BF16, name="h_bf%d" % half, align_bytes=64) for half in range(2)]
+
+        def reorder(raw, name):
+            codes = keep.tile(list(raw.shape), I32, name=name, align_bytes=64)
             nc.vector.tensor_copy(
-                codes[:].rearrange("p (b t q w) -> p b t q w", b=passes, t=PACK, q=BLOCKS),
-                raw.rearrange("p (b q t w) -> p b t q w", b=passes, t=PACK, q=BLOCKS),
+                codes[:].rearrange("p (t q w) -> p t q w", t=PACK, q=BLOCKS),
+                raw.rearrange("p (q t w) -> p t q w", t=PACK, q=BLOCKS),
             )
             return codes
 
         def gather_words(j0, width, tag):
             words = keep.tile([P, width], U32, name="v_words%d" % j0, tag=tag, align_bytes=64)
-            nc.vector.tensor_copy(words[:], tab[:].indirect(offs_sb[:, j0 // 16 : (j0 + width) // 16]))
+            nc.vector.tensor_copy(words[:], tab[:].indirect(offs_sb[:, j0 // LIST_ROWS : (j0 + width) // LIST_ROWS]))
             return words
 
-        def round_wb(b, tag, shares):
-            grouped = keep.tile([P, PACK, BLOCKS, RUN, PACK], BF16, name="wb_grouped%d" % b, tag=tag, align_bytes=64)
-            q0 = 0
-            for copy, order, piece, q, count in shares:
-                blocks = wb_raw[b][piece].rearrange("p j (q t i) -> " + order, t=PACK, i=RUN)
-                copy(
-                    grouped[:, :, q0 : q0 + count].rearrange("p t q i j -> " + order),
-                    blocks[:, :, q : q + count],
-                )
-                q0 = q0 + count
-            return grouped[:].rearrange("p t q i j -> p (t q i j)")
-
-        def quantise(grouped, width, name, tag=None):
-            codes = keep.tile([P, width], U32, name=name + "_codes", tag=tag or name + "_codes", align_bytes=64)
+        def quantise(grouped, name, tag):
+            width = grouped.shape[1] // PACK
+            codes = keep.tile([P, width], U32, name=name + "_codes", tag=tag, align_bytes=64)
             plane = keep.tile([P, width], U8, name=name + "_plane", align_bytes=64)
             nc.vector.quantize_mx(out=codes[:].bitcast(FP8X4), scales=plane[:], in_=grouped)
             return codes, plane
 
-        h_bf = [keep.tile([P, PASSES, HALF, PACK], BF16, name="h_bf%d" % half, align_bytes=64) for half in range(HALVES)]
+        v_first = gather_words(0, QUARTER, "v_first")
+        wa_codes = {0: reorder(wa_first[:], "wa_codes0")}
+        v_rest = gather_words(QUARTER, S - QUARTER, "tab_bytes")
 
-        def v_cols(j0, width):
-            if j0 < GATE_N:
-                words = v_first[:, j0 : j0 + width]
-            else:
-                words = v_rest[:, j0 - GATE_N : j0 - GATE_N + width]
-            return words.bitcast(FP8X4), v_plane[:, j0 : j0 + width]
+        wb_grouped = keep.tile([P, PACK, BLOCKS, RUN, PACK], BF16, name="wb_grouped0", align_bytes=64)
+        piece_blocks = BLOCKS // 2
+        shares = [(nc.scalar.copy, "p t q row i", 0, q, piece_blocks // 2) for q in (0, piece_blocks // 2)]
+        shares.append((nc.scalar.copy, "p t q row i", 1, 0, SCALAR_BLOCKS))
+        shares.append((nc.vector.tensor_copy, "p t q i row", 1, SCALAR_BLOCKS, piece_blocks - SCALAR_BLOCKS))
+        for copy, order, piece, q, count in shares:
+            blocks = wb_pieces[piece][:].rearrange("p row (q t i) -> " + order, t=PACK, i=RUN)
+            q0 = piece * piece_blocks + q
+            copy(wb_grouped[:, :, q0 : q0 + count].rearrange("p t q i row -> " + order), blocks[:, :, q : q + count])
+        wb_mx = {0: quantise(wb_grouped[:].rearrange("p t q i row -> p (t q i row)"), "wb0", "wb0_codes")}
 
-        def tanh_branch(b, j0, width):
-            wb_codes, wb_plane = wb_mx[b]
-            rhs, rhs_scale = v_cols(j0, width)
-            per_bank = BANK // width
-            tb = []
-            for t0 in range(0, PACK, per_bank):
-                bank = psum.tile([P, per_bank, width], F32, name="bank_b", tag="scalar_bank")
-                for t in range(t0, t0 + per_bank):
-                    nc.tensor.matmul_mx(
-                        out=bank[:, t - t0, :],
-                        lhsT=wb_codes[:, t * P : (t + 1) * P].bitcast(FP8X4),
-                        lhsT_scale=wb_plane[:, t * P : (t + 1) * P],
-                        rhs=rhs, rhs_scale=rhs_scale, start=True, stop=True,
-                    )
-                name = "tb%d_%d_%d" % (b, j0, t0)
-                tag = "tb%d_%d_%d" % (b, j0 - HALF, t0) if b == 1 and j0 >= HALF else name
-                part = keep.tile([P, per_bank, width], F32, name=name, tag=tag, align_bytes=64)
-                nc.scalar.activation(part[:], bank[:], ACT.Tanh)
-                tb.extend(part[:, t, :] for t in range(per_bank))
-            return tb
-
-        def gate(b, j0, width):
-            rhs, rhs_scale = v_cols(j0, width)
-            per_bank = BANK // width
-            z = ring.tile([P, PACK, width], F32, name="z", bufs=4)
-            for t0 in range(0, PACK, per_bank):
-                bank = psum.tile([P, per_bank, width], F32, name="bank_a", tag="scalar_bank")
-                for t in range(t0, t0 + per_bank):
-                    c0 = b * PASS + t * P
-                    nc.tensor.matmul_mx(
-                        out=bank[:, t - t0, :],
-                        lhsT=wa_codes[b][:].bitcast(U8)[:, 2 * t * P : 2 * (t + 1) * P].bitcast(FP4X4),
-                        lhsT_scale=w_scales[:, 0, c0 : c0 + P],
-                        rhs=rhs, rhs_scale=rhs_scale, start=True, stop=True,
-                    )
-                nc.scalar.activation(z[:, t0 : t0 + per_bank, :], bank[:], ACT.Sigmoid)
-            return z
-
-        def gates(b, j0, width):
-            return tanh_branch(b, j0, width), gate(b, j0, width)
-
-        def linear_branch(b, j0):
-            rhs, rhs_scale = v_cols(j0, LIN_N)
-            bank = psum.tile([P, PACK, LIN_N], F32, name="bank_c", bufs=C_BANKS)
-            for t in range(PACK):
-                c0 = b * PASS + t * P
-                nc.tensor.matmul_mx(
-                    out=bank[:, t, :],
-                    lhsT=wc_codes[b][:, t * P : (t + 1) * P].bitcast(FP8X4),
-                    lhsT_scale=w_scales[:, 1, c0 : c0 + P],
-                    rhs=rhs, rhs_scale=rhs_scale, start=True, stop=True,
-                )
-            return bank
-
-        def difference(b, cols, slices, tb, bank, d):
-            for t in slices:
-                nc.vector.scalar_tensor_tensor(
-                    d[:, t, cols], tb[t][:, cols], gains[:, b * PACK + t : b * PACK + t + 1], bank[:, t, :], ALU.mult, ALU.subtract
-                )
-
-        def interpolate(b, j0, e, bank):
-            nc.vector.tensor_tensor(
-                h_bf[j0 // HALF][:, b, j0 % HALF : j0 % HALF + LIN_N, :].rearrange("p (c i) t -> p c t i", i=2),
-                e.rearrange("p t (c i) -> p c t i", i=2),
-                bank[:].rearrange("p t (c i) -> p c t i", i=2),
-                ALU.add,
-            )
-
-        def round_wd(tag):
-            grouped = keep.tile([P, 2, PASSES, 2, P, PACK], BF16, name="wd_grouped", tag=tag, align_bytes=64)
-            for u in range(2):
-                for b in range(PASSES):
-                    for m0 in range(0, P, P // 2):
-                        nc.scalar.copy(
-                            grouped[:, u, b, :, m0 : m0 + P // 2, :].rearrange("p i m t -> p m t i"),
-                            wd_raw[:, b, :, PACK * m0 : PACK * (m0 + P // 2)].rearrange("p t (m i) -> p m t i", i=PACK)[
-                                :, :, :, 2 * u : 2 * u + 2
-                            ],
-                        )
-            return grouped[:].rearrange("p u b i m t -> p (u b i m t)")
-
-        def projection_bank(i, half, for_vector=False):
-            wd_codes, wd_plane = wd_mx[i // 2]
-            h_codes, h_plane = h_mx[half]
-            if for_vector:
-                bank = psum.tile([P, HALF], F32, name="bank_y", tag="bank_c", bufs=C_BANKS)
-            else:
-                bank = psum.tile([P, HALF], F32, name="bank_y", tag="scalar_bank")
-            for b in range(PASSES):
-                w_cols = slice((2 * b + i % 2) * P, (2 * b + i % 2 + 1) * P)
-                h_cols = slice(b * HALF, (b + 1) * HALF)
-                nc.tensor.matmul_mx(
-                    out=bank[:],
-                    lhsT=wd_codes[:, w_cols].bitcast(FP8X4),
-                    lhsT_scale=wd_plane[:, w_cols],
-                    rhs=h_codes[:, h_cols].bitcast(FP8X4),
-                    rhs_scale=h_plane[:, h_cols],
-                    start=(b == 0), stop=(b == PASSES - 1),
-                )
-            return bank
-
-        def projection(i, half, tag=None):
-            if tag is None:
-                y = keep.tile([P, HALF], F32, name="y%d_%d" % (i, half), tag="y%d" % i, align_bytes=64)
-            else:
-                y = shared.tile([P, 2 * HALF], F32, name="y%d_%d" % (i, half), offset=tag)[:, :HALF]
-            nc.scalar.copy(y[:], projection_bank(i, half, tag is not None)[:])
-            return y
-
-        def window(i, half):
-            return pages[i][:].indirect(offs2_sb[:, half * HALF // 16 : (half + 1) * HALF // 16])
-
-        def quantise_h(half, tag=None):
-            h_mx[half] = quantise(h_bf[half][:].rearrange("p b j t -> p (b j t)"), PASSES * HALF, "h%d" % half, tag)
-
-        wb_mx, wd_mx, h_mx = {}, {}, {}
-        v_first = gather_words(0, GATE_N, "v_first")
-        wa_codes = {0: reorder(wa_first[:], 1, "wa_codes0")}
-        v_rest = gather_words(GATE_N, S - GATE_N, "tab_bytes")
-        quarter = BLOCKS // 4
-        shares = [(nc.scalar.copy, "p t q j i", 0, 0, quarter), (nc.scalar.copy, "p t q j i", 0, quarter, quarter)]
-        shares = shares + [(nc.scalar.copy, "p t q j i", 1, 0, 2), (nc.vector.tensor_copy, "p t q i j", 1, 2, 6)]
-        wb_mx[0] = quantise(round_wb(0, "wb_grouped0", shares), PASS, "wb0")
         gain_bank = psum.tile([P, P], F32, name="gain_bank", tag="scalar_bank")
         nc.tensor.transpose(gain_bank[:], gain_rows[:], identity[:])
         gains = keep.tile([P, PASSES * PACK], F32, name="gains")
         nc.scalar.copy(gains[:], gain_bank[:, : PASSES * PACK])
-        negated = keep.tile([P, PASSES * PACK], F32, name="negated")
-        nc.gpsimd.tensor_scalar(negated[:], gains[:], -1.0, 0.0, ALU.mult, ALU.add)
+        negated_gains = keep.tile([P, PASSES * PACK], F32, name="negated_gains")
+        nc.gpsimd.tensor_scalar(negated_gains[:], gains[:], -1.0, 0.0, ALU.mult, ALU.add)
+        wc_codes = {0: reorder(words_raw[:, :PASS], "wc_codes0")}
 
-        wc_codes = {0: reorder(wc_raw[:, :PASS], 1, "wc_codes0")}
+        tanh, gate, c_banks, from_c, from_gate, h_rows = {}, {}, {}, {}, {}, {}
+        wd_mx, h_mx = {}, {}
 
-        def second_pass(tag):
+        def steps(n):
+            return [slice(j, j + STEP) for j in range(0, GROUPS[n][2], STEP)]
+
+        def first_stage(bank, codes, plane, j0, width):
+            words = v_first[:, j0 : j0 + width] if j0 < QUARTER else v_rest[:, j0 - QUARTER : j0 - QUARTER + width]
+            nc.tensor.matmul_mx(
+                out=bank, lhsT=codes, lhsT_scale=plane,
+                rhs=words.bitcast(FP8X4), rhs_scale=v_plane[:, j0 : j0 + width], start=True, stop=True,
+            )
+
+        def tanh_tag(n, t0):
+            return "tanh%d_%d" % (n - (LAST - LAST_OF_HALF) if n > LATE_A else n, t0)
+
+        def tanh_of(n):
+            b, j0, width = GROUPS[n]
+            codes, plane = wb_mx[b]
+            per_bank = BANK // width
+            tanh[n] = []
+            for t0 in range(0, PACK, per_bank):
+                bank = psum.tile([P, per_bank, width], F32, name="bank_b", tag="scalar_bank")
+                for t in range(t0, t0 + per_bank):
+                    cols = slice(t * P, (t + 1) * P)
+                    first_stage(bank[:, t - t0, :], codes[:, cols].bitcast(FP8X4), plane[:, cols], j0, width)
+                part = keep.tile([P, per_bank, width], F32, name="tanh", tag=tanh_tag(n, t0), align_bytes=64)
+                nc.scalar.activation(part[:], bank[:], ACT.Tanh)
+                tanh[n].extend(part[:, t, :] for t in range(per_bank))
+
+        def gate_of(n):
+            b, j0, width = GROUPS[n]
+            per_bank = BANK // width
+            gate[n] = ring.tile([P, PACK, width], F32, name="gate", bufs=4)
+            for t0 in range(0, PACK, per_bank):
+                bank = psum.tile([P, per_bank, width], F32, name="bank_a", tag="scalar_bank")
+                for t in range(t0, t0 + per_bank):
+                    codes = wa_codes[b][:].bitcast(U8)[:, 2 * t * P : 2 * (t + 1) * P].bitcast(FP4X4)
+                    c0 = b * PASS + t * P
+                    first_stage(bank[:, t - t0, :], codes, w_scales[:, 0, c0 : c0 + P], j0, width)
+                nc.scalar.activation(gate[n][:, t0 : t0 + per_bank, :], bank[:], ACT.Sigmoid)
+
+        def linear_of(n, step):
+            b, j0, width = GROUPS[n]
+            bank = psum.tile([P, PACK, STEP], F32, name="bank_c", tag="slow_bank", bufs=SLOW_BANKS)
+            for t in range(PACK):
+                codes = wc_codes[b][:, t * P : (t + 1) * P].bitcast(FP8X4)
+                c0 = b * PASS + t * P
+                first_stage(bank[:, t, :], codes, w_scales[:, 1, c0 : c0 + P], j0 + step * STEP, STEP)
+            c_banks[n, step] = bank
+
+        def from_c_tile(n):
+            if n not in from_c and n == LAST_OF_HALF:
+                from_c[n] = placed.tile(
+                    [P, PACK, QUARTER], F32, name="from_c_half", offset=HALF_DIFFERENCE_AT, align_bytes=64
+                )
+            if n not in from_c:
+                from_c[n] = ring.tile([P, PACK, GROUPS[n][2]], F32, name="from_c", bufs=3)
+            return from_c[n]
+
+        def h_cols(n, j, width):
+            b, j0 = GROUPS[n][:2]
+            return h_bf[j0 // HALF][:, b, j0 % HALF + j : j0 % HALF + j + width, :]
+
+        def by_pairs(tile):
+            return tile.rearrange("p t (c two) -> p c t two", two=2)
+
+        def woven(h_part):
+            return h_part.rearrange("p (c two) t -> p c t two", two=2)
+
+        def difference(n, step, slices):
+            b, cols = GROUPS[n][0], steps(n)[step]
+            for t in slices:
+                nc.vector.scalar_tensor_tensor(
+                    from_c_tile(n)[:, t, cols], tanh[n][t][:, cols], gains[:, b * PACK + t : b * PACK + t + 1],
+                    c_banks[n, step][:, t, :], ALU.mult, ALU.subtract,
+                )
+
+        def multiply(n, left, right, tag):
+            from_gate[n] = keep.tile([P, PACK, GROUPS[n][2]], F32, name="from_gate", tag=tag, align_bytes=64)
+            nc.gpsimd.tensor_tensor(from_gate[n][:], left[:], right[:], ALU.mult)
+
+        def product(n, tag):
+            multiply(n, from_c[n], gate[n], tag)
+
+        def product_tag(n):
+            return "product%d" % (n % 3)
+
+        def interpolate(n):
+            for step, cols in enumerate(steps(n)):
+                nc.vector.tensor_tensor(
+                    woven(h_cols(n, cols.start, STEP)),
+                    by_pairs(from_gate[n][:, :, cols]), by_pairs(c_banks[n, step][:]), ALU.add,
+                )
+
+        def linear_share(n, step):
+            cols = steps(n)[step]
+            nc.vector.scalar_tensor_tensor(
+                from_c_tile(n)[:, :, cols], gate[n][:, :, cols], 1.0, c_banks[n, step][:], ALU.subtract, ALU.mult
+            )
+
+        def scaled_tanh(n, factors):
+            b = GROUPS[n][0]
+            scaled = ring.tile([P, PACK, QUARTER], F32, name="scaled")
+            for t in range(PACK):
+                factor = factors[:, b * PACK + t : b * PACK + t + 1]
+                nc.scalar.activation(scaled[:, t, :], tanh[n][t], ACT.Copy, scale=factor)
+            return scaled
+
+        def sum_on_tensor(n, tag, bufs):
+            h_rows[n] = []
+            for cols in steps(n):
+                turned = psum.tile([P, PACK, P], F32, name="bank_turned", tag=tag, bufs=bufs)
+                for t in range(PACK):
+                    for term, share in enumerate((from_gate[n], from_c[n])):
+                        nc.tensor.matmul(
+                            out=turned[:, t, :], lhsT=share[:, t, cols], rhs=identity[:],
+                            is_transpose=True, start=(term == 0), stop=(term == 1),
+                        )
+                if cols.start == 0:
+                    rows = ring.tile([P, P, PACK], BF16, name="h_rows")
+                else:
+                    rows = placed.tile([P, P, PACK], BF16, name="last_rows%d" % n, offset=LAST_ROWS_AT[n])
+                nc.scalar.activation(rows[:], turned[:].rearrange("j t p -> j p t"), ACT.Copy, scale=-1.0)
+                h_rows[n].append(rows)
+
+        def turn_back(n):
+            pairs = psum.tile([P, 2, 2, STEP], F32, name="bank_pairs", tag="slow_bank", bufs=SLOW_BANKS)
+            for step, rows in enumerate(h_rows[n]):
+                row_words = rows[:].rearrange("j p t -> j (p t)").bitcast(F32).rearrange("j (p u) -> j u p", u=2)
+                for u in range(2):
+                    nc.tensor.transpose(pairs[:, step, u, :], row_words[:, u, :], identity[:])
+            h_words = h_cols(n, 0, QUARTER).rearrange("p j t -> p (j t)").bitcast(F32)
+            nc.scalar.copy(
+                h_words.rearrange("p (step j u) -> p step j u", step=2, u=2),
+                pairs[:].rearrange("p step u j -> p step j u"),
+            )
+
+        def second_pass_weights(tag):
             grouped = keep.tile([P, PACK, BLOCKS, RUN, PACK], BF16, name="wb_grouped1", tag=tag, align_bytes=64)
             codes = keep.tile([P, PASS], U32, name="wb1_codes", align_bytes=64)
             plane = keep.tile([P, PASS], U8, name="wb1_plane", align_bytes=64)
-            blocks = wb_raw[1][0].rearrange("p j (q t i) -> p t q i j", t=PACK, i=RUN)
+            blocks = wb_second.rearrange("p row (q t i) -> p t q i row", t=PACK, i=RUN)
             for t0 in range(0, PACK, 2):
                 nc.vector.tensor_copy(grouped[:, t0 : t0 + 2], blocks[:, t0 : t0 + 2])
             for t0 in range(0, PACK, 2):
                 cols = slice(t0 * P, (t0 + 2) * P)
                 nc.vector.quantize_mx(
                     out=codes[:, cols].bitcast(FP8X4), scales=plane[:, cols],
-                    in_=grouped[:, t0 : t0 + 2].rearrange("p t q i j -> p (t q i j)"),
+                    in_=grouped[:, t0 : t0 + 2].rearrange("p t q i row -> p (t q i row)"),
                 )
                 if t0 == 0:
-                    wc_codes[1] = reorder(wc_raw[:, PASS:], 1, "wc_codes1")
-                    wa_codes[1] = reorder(words_raw[:, H:], 1, "wa_codes1")
+                    wc_codes[1] = reorder(words_raw[:, PASS:H], "wc_codes1")
+                    wa_codes[1] = reorder(words_raw[:, H:], "wa_codes1")
             wb_mx[1] = codes, plane
 
-        groups = [(0, j0, LIN_N) for j0 in range(0, GATE_N, LIN_N)]
-        groups = groups + [(b, q * GATE_N, GATE_N) for b, q in ((0, 1), (0, 2), (1, 0), (1, 1), (0, 3), (1, 2), (1, 3))]
-        tb, z, banks, d, e, y, weighted, scaled, copied = {}, {}, {}, {}, {}, {}, {}, {}, {}
-
-        def steps(n):
-            return [slice(l0, l0 + LIN_N) for l0 in range(0, groups[n][2], LIN_N)]
-
-        def tanh_of(n):
-            tb[n] = tanh_branch(*groups[n])
-
-        def gate_of(n):
-            z[n] = gate(*groups[n])
-
-        def gates_of(n):
-            tanh_of(n)
-            gate_of(n)
-
-        def linear_of(n, step=None):
-            b, g0, width = groups[n]
-            for cols in steps(n) if step is None else [steps(n)[step]]:
-                banks.setdefault(n, []).append(linear_branch(b, g0 + cols.start))
-
-        def d_vector(n, step=None):
-            b, g0, width = groups[n]
-            if n not in d and n == 5:
-                d[n] = keep.tile([P, PACK, width], F32, name="d5", align_bytes=64)
-            if n not in d:
-                d[n] = ring.tile([P, PACK, width], F32, name="d", bufs=3)
-            if step is not None:
-                difference(b, steps(n)[step], range(PACK), tb[n], banks[n][step], d[n])
-                return
-            for t0 in range(0, PACK, 2):
-                for cols, bank in zip(steps(n), banks[n]):
-                    difference(b, cols, range(t0, t0 + 2), tb[n], bank, d[n])
-
-        def stage(n):
-            b, g0, width = groups[n]
-            scaled[n] = ring.tile([P, PACK, width], F32, name="scaled")
-            copied[n] = ring.tile([P, PACK, width], F32, name="copied")
-            for t in range(PACK):
-                nc.scalar.activation(scaled[n][:, t, :], tb[n][t], ACT.Copy, scale=gains[:, b * PACK + t : b * PACK + t + 1])
-            for cols, bank in zip(steps(n), banks[n]):
-                nc.scalar.copy(copied[n][:, :, cols], bank[:])
-
-        def scale_of(n, gains=gains):
-            b, g0, width = groups[n]
-            scaled[n] = ring.tile([P, PACK, width], F32, name="scaled")
-            for t in range(PACK):
-                nc.scalar.activation(scaled[n][:, t, :], tb[n][t], ACT.Copy, scale=gains[:, b * PACK + t : b * PACK + t + 1])
-
-        def linear_share(n, step=None):
-            if n not in d:
-                d[n] = ring.tile([P, PACK, groups[n][2]], F32, name="d", bufs=3)
-            for cols, bank in zip(steps(n), banks[n]) if step is None else [(steps(n)[step], banks[n][step])]:
-                nc.vector.scalar_tensor_tensor(d[n][:, :, cols], z[n][:, :, cols], 1.0, bank[:], ALU.subtract, ALU.mult)
-
-        def tanh_share(n, tag=None):
-            if tag == 0:
-                e[n] = shared.tile([P, PACK, groups[n][2]], F32, name="e%d" % n, offset=0)
-            else:
-                e[n] = keep.tile([P, PACK, groups[n][2]], F32, name="e%d" % n, tag=tag or "e%d" % (n % 3), align_bytes=64)
-            nc.gpsimd.tensor_tensor(e[n][:], z[n][:], scaled[n][:], ALU.mult)
-
-        def join(n):
-            b, g0, width = groups[n]
-            nc.gpsimd.tensor_tensor(
-                h_bf[g0 // HALF][:, b, g0 % HALF : g0 % HALF + width, :].rearrange("p (c i) t -> p c t i", i=2),
-                e[n][:].rearrange("p t (c i) -> p c t i", i=2),
-                d[n][:].rearrange("p t (c i) -> p c t i", i=2),
-                ALU.subtract,
-            )
-
-        rows = {}
-
-        def join_on_tensor(n, offset, scalar_banks, step=None):
-            rows.setdefault(n, [])
-            for cols in steps(n) if step is None else [steps(n)[step]]:
-                if not scalar_banks:
-                    turned = psum.tile([P, PACK, P], F32, name="bank_turned", tag="bank_c", bufs=C_BANKS)
-                else:
-                    turned = psum.tile([P, PACK, P], F32, name="bank_turned", tag="scalar_bank")
-                for t in range(PACK):
-                    for k, share in enumerate((e[n], d[n])):
-                        nc.tensor.matmul(
-                            out=turned[:, t, :], lhsT=share[:, t, cols], rhs=identity[:], is_transpose=True, start=(k == 0), stop=(k == 1)
+        def round_wd(tag):
+            grouped = keep.tile([P, 2, PASSES, 2, P, PACK], BF16, name="wd_grouped", tag=tag, align_bytes=64)
+            for pair in range(2):
+                for b in range(PASSES):
+                    for m0 in range(0, P, P // 2):
+                        source = wd_raw[:, b, :, PACK * m0 : PACK * (m0 + P // 2)]
+                        source = source.rearrange("p t (m pg) -> p m t pg", pg=PACK)
+                        nc.scalar.copy(
+                            grouped[:, pair, b, :, m0 : m0 + P // 2, :].rearrange("p side m t -> p m t side"),
+                            source[:, :, :, 2 * pair : 2 * pair + 2],
                         )
-                if offset is not None and cols.start:
-                    row = shared.tile([P, P, PACK], BF16, name="last_rows%d" % n, offset=offset)
-                else:
-                    row = ring.tile([P, P, PACK], BF16, name="h_rows", bufs=2)
-                nc.scalar.activation(row[:], turned[:].rearrange("j t p -> j p t"), ACT.Copy, scale=-1.0)
-                rows[n].append(row)
+            return grouped[:].rearrange("p pair b side m t -> p pair (b side m t)")
 
-        def turn_back(n):
-            b, g0, width = groups[n]
-            pairs = psum.tile([P, len(steps(n)), 2, LIN_N], F32, name="bank_pairs", tag="bank_c", bufs=C_BANKS)
-            for s, row in enumerate(rows[n]):
-                words = row[:].rearrange("j p t -> j (p t)").bitcast(F32).rearrange("j (p u) -> j u p", u=2)
-                for u in range(2):
-                    nc.tensor.transpose(pairs[:, s, u, :], words[:, u, :], identity[:])
-            nc.scalar.copy(
-                h_bf[g0 // HALF][:, b, g0 % HALF : g0 % HALF + width, :].rearrange("p j t -> p (j t)").bitcast(F32).rearrange("p (s j u) -> p s j u", s=len(rows[n]), u=2),
-                pairs[:].rearrange("p s u j -> p s j u"),
-            )
+        def projection(pg, half, tag, bufs):
+            wd_codes, wd_plane = wd_mx[pg // 2]
+            h_codes, h_plane = h_mx[half]
+            bank = psum.tile([P, HALF], F32, name="bank_y", tag=tag, bufs=bufs)
+            for b in range(PASSES):
+                w_cols = slice((2 * b + pg % 2) * P, (2 * b + pg % 2 + 1) * P)
+                j_cols = slice(b * HALF, (b + 1) * HALF)
+                nc.tensor.matmul_mx(
+                    out=bank[:],
+                    lhsT=wd_codes[:, w_cols].bitcast(FP8X4), lhsT_scale=wd_plane[:, w_cols],
+                    rhs=h_codes[:, j_cols].bitcast(FP8X4), rhs_scale=h_plane[:, j_cols],
+                    start=(b == 0), stop=(b == PASSES - 1),
+                )
+            return bank
 
-        def weigh_from_bank(i, tag):
-            weighted[i] = keep.tile([P, HALF], F32, name="weighted%d" % i, tag=tag, align_bytes=64)
-            nc.vector.tensor_tensor(weighted[i][:], projection_bank(i, 0, True)[:], wgo_sb[:, :HALF], ALU.mult)
+        def copied_projection(pg, half):
+            y = keep.tile([P, HALF], F32, name="y%d_%d" % (pg, half), tag="y%d" % pg, align_bytes=64)
+            nc.scalar.copy(y[:], projection(pg, half, "scalar_bank", SCALAR_BANKS)[:])
+            return y
 
-        def place_fused(i):
-            nc.vector.tensor_tensor(window(i, 0), y[i][:], wgo_sb[:, :HALF], ALU.mult)
+        def weighted_by_vector(pg, tag):
+            weighted = keep.tile([P, HALF], F32, name="weighted%d" % pg, tag=tag, align_bytes=64)
+            bank = projection(pg, 0, "slow_bank", SLOW_BANKS)
+            nc.vector.tensor_tensor(weighted[:], bank[:], wgo_sb[:, :HALF], ALU.mult)
+            return weighted
 
-        def d_gpsimd(n):
-            d[n] = ring.tile([P, PACK, groups[n][2]], F32, name="d", bufs=3)
-            nc.gpsimd.tensor_tensor(d[n][:], scaled[n][:], copied[n][:], ALU.subtract)
+        def window(pg, half):
+            return pages[pg][:].indirect(offs2_sb[:, half * HALF // LIST_ROWS : (half + 1) * HALF // LIST_ROWS])
 
-        def product(n, step=None, tag=None):
-            cols = slice(0, groups[n][2]) if step is None else steps(n)[step]
-            part = keep.tile(
-                [P, PACK, cols.stop - cols.start], F32, name="e%d_%d" % (n, cols.start), tag=tag or "e%d" % (n % 3), align_bytes=64
-            )
-            nc.gpsimd.tensor_tensor(part[:], d[n][:, :, cols], z[n][:, :, cols], ALU.mult)
-            e.setdefault(n, []).extend(part[:, :, l0 : l0 + LIN_N] for l0 in range(0, cols.stop - cols.start, LIN_N))
-
-        def h_of(n):
-            b, g0, width = groups[n]
-            for cols, part, bank in zip(steps(n), e[n], banks[n]):
-                interpolate(b, g0 + cols.start, part, bank)
-
-        def slot(n):
-            return "tb%d_%d_0" % groups[n][:2]
-
-        def project(i, tag=None):
-            y[i] = projection(i, 0, tag)
-
-        def weigh(i, tag="weighted"):
-            weighted[i] = ring.tile([P, HALF], F32, name="weighted", tag=tag, bufs=1)
-            nc.gpsimd.tensor_tensor(weighted[i][:], y[i][:], wgo_sb[:, :HALF], ALU.mult)
-
-        def place(i):
-            nc.vector.tensor_copy(window(i, 0), weighted[i][:])
-
-        gate_of(0)
-        gate_of(1)
-        tanh_of(0)
-        tanh_of(1)
-        linear_of(0)
-        linear_of(1)
+        for make in (gate_of, tanh_of):
+            for n in range(2):
+                make(n)
+        for n in range(2):
+            linear_of(n, 0)
         tanh_of(2)
-        linear_of(2)
+        for step in range(2):
+            linear_of(2, step)
         gate_of(2)
-        d_vector(0)
-        product(0)
-        d_vector(1)
-        product(1)
-        tanh_of(3)
-        linear_of(3, 0)
-        gate_of(3)
-        d_vector(2)
-        h_of(0)
-        second_pass(slot(2))
-        product(2, None, slot(2))
-        d_vector(3, 0)
-        h_of(1)
-        linear_of(3, 1)
-        tanh_of(4)
-        linear_of(4, 0)
-        gate_of(4)
-        d_vector(3, 1)
-        product(3)
-        d_vector(4, 0)
-        h_of(2)
-        linear_of(4, 1)
-        tanh_of(5)
-        linear_of(5, 0)
-        gate_of(5)
-        d_vector(4, 1)
-        product(4)
-        d_vector(5, 0)
-        h_of(3)
-        linear_of(5, 1)
-        gate_of(6)
-        gate_of(7)
-        wd_first = round_wd(slot(3))
-        d_vector(5, 1)
-        product(5, None, "e2")
-        h_of(4)
-        linear_of(6)
-        linear_share(6)
-        linear_of(7, 0)
-        linear_share(7, 0)
-        tanh_of(6)
-        scale_of(6, negated)
-        h_of(5)
-        wd_mx[0] = quantise(wd_first[:, : PASS * PACK], PASS, "wd0", "d5")
-        quantise_h(0)
-        wd_mx[1] = quantise(wd_first[:, PASS * PACK :], PASS, "wd1", "e2")
-        tanh_share(6, slot(3))
-        tanh_of(7)
-        linear_of(7, 1)
-        linear_share(7, 1)
-        weigh_from_bank(0, "weighted0")
-        scale_of(7, negated)
-        tanh_share(7)
-        place(0)
-        gate_of(8)
-        project(1)
-        weigh(1)
-        linear_of(8)
-        linear_share(8)
-        tanh_of(8)
-        weigh_from_bank(2, "wb1_codes")
-        place(2)
-        scale_of(8)
-        tanh_share(8, 0)
-        place(1)
-        join_on_tensor(6, 4096, False)
-        join_on_tensor(7, 5120, True)
-        turn_back(6)
-        turn_back(7)
-        join(8)
-        project(3, 2048)
-        quantise_h(1)
-        place_fused(3)
+        for n in range(2):
+            difference(n, 0, range(PACK))
+            product(n, product_tag(n))
 
-        out_rows = out.rearrange("(p i) c -> p i c", i=PACK)
-        for i in range(PACK):
-            last = projection(i, 1)
-            nc.vector.tensor_tensor(window(i, 1), last[:], wgo_sb[:, HALF:], ALU.mult)
-            nc.sync.dma_start(out_rows[:, i, :], pages[i][:])
+        for n in range(3, LAST_OF_HALF + 1):
+            tanh_of(n)
+            linear_of(n, 0)
+            gate_of(n)
+            if n == 3:
+                for t0 in range(0, PACK, 2):
+                    for step in range(2):
+                        difference(2, step, range(t0, t0 + 2))
+                interpolate(0)
+                second_pass_weights(tanh_tag(2, 0))
+                product(2, tanh_tag(2, 0))
+            else:
+                difference(n - 1, 1, range(PACK))
+                product(n - 1, product_tag(n - 1))
+            difference(n, 0, range(PACK))
+            interpolate(n - 2)
+            linear_of(n, 1)
+
+        gate_of(LATE_A)
+        gate_of(LATE_B)
+        wd_grouped = round_wd(tanh_tag(3, 0))
+        difference(LAST_OF_HALF, 1, range(PACK))
+        product(LAST_OF_HALF, product_tag(LAST_OF_HALF))
+        interpolate(LAST_OF_HALF - 1)
+        for step in range(2):
+            linear_of(LATE_A, step)
+        for step in range(2):
+            linear_share(LATE_A, step)
+        linear_of(LATE_B, 0)
+        linear_share(LATE_B, 0)
+        tanh_of(LATE_A)
+        scaled = scaled_tanh(LATE_A, negated_gains)
+        interpolate(LAST_OF_HALF)
+
+        codes = placed.tile([P, PASS], U32, name="wd0_codes", offset=HALF_DIFFERENCE_AT, align_bytes=64)
+        plane = keep.tile([P, PASS], U8, name="wd0_plane", align_bytes=64)
+        nc.vector.quantize_mx(out=codes[:].bitcast(FP8X4), scales=plane[:], in_=wd_grouped[:, 0])
+        wd_mx[0] = codes, plane
+        codes = keep.tile([P, PASSES * HALF], U32, name="h0_codes", align_bytes=64)
+        plane = placed.tile([P, PASSES * HALF], U8, name="h0_plane", offset=HALF_DIFFERENCE_AT + 4 * PASS, align_bytes=64)
+        for b in range(PASSES):
+            cols = slice(b * HALF, (b + 1) * HALF)
+            nc.vector.quantize_mx(
+                out=codes[:, cols].bitcast(FP8X4), scales=plane[:, cols], in_=h_bf[0][:, b].rearrange("p j t -> p (j t)")
+            )
+        h_mx[0] = codes, plane
+        wd_mx[1] = quantise(wd_grouped[:, 1], "wd1", product_tag(LAST_OF_HALF))
+
+        multiply(LATE_A, gate[LATE_A], scaled, tanh_tag(3, 0))
+        tanh_of(LATE_B)
+        linear_of(LATE_B, 1)
+        linear_share(LATE_B, 1)
+        weighted = weighted_by_vector(0, "weighted0")
+        scaled = scaled_tanh(LATE_B, negated_gains)
+        multiply(LATE_B, gate[LATE_B], scaled, product_tag(LATE_B))
+        nc.vector.tensor_copy(window(0, 0), weighted[:])
+
+        gate_of(LAST)
+        y = copied_projection(1, 0)
+        weighted_by_gpsimd = keep.tile([P, HALF], F32, name="weighted1")
+        nc.gpsimd.tensor_tensor(weighted_by_gpsimd[:], y[:], wgo_sb[:, :HALF], ALU.mult)
+        for step in range(2):
+            linear_of(LAST, step)
+        for step in range(2):
+            linear_share(LAST, step)
+        tanh_of(LAST)
+        weighted = weighted_by_vector(2, "wb1_codes")
+        nc.vector.tensor_copy(window(2, 0), weighted[:])
+        scaled = scaled_tanh(LAST, gains)
+        last_share = placed.tile([P, PACK, QUARTER], F32, name="last_share", offset=LAST_SHARE_AT)
+        nc.gpsimd.tensor_tensor(last_share[:], gate[LAST][:], scaled[:], ALU.mult)
+        nc.vector.tensor_copy(window(1, 0), weighted_by_gpsimd[:])
+
+        sum_on_tensor(LATE_A, "slow_bank", SLOW_BANKS)
+        sum_on_tensor(LATE_B, "scalar_bank", SCALAR_BANKS)
+        for n in (LATE_A, LATE_B):
+            turn_back(n)
+        nc.gpsimd.tensor_tensor(
+            woven(h_cols(LAST, 0, QUARTER)), by_pairs(last_share[:]), by_pairs(from_c[LAST][:]), ALU.subtract
+        )
+
+        y = placed.tile([P, GROUP_BYTES // 4], F32, name="y3_0", offset=LAST_Y_AT)[:, :HALF]
+        nc.scalar.copy(y, projection(PACK - 1, 0, "slow_bank", SLOW_BANKS)[:])
+        h_mx[1] = quantise(h_bf[1][:].rearrange("p b j t -> p (b j t)"), "h1", "h1_codes")
+        nc.vector.tensor_tensor(window(PACK - 1, 0), y, wgo_sb[:, :HALF], ALU.mult)
+
+        out_rows = out.rearrange("(p pg) c -> p pg c", pg=PACK)
+        for pg in range(PACK):
+            y = copied_projection(pg, 1)
+            nc.vector.tensor_tensor(window(pg, 1), y[:], wgo_sb[:, HALF:], ALU.mult)
+            nc.sync.dma_start(out_rows[:, pg, :], pages[pg][:])

@@ -31,7 +31,7 @@ QUARTER = S // 4
 STEP = BANK // PACK
 SLOW_BANKS = 5
 SCALAR_BANKS = 8 - SLOW_BANKS
-SCALAR_BLOCKS = 2
+SCALAR_BLOCKS = 10
 
 GROUPS = [(0, 0, STEP), (0, STEP, STEP), (0, QUARTER, QUARTER), (0, 2 * QUARTER, QUARTER)]
 GROUPS = GROUPS + [(1, 0, QUARTER), (1, QUARTER, QUARTER)]
@@ -57,6 +57,19 @@ def tile_list_motet_voice_completion_kernel(
         psum = ctx.enter_context(tc.psum_pool(name="psum", bufs=SCALAR_BANKS))
         placed = ctx.enter_context(tc.tile_pool(name="placed", bufs=1))
 
+        def reorder(raw, name):
+            codes = keep.tile(list(raw.shape), I32, name=name, align_bytes=64)
+            nc.vector.tensor_copy(
+                codes[:].rearrange("p (t q w) -> p t q w", t=PACK, q=BLOCKS),
+                raw.rearrange("p (q t w) -> p t q w", t=PACK, q=BLOCKS),
+            )
+            return codes
+
+        def zero_on_vector(tile):
+            width = tile.shape[1]
+            for cols in (slice(0, width // 2 - 1), slice(width // 2 - 1, width)):
+                nc.vector.memset(tile[:, cols], 0.0)
+
         offs_sb = keep.tile([P, S // LIST_ROWS], U16, name="offs_sb")
         nc.sync.dma_start(offs_sb[:], offs)
         tab_bytes = keep.tile([P, T], U8, name="tab_bytes", align_bytes=64)
@@ -69,33 +82,36 @@ def tile_list_motet_voice_completion_kernel(
             repeated = scales[0].bitcast(I32).unsqueeze(1).broadcast_to([BLOCKS, RUN, H // 4])
             nc.sync.dma_start(raw_scales[:, which, :].bitcast(I32), repeated)
 
-        gain_rows = keep.tile([P, P], F32, name="gain_rows")
-        nc.gpsimd.memset(gain_rows[:], 0.0)
-        gain_src = gain.rearrange("(b q t i) -> b t q i", b=PASSES, t=PACK, i=RUN)
-        for b in range(PASSES):
-            nc.sync.dma_start(
-                gain_rows[b * PACK : (b + 1) * PACK, :].rearrange("t (q i) -> t q i", i=RUN), gain_src[b]
-            )
-
-        tab = keep.tile([P, T], U32, name="tab", align_bytes=64)
-        nc.sync.dma_start(tab[:].bitcast(I32), tab_words[0].rearrange("p t i -> p (t i)").bitcast(I32))
         wa_rows = wa_words[0].bitcast(I32)
         wa_first = keep.tile([P, PASS // 2], I32, name="wa_first", align_bytes=64)
         nc.sync.dma_start(wa_first[:], wa_rows[:, : PASS // 2])
         wb_rows = wb.rearrange("(p row) c -> p row c", row=PACK)
-        wb_pieces = [keep.tile([P, PACK, PASS // 2], F32, name="wb_piece%d" % piece, align_bytes=64) for piece in range(2)]
-        for piece in range(2):
-            nc.sync.dma_start(wb_pieces[piece][:], wb_rows[:, :, piece * PASS // 2 : (piece + 1) * PASS // 2])
+        wb_first = keep.tile([P, PACK, PASS], F32, name="wb_first", align_bytes=64)
+        nc.sync.dma_start(wb_first[:], wb_rows[:, :, :PASS])
+        tab = keep.tile([P, T], U32, name="tab", align_bytes=64)
+        nc.sync.dma_start(tab[:].bitcast(I32), tab_words[0].rearrange("p t i -> p (t i)").bitcast(I32))
+        wc_rows = wc_words[0].rearrange("p e i -> p (e i)").bitcast(I32)
+        wc_first = keep.tile([P, PASS], I32, name="wc_first", align_bytes=64)
+        nc.sync.dma_start(wc_first[:], wc_rows[:, :PASS])
+
+        gain_tile = keep.tile([P, PASSES * P], F32, name="gain_tile")
+        zero_on_vector(gain_tile)
+        gain_rows = gain_tile[:].rearrange("p (b c) -> p b c", b=PASSES)
+        nc.scalar.dma_start(
+            gain_rows[:PACK].rearrange("t b (q i) -> t (b q) i", i=RUN),
+            gain.rearrange("(bq t i) -> t bq i", t=PACK, i=RUN),
+        )
 
         offs2_sb = keep.tile([P, S // LIST_ROWS], U16, name="offs2_sb")
         nc.sync.dma_start(offs2_sb[:], offs2)
         planes = keep.tile([P, 2 * H + S], U8, name="planes", align_bytes=64)
-        identity = keep.tile([P, P], F32, name="identity")
-        make_identity(nc, identity[:])
+        identity_tile = keep.tile([P, P], F32, name="identity")
+        zero_on_vector(identity_tile)
+        identity = identity_tile[:]
+        make_identity(nc, identity, nomemset=True)
 
         pages = [keep.tile([P, T2], F32, name="page%d" % pg) for pg in range(PACK - 1)]
-        for cols in (slice(0, T2 // 2 - 1), slice(T2 // 2 - 1, T2)):
-            nc.vector.memset(pages[0][:, cols].bitcast(I32), 0)
+        zero_on_vector(pages[0])
         for page in pages[1:]:
             nc.gpsimd.memset(page[:], 0.0)
 
@@ -111,21 +127,20 @@ def tile_list_motet_voice_completion_kernel(
         )
         nc.vector.tensor_copy(v_plane.bitcast(I32), v_bytes[:].bitcast(I32))
         for x in range(1, PACK):
-            nc.sync.dma_start(planes[x:P:QUADRANT, :].bitcast(I32), planes[RUN * x : P : QUADRANT, :].bitcast(I32))
+            nc.scalar.dma_start(planes[x:P:QUADRANT, :].bitcast(I32), planes[RUN * x : P : QUADRANT, :].bitcast(I32))
 
+        wa_codes = {0: reorder(wa_first[:], "wa_codes0")}
         pages.append(keep.tile([P, T2], F32, name="page3", tag="raw_scales", align_bytes=64))
-        nc.gpsimd.memset(pages[-1][:], 0.0)
 
-        words_raw = keep.tile([P, H + PASS // 2], I32, name="words_raw", tag="v_bytes", align_bytes=64)
-        wc_rows = wc_words[0].rearrange("p e i -> p (e i)").bitcast(I32)
-        for b in range(PASSES):
-            nc.sync.dma_start(words_raw[:, b * PASS : (b + 1) * PASS], wc_rows[:, b * PASS : (b + 1) * PASS])
-        nc.sync.dma_start(words_raw[:, H:], wa_rows[:, PASS // 2 :])
         widths = [PACK * PASS, PASSES * PACK * N, S]
-        late = keep.tile([P, sum(widths)], F32, name="late", tag="wb_piece0", align_bytes=64)
+        late = keep.tile([P, sum(widths)], F32, name="late", tag="wa_first", align_bytes=64)
         parts = [late[:, sum(widths[:part]) : sum(widths[: part + 1])] for part in range(len(widths))]
         wb_second = parts[0].rearrange("p (row c) -> p row c", row=PACK)
+        words_second = keep.tile([P, PASS + PASS // 2], I32, name="words_second", tag="wb_first", align_bytes=64)
+        wc_second, wa_second = words_second[:, :PASS], words_second[:, PASS:]
         nc.sync.dma_start(wb_second, wb_rows[:, :, PASS:])
+        nc.sync.dma_start(wc_second, wc_rows[:, PASS:])
+        nc.sync.dma_start(wa_second, wa_rows[:, PASS // 2 :])
         wd_rows = wd.rearrange("(b q t i) n -> b t q i n", b=PASSES, t=PACK, i=RUN)
         wd_raw = parts[1].rearrange("p (b t n) -> p b t n", b=PASSES, t=PACK)
         for b in range(PASSES):
@@ -135,14 +150,6 @@ def tile_list_motet_voice_completion_kernel(
         nc.sync.dma_start(wgo_sb, wgo)
 
         h_bf = [keep.tile([P, PASSES, HALF, PACK], BF16, name="h_bf%d" % half, align_bytes=64) for half in range(2)]
-
-        def reorder(raw, name):
-            codes = keep.tile(list(raw.shape), I32, name=name, align_bytes=64)
-            nc.vector.tensor_copy(
-                codes[:].rearrange("p (t q w) -> p t q w", t=PACK, q=BLOCKS),
-                raw.rearrange("p (q t w) -> p t q w", t=PACK, q=BLOCKS),
-            )
-            return codes
 
         def gather_words(j0, width, tag):
             words = keep.tile([P, width], U32, name="v_words%d" % j0, tag=tag, align_bytes=64)
@@ -156,28 +163,26 @@ def tile_list_motet_voice_completion_kernel(
             nc.vector.quantize_mx(out=codes[:].bitcast(FP8X4), scales=plane[:], in_=grouped)
             return codes, plane
 
-        v_first = gather_words(0, QUARTER, "v_first")
-        wa_codes = {0: reorder(wa_first[:], "wa_codes0")}
-        v_rest = gather_words(QUARTER, S - QUARTER, "tab_bytes")
-
         wb_grouped = keep.tile([P, PACK, BLOCKS, RUN, PACK], BF16, name="wb_grouped0", align_bytes=64)
-        piece_blocks = BLOCKS // 2
-        shares = [(nc.scalar.copy, "p t q row i", 0, q, piece_blocks // 2) for q in (0, piece_blocks // 2)]
-        shares.append((nc.scalar.copy, "p t q row i", 1, 0, SCALAR_BLOCKS))
-        shares.append((nc.vector.tensor_copy, "p t q i row", 1, SCALAR_BLOCKS, piece_blocks - SCALAR_BLOCKS))
-        for copy, order, piece, q, count in shares:
-            blocks = wb_pieces[piece][:].rearrange("p row (q t i) -> " + order, t=PACK, i=RUN)
-            q0 = piece * piece_blocks + q
-            copy(wb_grouped[:, :, q0 : q0 + count].rearrange("p t q i row -> " + order), blocks[:, :, q : q + count])
+        shares = [(nc.scalar.copy, "p t q row i", 0, SCALAR_BLOCKS), (nc.vector.tensor_copy, "p t q i row", SCALAR_BLOCKS, BLOCKS)]
+        for copy, order, q0, q1 in shares:
+            blocks = wb_first[:].rearrange("p row (q t i) -> " + order, t=PACK, i=RUN)
+            copy(wb_grouped[:, :, q0:q1].rearrange("p t q i row -> " + order), blocks[:, :, q0:q1])
+        nc.vector.memset(pages[-1][:].bitcast(I32), 0)
         wb_mx = {0: quantise(wb_grouped[:].rearrange("p t q i row -> p (t q i row)"), "wb0", "wb0_codes")}
-
-        gain_bank = psum.tile([P, P], F32, name="gain_bank", tag="scalar_bank")
-        nc.tensor.transpose(gain_bank[:], gain_rows[:], identity[:])
+        v_first = gather_words(0, QUARTER, "v_first")
+        wc_codes = {0: reorder(wc_first[:], "wc_codes0")}
+        v_rest = gather_words(QUARTER, S - QUARTER, "wc_first")
         gains = keep.tile([P, PASSES * PACK], F32, name="gains")
-        nc.scalar.copy(gains[:], gain_bank[:, : PASSES * PACK])
         negated_gains = keep.tile([P, PASSES * PACK], F32, name="negated_gains")
-        nc.gpsimd.tensor_scalar(negated_gains[:], gains[:], -1.0, 0.0, ALU.mult, ALU.add)
-        wc_codes = {0: reorder(words_raw[:, :PASS], "wc_codes0")}
+
+        def fetch_gains():
+            gain_bank = psum.tile([P, PASSES, P], F32, name="gain_bank", tag="scalar_bank")
+            for b in range(PASSES):
+                nc.tensor.transpose(gain_bank[:, b, :], gain_rows[:, b, :], identity)
+            for tile, sign in ((gains, 1.0), (negated_gains, -1.0)):
+                by_pass = tile[:].rearrange("p (b t) -> p b t", b=PASSES)
+                nc.scalar.activation(by_pass, gain_bank[:, :, :PACK], ACT.Copy, scale=sign)
 
         tanh, gate, c_banks, from_c, from_gate, h_rows = {}, {}, {}, {}, {}, {}
         wd_mx, h_mx = {}, {}
@@ -195,13 +200,18 @@ def tile_list_motet_voice_completion_kernel(
         def tanh_tag(n, t0):
             return "tanh%d_%d" % (n - (LAST - LAST_OF_HALF) if n > LATE_A else n, t0)
 
+        def gate_bank(shape, name, slow):
+            if slow:
+                return psum.tile(shape, F32, name=name, tag="slow_bank", bufs=SLOW_BANKS)
+            return psum.tile(shape, F32, name=name, tag="scalar_bank")
+
         def tanh_of(n):
             b, j0, width = GROUPS[n]
             codes, plane = wb_mx[b]
             per_bank = BANK // width
             tanh[n] = []
             for t0 in range(0, PACK, per_bank):
-                bank = psum.tile([P, per_bank, width], F32, name="bank_b", tag="scalar_bank")
+                bank = gate_bank([P, per_bank, width], "bank_b", n < 2 or (n == 2 and t0 == 0))
                 for t in range(t0, t0 + per_bank):
                     cols = slice(t * P, (t + 1) * P)
                     first_stage(bank[:, t - t0, :], codes[:, cols].bitcast(FP8X4), plane[:, cols], j0, width)
@@ -214,7 +224,7 @@ def tile_list_motet_voice_completion_kernel(
             per_bank = BANK // width
             gate[n] = ring.tile([P, PACK, width], F32, name="gate", bufs=4)
             for t0 in range(0, PACK, per_bank):
-                bank = psum.tile([P, per_bank, width], F32, name="bank_a", tag="scalar_bank")
+                bank = gate_bank([P, per_bank, width], "bank_a", n < 2)
                 for t in range(t0, t0 + per_bank):
                     codes = wa_codes[b][:].bitcast(U8)[:, 2 * t * P : 2 * (t + 1) * P].bitcast(FP4X4)
                     c0 = b * PASS + t * P
@@ -295,7 +305,7 @@ def tile_list_motet_voice_completion_kernel(
                 for t in range(PACK):
                     for term, share in enumerate((from_gate[n], from_c[n])):
                         nc.tensor.matmul(
-                            out=turned[:, t, :], lhsT=share[:, t, cols], rhs=identity[:],
+                            out=turned[:, t, :], lhsT=share[:, t, cols], rhs=identity,
                             is_transpose=True, start=(term == 0), stop=(term == 1),
                         )
                 if cols.start == 0:
@@ -310,7 +320,7 @@ def tile_list_motet_voice_completion_kernel(
             for step, rows in enumerate(h_rows[n]):
                 row_words = rows[:].rearrange("j p t -> j (p t)").bitcast(F32).rearrange("j (p u) -> j u p", u=2)
                 for u in range(2):
-                    nc.tensor.transpose(pairs[:, step, u, :], row_words[:, u, :], identity[:])
+                    nc.tensor.transpose(pairs[:, step, u, :], row_words[:, u, :], identity)
             h_words = h_cols(n, 0, QUARTER).rearrange("p j t -> p (j t)").bitcast(F32)
             nc.scalar.copy(
                 h_words.rearrange("p (step j u) -> p step j u", step=2, u=2),
@@ -322,17 +332,16 @@ def tile_list_motet_voice_completion_kernel(
             codes = keep.tile([P, PASS], U32, name="wb1_codes", align_bytes=64)
             plane = keep.tile([P, PASS], U8, name="wb1_plane", align_bytes=64)
             blocks = wb_second.rearrange("p row (q t i) -> p t q i row", t=PACK, i=RUN)
-            for t0 in range(0, PACK, 2):
-                nc.vector.tensor_copy(grouped[:, t0 : t0 + 2], blocks[:, t0 : t0 + 2])
+            nc.vector.tensor_copy(grouped[:, :2], blocks[:, :2])
+            wc_codes[1] = reorder(wc_second, "wc_codes1")
+            nc.vector.tensor_copy(grouped[:, 2:], blocks[:, 2:])
+            wa_codes[1] = reorder(wa_second, "wa_codes1")
             for t0 in range(0, PACK, 2):
                 cols = slice(t0 * P, (t0 + 2) * P)
                 nc.vector.quantize_mx(
                     out=codes[:, cols].bitcast(FP8X4), scales=plane[:, cols],
                     in_=grouped[:, t0 : t0 + 2].rearrange("p t q i row -> p (t q i row)"),
                 )
-                if t0 == 0:
-                    wc_codes[1] = reorder(words_raw[:, PASS:H], "wc_codes1")
-                    wa_codes[1] = reorder(words_raw[:, H:], "wa_codes1")
             wb_mx[1] = codes, plane
 
         def round_wd(tag):
@@ -377,33 +386,27 @@ def tile_list_motet_voice_completion_kernel(
         def window(pg, half):
             return pages[pg][:].indirect(offs2_sb[:, half * HALF // LIST_ROWS : (half + 1) * HALF // LIST_ROWS])
 
-        for make in (gate_of, tanh_of):
-            for n in range(2):
-                make(n)
+        fetch_gains()
         for n in range(2):
-            linear_of(n, 0)
+            gate_of(n)
+            tanh_of(n)
         tanh_of(2)
-        for step in range(2):
-            linear_of(2, step)
         gate_of(2)
+        for n, step in ((0, 0), (1, 0), (2, 0), (2, 1)):
+            linear_of(n, step)
+        second_pass_weights(product_tag(0))
         for n in range(2):
             difference(n, 0, range(PACK))
             product(n, product_tag(n))
+        difference(2, 0, range(PACK))
+        interpolate(0)
 
         for n in range(3, LAST_OF_HALF + 1):
             tanh_of(n)
             linear_of(n, 0)
             gate_of(n)
-            if n == 3:
-                for t0 in range(0, PACK, 2):
-                    for step in range(2):
-                        difference(2, step, range(t0, t0 + 2))
-                interpolate(0)
-                second_pass_weights(tanh_tag(2, 0))
-                product(2, tanh_tag(2, 0))
-            else:
-                difference(n - 1, 1, range(PACK))
-                product(n - 1, product_tag(n - 1))
+            difference(n - 1, 1, range(PACK))
+            product(n - 1, product_tag(n - 1))
             difference(n, 0, range(PACK))
             interpolate(n - 2)
             linear_of(n, 1)

@@ -290,12 +290,15 @@ def tile_list_motet_voice_completion_kernel(
                 from_c_tile(n)[:, :, cols], gate[n][:, :, cols], 1.0, c_banks[n, step][:], ALU.subtract, ALU.mult
             )
 
-        def scaled_tanh(n, factors):
+        def scaled_tanh(n, factors, on_gpsimd=0):
             b = GROUPS[n][0]
             scaled = ring.tile([P, PACK, QUARTER], F32, name="scaled")
             for t in range(PACK):
                 factor = factors[:, b * PACK + t : b * PACK + t + 1]
-                nc.scalar.activation(scaled[:, t, :], tanh[n][t], ACT.Copy, scale=factor)
+                if t < on_gpsimd:
+                    nc.gpsimd.tensor_scalar(scaled[:, t, :], tanh[n][t], factor, 0.0, ALU.mult, ALU.add)
+                else:
+                    nc.scalar.activation(scaled[:, t, :], tanh[n][t], ACT.Copy, scale=factor)
             return scaled
 
         def sum_on_tensor(n, tag, bufs):
@@ -309,16 +312,16 @@ def tile_list_motet_voice_completion_kernel(
                             is_transpose=True, start=(term == 0), stop=(term == 1),
                         )
                 if cols.start == 0:
-                    rows = ring.tile([P, P, PACK], BF16, name="h_rows")
+                    rows = ring.tile([P, 2, P, 2], BF16, name="h_rows")
                 else:
-                    rows = placed.tile([P, P, PACK], BF16, name="last_rows%d" % n, offset=LAST_ROWS_AT[n])
-                nc.scalar.activation(rows[:], turned[:].rearrange("j t p -> j p t"), ACT.Copy, scale=-1.0)
+                    rows = placed.tile([P, 2, P, 2], BF16, name="last_rows%d" % n, offset=LAST_ROWS_AT[n])
+                nc.scalar.activation(rows[:], turned[:].rearrange("j (u e) p -> j u p e", e=2), ACT.Copy, scale=-1.0)
                 h_rows[n].append(rows)
 
         def turn_back(n):
             pairs = psum.tile([P, 2, 2, STEP], F32, name="bank_pairs", tag="slow_bank", bufs=SLOW_BANKS)
             for step, rows in enumerate(h_rows[n]):
-                row_words = rows[:].rearrange("j p t -> j (p t)").bitcast(F32).rearrange("j (p u) -> j u p", u=2)
+                row_words = rows[:].rearrange("j u p e -> j u (p e)").bitcast(F32)
                 for u in range(2):
                     nc.tensor.transpose(pairs[:, step, u, :], row_words[:, u, :], identity)
             h_words = h_cols(n, 0, QUARTER).rearrange("p j t -> p (j t)").bitcast(F32)
@@ -413,6 +416,7 @@ def tile_list_motet_voice_completion_kernel(
 
         gate_of(LATE_A)
         gate_of(LATE_B)
+        tanh_of(LATE_A)
         wd_grouped = round_wd(tanh_tag(3, 0))
         difference(LAST_OF_HALF, 1, range(PACK))
         product(LAST_OF_HALF, product_tag(LAST_OF_HALF))
@@ -423,8 +427,7 @@ def tile_list_motet_voice_completion_kernel(
             linear_share(LATE_A, step)
         linear_of(LATE_B, 0)
         linear_share(LATE_B, 0)
-        tanh_of(LATE_A)
-        scaled = scaled_tanh(LATE_A, negated_gains)
+        scaled = scaled_tanh(LATE_A, negated_gains, 2)
         interpolate(LAST_OF_HALF)
 
         codes = placed.tile([P, PASS], U32, name="wd0_codes", offset=HALF_DIFFERENCE_AT, align_bytes=64)

@@ -185,7 +185,7 @@ def tile_list_motet_voice_completion_kernel(
                 nc.scalar.activation(by_pass, gain_bank[:, :, :PACK], ACT.Copy, scale=sign)
 
         tanh, gate, c_banks, from_c, from_gate, h_rows = {}, {}, {}, {}, {}, {}
-        wd_mx, h_mx = {}, {}
+        wd_mx, h_mx, wide_banks = {}, {}, {}
 
         def steps(n):
             return [slice(j, j + STEP) for j in range(0, GROUPS[n][2], STEP)]
@@ -239,6 +239,23 @@ def tile_list_motet_voice_completion_kernel(
                 c0 = b * PASS + t * P
                 first_stage(bank[:, t, :], codes, w_scales[:, 1, c0 : c0 + P], j0 + step * STEP, STEP)
             c_banks[n, step] = bank
+
+        def wide_linear_of(n, pair):
+            b, j0, width = GROUPS[n]
+            bank = psum.tile([P, 2, width], F32, name="bank_wide", tag="slow_bank", bufs=SLOW_BANKS)
+            for t in range(2 * pair, 2 * pair + 2):
+                codes = wc_codes[b][:, t * P : (t + 1) * P].bitcast(FP8X4)
+                c0 = b * PASS + t * P
+                first_stage(bank[:, t % 2, :], codes, w_scales[:, 1, c0 : c0 + P], j0, width)
+            wide_banks[n, pair] = bank
+
+        def wide_difference(n, pair):
+            b = GROUPS[n][0]
+            for t in range(2 * pair, 2 * pair + 2):
+                nc.vector.scalar_tensor_tensor(
+                    from_c_tile(n)[:, t, :], tanh[n][t], gains[:, b * PACK + t : b * PACK + t + 1],
+                    wide_banks[n, pair][:, t % 2, :], ALU.mult, ALU.subtract,
+                )
 
         def from_c_tile(n):
             if n not in from_c and n == LAST_OF_HALF:
@@ -406,20 +423,29 @@ def tile_list_motet_voice_completion_kernel(
 
         for n in range(3, LAST_OF_HALF + 1):
             tanh_of(n)
-            linear_of(n, 0)
+            wide_linear_of(n, 0)
             gate_of(n)
-            difference(n - 1, 1, range(PACK))
+            if n == 3:
+                difference(n - 1, 1, range(PACK))
+            else:
+                wide_difference(n - 1, 1)
             product(n - 1, product_tag(n - 1))
-            difference(n, 0, range(PACK))
+            wide_difference(n, 0)
+            if n == LAST_OF_HALF:
+                for step in range(2):
+                    linear_of(n - 2, step)
             interpolate(n - 2)
-            linear_of(n, 1)
+            wide_linear_of(n, 1)
 
         gate_of(LATE_A)
         gate_of(LATE_B)
         tanh_of(LATE_A)
         wd_grouped = round_wd(tanh_tag(3, 0))
-        difference(LAST_OF_HALF, 1, range(PACK))
+        wide_difference(LAST_OF_HALF, 1)
         product(LAST_OF_HALF, product_tag(LAST_OF_HALF))
+        for n in (LAST_OF_HALF - 1, LAST_OF_HALF):
+            for step in range(2):
+                linear_of(n, step)
         interpolate(LAST_OF_HALF - 1)
         for step in range(2):
             linear_of(LATE_A, step)

@@ -1,7 +1,6 @@
 from contextlib import ExitStack
 
 import concourse.mybir as mybir
-from concourse.masks import make_identity
 
 K, H, N, T, S, T2 = 512, 1024, 512, 2048, 1024, 2048
 FLOPS = 2 * S * (3 * K * H + H * N)
@@ -29,14 +28,15 @@ BANK = 512
 HALF = S // 2
 QUARTER = S // 4
 STEP = BANK // PACK
+STEPS = [slice(j, j + STEP) for j in range(0, QUARTER, STEP)]
+PAIRS = range(2)
 SLOW_BANKS = 5
 SCALAR_BANKS = 8 - SLOW_BANKS
-SCALAR_BLOCKS = 10
 
-GROUPS = [(0, 0, STEP), (0, STEP, STEP), (0, QUARTER, QUARTER), (0, 2 * QUARTER, QUARTER)]
-GROUPS = GROUPS + [(1, 0, QUARTER), (1, QUARTER, QUARTER)]
+GROUPS = [(0, 0), (0, QUARTER), (0, 2 * QUARTER), (1, 0), (1, QUARTER)]
+FIRST_OF_PASS_1 = 3
 LAST_OF_HALF = len(GROUPS) - 1
-GROUPS = GROUPS + [(0, 3 * QUARTER, QUARTER), (1, 2 * QUARTER, QUARTER), (1, 3 * QUARTER, QUARTER)]
+GROUPS = GROUPS + [(0, 3 * QUARTER), (1, 2 * QUARTER), (1, 3 * QUARTER)]
 LATE_A, LATE_B, LAST = range(LAST_OF_HALF + 1, len(GROUPS))
 
 GROUP_BYTES = PACK * QUARTER * 4
@@ -45,6 +45,9 @@ LAST_SHARE_AT = 0
 LAST_ROWS_AT = {LATE_A: GROUP_BYTES, LATE_B: GROUP_BYTES + ROW_BYTES}
 LAST_Y_AT = GROUP_BYTES // 2
 HALF_DIFFERENCE_AT = GROUP_BYTES + 2 * ROW_BYTES
+WA_SECOND_AT = HALF_DIFFERENCE_AT + GROUP_BYTES
+LAST_PAGE_AT = WA_SECOND_AT + 2 * PASS
+WA_FIRST_AT = LAST_PAGE_AT - PASS
 
 
 def tile_list_motet_voice_completion_kernel(
@@ -57,13 +60,13 @@ def tile_list_motet_voice_completion_kernel(
         psum = ctx.enter_context(tc.psum_pool(name="psum", bufs=SCALAR_BANKS))
         placed = ctx.enter_context(tc.tile_pool(name="placed", bufs=1))
 
-        def reorder(raw, name):
-            codes = keep.tile(list(raw.shape), I32, name=name, align_bytes=64)
-            nc.vector.tensor_copy(
-                codes[:].rearrange("p (t q w) -> p t q w", t=PACK, q=BLOCKS),
-                raw.rearrange("p (q t w) -> p t q w", t=PACK, q=BLOCKS),
-            )
-            return codes
+        def kept(shape, dtype, name, tag=None):
+            return keep.tile(shape, dtype, name=name, tag=tag or name, align_bytes=64)
+
+        def load(shape, dtype, name, source):
+            tile = kept(shape, dtype, name)
+            nc.sync.dma_start(tile[:], source)
+            return tile
 
         def zero_on_vector(tile):
             width = tile.shape[1]
@@ -72,52 +75,64 @@ def tile_list_motet_voice_completion_kernel(
 
         offs_sb = keep.tile([P, S // LIST_ROWS], U16, name="offs_sb")
         nc.sync.dma_start(offs_sb[:], offs)
-        tab_bytes = keep.tile([P, T], U8, name="tab_bytes", align_bytes=64)
+        tab_bytes = kept([P, T], U8, "tab_bytes")
         nc.sync.dma_start(
             tab_bytes[:].bitcast(I32),
             tab_scales[0].bitcast(I32).unsqueeze(1).broadcast_to([BLOCKS, RUN, T // 4]),
         )
-        raw_scales = keep.tile([P, 2, H], U8, name="raw_scales", align_bytes=64)
+        raw_scales = kept([P, 2, H], U8, "raw_scales")
         for which, scales in enumerate((wa_scales, wc_scales)):
             repeated = scales[0].bitcast(I32).unsqueeze(1).broadcast_to([BLOCKS, RUN, H // 4])
             nc.sync.dma_start(raw_scales[:, which, :].bitcast(I32), repeated)
-
         wa_rows = wa_words[0].bitcast(I32)
-        wa_first = keep.tile([P, PASS // 2], I32, name="wa_first", align_bytes=64)
-        nc.sync.dma_start(wa_first[:], wa_rows[:, : PASS // 2])
         wb_rows = wb.rearrange("(p row) c -> p row c", row=PACK)
-        wb_first = keep.tile([P, PACK, PASS], F32, name="wb_first", align_bytes=64)
-        nc.sync.dma_start(wb_first[:], wb_rows[:, :, :PASS])
-        tab = keep.tile([P, T], U32, name="tab", align_bytes=64)
-        nc.sync.dma_start(tab[:].bitcast(I32), tab_words[0].rearrange("p t i -> p (t i)").bitcast(I32))
         wc_rows = wc_words[0].rearrange("p e i -> p (e i)").bitcast(I32)
-        wc_first = keep.tile([P, PASS], I32, name="wc_first", align_bytes=64)
-        nc.sync.dma_start(wc_first[:], wc_rows[:, :PASS])
+        wa_raw = {0: placed.tile([P, PASS // 2], I32, name="wa_raw0", offset=WA_FIRST_AT, align_bytes=64)}
+        nc.sync.dma_start(wa_raw[0][:], wa_rows[:, : PASS // 2])
+        tab = kept([P, T], U32, "tab")
+        nc.sync.dma_start(tab[:].bitcast(I32), tab_words[0].rearrange("p t i -> p (t i)").bitcast(I32))
+        wb_raw = {0: load([P, PACK, PASS], F32, "wb_raw0", wb_rows[:, :, :PASS])}
 
-        gain_tile = keep.tile([P, PASSES * P], F32, name="gain_tile")
-        zero_on_vector(gain_tile)
-        gain_rows = gain_tile[:].rearrange("p (b c) -> p b c", b=PASSES)
-        nc.scalar.dma_start(
-            gain_rows[:PACK].rearrange("t b (q i) -> t (b q) i", i=RUN),
-            gain.rearrange("(bq t i) -> t bq i", t=PACK, i=RUN),
+        block_gains = kept([P, PASSES, PACK * RUN], F32, "block_gains")
+        gain_blocks = gain.rearrange("(b q c) -> b q c", b=PASSES, q=BLOCKS)
+        for b in range(PASSES):
+            repeated = gain_blocks[b].unsqueeze(1).broadcast_to([BLOCKS, RUN, PACK * RUN])
+            nc.scalar.dma_start(block_gains[:, b, :], repeated)
+
+        zeros = kept([P, P], F32, "zeros", tag="page1")
+        nc.gpsimd.memset(zeros[:], 0.0)
+        identity_tile = kept([P, P], F32, "identity")
+        identity = identity_tile[:]
+        nc.gpsimd.affine_select(
+            out=identity, in_=zeros[:], compare_op=ALU.not_equal, fill=1.0, base=0,
+            pattern=[[-1, P]], channel_multiplier=1,
         )
 
-        offs2_sb = keep.tile([P, S // LIST_ROWS], U16, name="offs2_sb")
-        nc.sync.dma_start(offs2_sb[:], offs2)
-        planes = keep.tile([P, 2 * H + S], U8, name="planes", align_bytes=64)
-        identity_tile = keep.tile([P, P], F32, name="identity")
-        zero_on_vector(identity_tile)
-        identity = identity_tile[:]
-        make_identity(nc, identity, nomemset=True)
+        own = kept([P, RUN], F32, "own")
+        nc.vector.tensor_reduce(own[:], identity.rearrange("p (q i) -> p i q", i=RUN), mybir.AxisListType.X, ALU.add)
+        masked = kept([P, PASSES * PACK, RUN], F32, "masked")
+        nc.gpsimd.tensor_tensor(
+            masked[:], block_gains[:].rearrange("p b (t i) -> p (b t) i", i=RUN),
+            own[:].unsqueeze(1).broadcast_to([P, PASSES * PACK, RUN]), ALU.mult,
+        )
 
-        pages = [keep.tile([P, T2], F32, name="page%d" % pg) for pg in range(PACK - 1)]
+        pages = [kept([P, T2], F32, "page%d" % pg) for pg in range(PACK - 1)]
         zero_on_vector(pages[0])
         for page in pages[1:]:
             nc.gpsimd.memset(page[:], 0.0)
 
+        def reorder(raw, name):
+            codes = kept(list(raw.shape), I32, name)
+            nc.vector.tensor_copy(
+                codes[:].rearrange("p (t q w) -> p t q w", t=PACK, q=BLOCKS),
+                raw[:].rearrange("p (q t w) -> p t q w", t=PACK, q=BLOCKS),
+            )
+            return codes
+
+        planes = kept([P, 2 * H + S], U8, "planes")
         w_scales = planes[:, : 2 * H].rearrange("p (s c) -> p s c", s=2)
         v_plane = planes[:, 2 * H :]
-        v_bytes = keep.tile([P, S], U8, name="v_bytes", align_bytes=64)
+        v_bytes = kept([P, S], U8, "v_bytes")
         nc.vector.tensor_copy(v_bytes[:], tab_bytes[:].indirect(offs_sb[:]))
         nc.vector.tensor_copy(
             planes[:, : 2 * H].bitcast(I32).rearrange("p (g t q w) -> p g t q w", t=PACK, q=BLOCKS, w=RUN // 4),
@@ -129,199 +144,210 @@ def tile_list_motet_voice_completion_kernel(
         for x in range(1, PACK):
             nc.scalar.dma_start(planes[x:P:QUADRANT, :].bitcast(I32), planes[RUN * x : P : QUADRANT, :].bitcast(I32))
 
-        wa_codes = {0: reorder(wa_first[:], "wa_codes0")}
-        pages.append(keep.tile([P, T2], F32, name="page3", tag="raw_scales", align_bytes=64))
+        wa_codes = {0: reorder(wa_raw[0], "wa_codes0")}
+        pages.append(placed.tile([P, T2], F32, name="page3", offset=LAST_PAGE_AT, align_bytes=64))
+        nc.gpsimd.memset(pages[-1][:], 0.0)
 
-        widths = [PACK * PASS, PASSES * PACK * N, S]
-        late = keep.tile([P, sum(widths)], F32, name="late", tag="wa_first", align_bytes=64)
-        parts = [late[:, sum(widths[:part]) : sum(widths[: part + 1])] for part in range(len(widths))]
-        wb_second = parts[0].rearrange("p (row c) -> p row c", row=PACK)
-        words_second = keep.tile([P, PASS + PASS // 2], I32, name="words_second", tag="wb_first", align_bytes=64)
-        wc_second, wa_second = words_second[:, :PASS], words_second[:, PASS:]
-        nc.sync.dma_start(wb_second, wb_rows[:, :, PASS:])
-        nc.sync.dma_start(wc_second, wc_rows[:, PASS:])
-        nc.sync.dma_start(wa_second, wa_rows[:, PASS // 2 :])
+        wa_raw[1] = placed.tile([P, PASS // 2], I32, name="wa_raw1", offset=WA_SECOND_AT, align_bytes=64)
+        nc.sync.dma_start(wa_raw[1][:], wa_rows[:, PASS // 2 :])
+        wc_raw = [load([P, PASS], I32, "wc_raw%d" % b, wc_rows[:, b * PASS : (b + 1) * PASS]) for b in range(PASSES)]
+        wb_raw[1] = load([P, PACK, PASS], F32, "wb_raw1", wb_rows[:, :, PASS:])
+        offs2_sb = keep.tile([P, S // LIST_ROWS], U16, name="offs2_sb")
+        nc.sync.dma_start(offs2_sb[:], offs2)
         wd_rows = wd.rearrange("(b q t i) n -> b t q i n", b=PASSES, t=PACK, i=RUN)
-        wd_raw = parts[1].rearrange("p (b t n) -> p b t n", b=PASSES, t=PACK)
+        wd_raw = [kept([P, PACK, N], F32, "wd_raw%d" % b) for b in range(PASSES)]
         for b in range(PASSES):
             for t in range(PACK):
-                nc.sync.dma_start(wd_raw[:, b, t, :], wd_rows[b, t])
-        wgo_sb = parts[2]
-        nc.sync.dma_start(wgo_sb, wgo)
+                nc.sync.dma_start(wd_raw[b][:, t, :], wd_rows[b, t])
+        wgo_sb = load([P, S], F32, "wgo_sb", wgo)
 
-        h_bf = [keep.tile([P, PASSES, HALF, PACK], BF16, name="h_bf%d" % half, align_bytes=64) for half in range(2)]
 
-        def gather_words(j0, width, tag):
-            words = keep.tile([P, width], U32, name="v_words%d" % j0, tag=tag, align_bytes=64)
-            nc.vector.tensor_copy(words[:], tab[:].indirect(offs_sb[:, j0 // LIST_ROWS : (j0 + width) // LIST_ROWS]))
-            return words
+        gains = kept([P, PASSES * PACK], F32, "gains", tag="v_bytes")
+        nc.vector.tensor_reduce(gains[:], masked[:], mybir.AxisListType.X, ALU.add)
+
+        v_words = []
+        for half in range(2):
+            words = kept([P, HALF], U32, "v_words%d" % half)
+            entries = offs_sb[:, half * HALF // LIST_ROWS : (half + 1) * HALF // LIST_ROWS]
+            nc.vector.tensor_copy(words[:], tab[:].indirect(entries))
+            v_words.append(words)
+
+        wb_mx, wc_codes = {}, {}
+
+        def round_wb(b, tag):
+            grouped = kept([P, PACK, BLOCKS, RUN, PACK], BF16, "wb_grouped%d" % b, tag=tag)
+            blocks = wb_raw[b][:].rearrange("p row (q t i) -> p t q i row", t=PACK, i=RUN)
+            for pair in PAIRS:
+                nc.vector.tensor_copy(grouped[:, 2 * pair : 2 * pair + 2], blocks[:, 2 * pair : 2 * pair + 2])
+            wb_mx[b] = kept([P, PASS], U32, "wb_codes%d" % b), kept([P, PASS], U8, "wb_plane%d" % b)
+            return grouped
+
+        def quantise_wb(b, grouped, pair):
+            codes, plane = wb_mx[b]
+            cols = slice(2 * pair * P, (2 * pair + 2) * P)
+            nc.vector.quantize_mx(
+                out=codes[:, cols].bitcast(FP8X4), scales=plane[:, cols],
+                in_=grouped[:, 2 * pair : 2 * pair + 2].rearrange("p t q i row -> p (t q i row)"),
+            )
+
+        grouped = round_wb(0, "wb_grouped0")
+        wa_codes[1] = reorder(wa_raw[1], "wa_codes1")
+        for pair in PAIRS:
+            quantise_wb(0, grouped, pair)
+            wc_codes[pair] = reorder(wc_raw[pair], "wc_codes%d" % pair)
+
+        h_bf = [
+            kept([P, PASSES, HALF, PACK], BF16, "h_bf0"),
+            kept([P, PASSES, HALF, PACK], BF16, "h_bf1", tag="wb_raw0"),
+        ]
 
         def quantise(grouped, name, tag):
             width = grouped.shape[1] // PACK
-            codes = keep.tile([P, width], U32, name=name + "_codes", tag=tag, align_bytes=64)
-            plane = keep.tile([P, width], U8, name=name + "_plane", align_bytes=64)
+            codes = kept([P, width], U32, name + "_codes", tag=tag)
+            plane = kept([P, width], U8, name + "_plane")
             nc.vector.quantize_mx(out=codes[:].bitcast(FP8X4), scales=plane[:], in_=grouped)
             return codes, plane
-
-        wb_grouped = keep.tile([P, PACK, BLOCKS, RUN, PACK], BF16, name="wb_grouped0", align_bytes=64)
-        shares = [(nc.scalar.copy, "p t q row i", 0, SCALAR_BLOCKS), (nc.vector.tensor_copy, "p t q i row", SCALAR_BLOCKS, BLOCKS)]
-        for copy, order, q0, q1 in shares:
-            blocks = wb_first[:].rearrange("p row (q t i) -> " + order, t=PACK, i=RUN)
-            copy(wb_grouped[:, :, q0:q1].rearrange("p t q i row -> " + order), blocks[:, :, q0:q1])
-        nc.vector.memset(pages[-1][:].bitcast(I32), 0)
-        wb_mx = {0: quantise(wb_grouped[:].rearrange("p t q i row -> p (t q i row)"), "wb0", "wb0_codes")}
-        v_first = gather_words(0, QUARTER, "v_first")
-        wc_codes = {0: reorder(wc_first[:], "wc_codes0")}
-        v_rest = gather_words(QUARTER, S - QUARTER, "wc_first")
-        gains = keep.tile([P, PASSES * PACK], F32, name="gains")
-        negated_gains = keep.tile([P, PASSES * PACK], F32, name="negated_gains")
-
-        def fetch_gains():
-            gain_bank = psum.tile([P, PASSES, P], F32, name="gain_bank", tag="scalar_bank")
-            for b in range(PASSES):
-                nc.tensor.transpose(gain_bank[:, b, :], gain_rows[:, b, :], identity)
-            for tile, sign in ((gains, 1.0), (negated_gains, -1.0)):
-                by_pass = tile[:].rearrange("p (b t) -> p b t", b=PASSES)
-                nc.scalar.activation(by_pass, gain_bank[:, :, :PACK], ACT.Copy, scale=sign)
 
         tanh, gate, c_banks, from_c, from_gate, h_rows = {}, {}, {}, {}, {}, {}
         wd_mx, h_mx, wide_banks = {}, {}, {}
 
-        def steps(n):
-            return [slice(j, j + STEP) for j in range(0, GROUPS[n][2], STEP)]
+        def slices(pair):
+            return range(2 * pair, 2 * pair + 2)
+
+        def new_bank(shape, name, slow):
+            if slow:
+                return psum.tile(shape, F32, name=name, tag="slow_bank", bufs=SLOW_BANKS)
+            return psum.tile(shape, F32, name=name, tag="scalar_bank")
 
         def first_stage(bank, codes, plane, j0, width):
-            words = v_first[:, j0 : j0 + width] if j0 < QUARTER else v_rest[:, j0 - QUARTER : j0 - QUARTER + width]
+            words = v_words[j0 // HALF][:, j0 % HALF : j0 % HALF + width]
             nc.tensor.matmul_mx(
                 out=bank, lhsT=codes, lhsT_scale=plane,
                 rhs=words.bitcast(FP8X4), rhs_scale=v_plane[:, j0 : j0 + width], start=True, stop=True,
             )
 
-        def tanh_tag(n, t0):
-            return "tanh%d_%d" % (n - (LAST - LAST_OF_HALF) if n > LATE_A else n, t0)
+        def tanh_tag(n, pair):
+            return "tanh%d_%d" % (n - (LAST - LAST_OF_HALF) if n > LATE_A else n, pair)
 
-        def gate_bank(shape, name, slow):
-            if slow:
-                return psum.tile(shape, F32, name=name, tag="slow_bank", bufs=SLOW_BANKS)
-            return psum.tile(shape, F32, name=name, tag="scalar_bank")
-
-        def tanh_of(n):
-            b, j0, width = GROUPS[n]
+        def tanh_of(n, pair, slow=False):
+            b, j0 = GROUPS[n]
             codes, plane = wb_mx[b]
-            per_bank = BANK // width
-            tanh[n] = []
-            for t0 in range(0, PACK, per_bank):
-                bank = gate_bank([P, per_bank, width], "bank_b", n < 2 or (n == 2 and t0 == 0))
-                for t in range(t0, t0 + per_bank):
-                    cols = slice(t * P, (t + 1) * P)
-                    first_stage(bank[:, t - t0, :], codes[:, cols].bitcast(FP8X4), plane[:, cols], j0, width)
-                part = keep.tile([P, per_bank, width], F32, name="tanh", tag=tanh_tag(n, t0), align_bytes=64)
-                nc.scalar.activation(part[:], bank[:], ACT.Tanh)
-                tanh[n].extend(part[:, t, :] for t in range(per_bank))
+            bank = new_bank([P, 2, QUARTER], "bank_b", slow)
+            for t in slices(pair):
+                cols = slice(t * P, (t + 1) * P)
+                first_stage(bank[:, t % 2, :], codes[:, cols].bitcast(FP8X4), plane[:, cols], j0, QUARTER)
+            part = kept([P, 2, QUARTER], F32, "tanh", tag=tanh_tag(n, pair))
+            nc.scalar.activation(part[:], bank[:], ACT.Tanh, scale=-1.0 if n in (LATE_A, LATE_B) else 1.0)
+            for t in slices(pair):
+                tanh[n, t] = part[:, t % 2, :]
 
-        def gate_of(n):
-            b, j0, width = GROUPS[n]
-            per_bank = BANK // width
-            gate[n] = ring.tile([P, PACK, width], F32, name="gate", bufs=4)
-            for t0 in range(0, PACK, per_bank):
-                bank = gate_bank([P, per_bank, width], "bank_a", n < 2)
-                for t in range(t0, t0 + per_bank):
-                    codes = wa_codes[b][:].bitcast(U8)[:, 2 * t * P : 2 * (t + 1) * P].bitcast(FP4X4)
-                    c0 = b * PASS + t * P
-                    first_stage(bank[:, t - t0, :], codes, w_scales[:, 0, c0 : c0 + P], j0, width)
-                nc.scalar.activation(gate[n][:, t0 : t0 + per_bank, :], bank[:], ACT.Sigmoid)
+        def gate_of(n, pair, slow=False):
+            b, j0 = GROUPS[n]
+            if pair == 0:
+                gate[n] = ring.tile([P, PACK, QUARTER], F32, name="gate", bufs=4)
+            bank = new_bank([P, 2, QUARTER], "bank_a", slow)
+            for t in slices(pair):
+                codes = wa_codes[b][:].bitcast(U8)[:, 2 * t * P : 2 * (t + 1) * P].bitcast(FP4X4)
+                c0 = b * PASS + t * P
+                first_stage(bank[:, t % 2, :], codes, w_scales[:, 0, c0 : c0 + P], j0, QUARTER)
+            nc.scalar.activation(gate[n][:, 2 * pair : 2 * pair + 2, :], bank[:], ACT.Sigmoid)
+
+        def both(function, n):
+            for pair in PAIRS:
+                function(n, pair)
+
+        def linear_slice(target, n, t, j, width):
+            b, j0 = GROUPS[n]
+            c0 = b * PASS + t * P
+            codes = wc_codes[b][:, t * P : (t + 1) * P].bitcast(FP8X4)
+            first_stage(target, codes, w_scales[:, 1, c0 : c0 + P], j0 + j, width)
 
         def linear_of(n, step):
-            b, j0, width = GROUPS[n]
-            bank = psum.tile([P, PACK, STEP], F32, name="bank_c", tag="slow_bank", bufs=SLOW_BANKS)
+            bank = new_bank([P, PACK, STEP], "bank_c", True)
             for t in range(PACK):
-                codes = wc_codes[b][:, t * P : (t + 1) * P].bitcast(FP8X4)
-                c0 = b * PASS + t * P
-                first_stage(bank[:, t, :], codes, w_scales[:, 1, c0 : c0 + P], j0 + step * STEP, STEP)
+                linear_slice(bank[:, t, :], n, t, step * STEP, STEP)
             c_banks[n, step] = bank
 
         def wide_linear_of(n, pair):
-            b, j0, width = GROUPS[n]
-            bank = psum.tile([P, 2, width], F32, name="bank_wide", tag="slow_bank", bufs=SLOW_BANKS)
-            for t in range(2 * pair, 2 * pair + 2):
-                codes = wc_codes[b][:, t * P : (t + 1) * P].bitcast(FP8X4)
-                c0 = b * PASS + t * P
-                first_stage(bank[:, t % 2, :], codes, w_scales[:, 1, c0 : c0 + P], j0, width)
+            bank = new_bank([P, 2, QUARTER], "bank_wide", True)
+            for t in slices(pair):
+                linear_slice(bank[:, t % 2, :], n, t, 0, QUARTER)
             wide_banks[n, pair] = bank
 
-        def wide_difference(n, pair):
-            b = GROUPS[n][0]
-            for t in range(2 * pair, 2 * pair + 2):
-                nc.vector.scalar_tensor_tensor(
-                    from_c_tile(n)[:, t, :], tanh[n][t], gains[:, b * PACK + t : b * PACK + t + 1],
-                    wide_banks[n, pair][:, t % 2, :], ALU.mult, ALU.subtract,
-                )
+        def gain_of(n, t):
+            column = GROUPS[n][0] * PACK + t
+            return gains[:, column : column + 1]
+
+        def product_tag(n):
+            return "product%d" % (n % 3)
 
         def from_c_tile(n):
+            if n not in from_c and n == 0:
+                from_c[n] = kept([P, PACK, QUARTER], F32, "from_c_first", tag=product_tag(1))
             if n not in from_c and n == LAST_OF_HALF:
                 from_c[n] = placed.tile(
                     [P, PACK, QUARTER], F32, name="from_c_half", offset=HALF_DIFFERENCE_AT, align_bytes=64
                 )
             if n not in from_c:
-                from_c[n] = ring.tile([P, PACK, GROUPS[n][2]], F32, name="from_c", bufs=3)
+                from_c[n] = ring.tile([P, PACK, QUARTER], F32, name="from_c", bufs=3)
             return from_c[n]
 
         def h_cols(n, j, width):
-            b, j0 = GROUPS[n][:2]
+            b, j0 = GROUPS[n]
             return h_bf[j0 // HALF][:, b, j0 % HALF + j : j0 % HALF + j + width, :]
 
-        def by_pairs(tile):
+        def by_twos(tile):
             return tile.rearrange("p t (c two) -> p c t two", two=2)
 
         def woven(h_part):
             return h_part.rearrange("p (c two) t -> p c t two", two=2)
 
-        def difference(n, step, slices):
-            b, cols = GROUPS[n][0], steps(n)[step]
-            for t in slices:
+        def difference(n, pair):
+            for step, cols in enumerate(STEPS):
+                for t in slices(pair):
+                    nc.vector.scalar_tensor_tensor(
+                        from_c_tile(n)[:, t, cols], tanh[n, t][:, cols], gain_of(n, t),
+                        c_banks[n, step][:, t, :], ALU.mult, ALU.subtract,
+                    )
+
+        def wide_difference(n, pair):
+            for t in slices(pair):
                 nc.vector.scalar_tensor_tensor(
-                    from_c_tile(n)[:, t, cols], tanh[n][t][:, cols], gains[:, b * PACK + t : b * PACK + t + 1],
-                    c_banks[n, step][:, t, :], ALU.mult, ALU.subtract,
+                    from_c_tile(n)[:, t, :], tanh[n, t], gain_of(n, t),
+                    wide_banks[n, pair][:, t % 2, :], ALU.mult, ALU.subtract,
                 )
 
-        def multiply(n, left, right, tag):
-            from_gate[n] = keep.tile([P, PACK, GROUPS[n][2]], F32, name="from_gate", tag=tag, align_bytes=64)
-            nc.gpsimd.tensor_tensor(from_gate[n][:], left[:], right[:], ALU.mult)
+        def multiply(n, left, right, tag, parts=(slice(0, PACK),)):
+            from_gate[n] = kept([P, PACK, QUARTER], F32, "from_gate", tag=tag)
+            for part in parts:
+                nc.gpsimd.tensor_tensor(from_gate[n][:, part], left[:, part], right[:, part], ALU.mult)
 
-        def product(n, tag):
-            multiply(n, from_c[n], gate[n], tag)
-
-        def product_tag(n):
-            return "product%d" % (n % 3)
+        def product(n):
+            multiply(n, from_c[n], gate[n], product_tag(n))
 
         def interpolate(n):
-            for step, cols in enumerate(steps(n)):
+            for step, cols in enumerate(STEPS):
                 nc.vector.tensor_tensor(
                     woven(h_cols(n, cols.start, STEP)),
-                    by_pairs(from_gate[n][:, :, cols]), by_pairs(c_banks[n, step][:]), ALU.add,
+                    by_twos(from_gate[n][:, :, cols]), by_twos(c_banks[n, step][:]), ALU.add,
                 )
 
         def linear_share(n, step):
-            cols = steps(n)[step]
+            cols = STEPS[step]
             nc.vector.scalar_tensor_tensor(
                 from_c_tile(n)[:, :, cols], gate[n][:, :, cols], 1.0, c_banks[n, step][:], ALU.subtract, ALU.mult
             )
 
-        def scaled_tanh(n, factors, on_gpsimd=0):
-            b = GROUPS[n][0]
+        def scaled_tanh(n):
             scaled = ring.tile([P, PACK, QUARTER], F32, name="scaled")
             for t in range(PACK):
-                factor = factors[:, b * PACK + t : b * PACK + t + 1]
-                if t < on_gpsimd:
-                    nc.gpsimd.tensor_scalar(scaled[:, t, :], tanh[n][t], factor, 0.0, ALU.mult, ALU.add)
-                else:
-                    nc.scalar.activation(scaled[:, t, :], tanh[n][t], ACT.Copy, scale=factor)
+                nc.scalar.activation(scaled[:, t, :], tanh[n, t], ACT.Copy, scale=gain_of(n, t))
             return scaled
 
-        def sum_on_tensor(n, tag, bufs):
+        def sum_on_tensor(n, slow):
             h_rows[n] = []
-            for cols in steps(n):
-                turned = psum.tile([P, PACK, P], F32, name="bank_turned", tag=tag, bufs=bufs)
+            for cols in STEPS:
+                turned = new_bank([P, PACK, P], "bank_turned", slow)
                 for t in range(PACK):
                     for term, share in enumerate((from_gate[n], from_c[n])):
                         nc.tensor.matmul(
@@ -336,51 +362,42 @@ def tile_list_motet_voice_completion_kernel(
                 h_rows[n].append(rows)
 
         def turn_back(n):
-            pairs = psum.tile([P, 2, 2, STEP], F32, name="bank_pairs", tag="slow_bank", bufs=SLOW_BANKS)
+            words = new_bank([P, 2, 2, STEP], "bank_words", True)
             for step, rows in enumerate(h_rows[n]):
                 row_words = rows[:].rearrange("j u p e -> j u (p e)").bitcast(F32)
                 for u in range(2):
-                    nc.tensor.transpose(pairs[:, step, u, :], row_words[:, u, :], identity)
+                    nc.tensor.transpose(words[:, step, u, :], row_words[:, u, :], identity)
             h_words = h_cols(n, 0, QUARTER).rearrange("p j t -> p (j t)").bitcast(F32)
             nc.scalar.copy(
                 h_words.rearrange("p (step j u) -> p step j u", step=2, u=2),
-                pairs[:].rearrange("p step u j -> p step j u"),
+                words[:].rearrange("p step u j -> p step j u"),
             )
 
-        def second_pass_weights(tag):
-            grouped = keep.tile([P, PACK, BLOCKS, RUN, PACK], BF16, name="wb_grouped1", tag=tag, align_bytes=64)
-            codes = keep.tile([P, PASS], U32, name="wb1_codes", align_bytes=64)
-            plane = keep.tile([P, PASS], U8, name="wb1_plane", align_bytes=64)
-            blocks = wb_second.rearrange("p row (q t i) -> p t q i row", t=PACK, i=RUN)
-            nc.vector.tensor_copy(grouped[:, :2], blocks[:, :2])
-            wc_codes[1] = reorder(wc_second, "wc_codes1")
-            nc.vector.tensor_copy(grouped[:, 2:], blocks[:, 2:])
-            wa_codes[1] = reorder(wa_second, "wa_codes1")
-            for t0 in range(0, PACK, 2):
-                cols = slice(t0 * P, (t0 + 2) * P)
+        def round_wd(b, tag):
+            grouped = kept([P, 2, 2, P, PACK], BF16, "wd_grouped%d" % b, tag=tag)
+            for pair in PAIRS:
+                for m0 in range(0, P, P // 2):
+                    source = wd_raw[b][:, :, PACK * m0 : PACK * (m0 + P // 2)]
+                    source = source.rearrange("p t (m pg) -> p m t pg", pg=PACK)
+                    nc.scalar.copy(
+                        grouped[:, pair, :, m0 : m0 + P // 2, :].rearrange("p side m t -> p m t side"),
+                        source[:, :, :, 2 * pair : 2 * pair + 2],
+                    )
+            return grouped[:].rearrange("p pair side m t -> p pair (side m t)")
+
+        def quantise_wd(pair, codes):
+            plane = kept([P, PASS], U8, "wd_plane%d" % pair)
+            for b in range(PASSES):
+                cols = slice(2 * b * P, 2 * (b + 1) * P)
                 nc.vector.quantize_mx(
-                    out=codes[:, cols].bitcast(FP8X4), scales=plane[:, cols],
-                    in_=grouped[:, t0 : t0 + 2].rearrange("p t q i row -> p (t q i row)"),
+                    out=codes[:, cols].bitcast(FP8X4), scales=plane[:, cols], in_=wd_grouped[b][:, pair]
                 )
-            wb_mx[1] = codes, plane
+            wd_mx[pair] = codes, plane
 
-        def round_wd(tag):
-            grouped = keep.tile([P, 2, PASSES, 2, P, PACK], BF16, name="wd_grouped", tag=tag, align_bytes=64)
-            for pair in range(2):
-                for b in range(PASSES):
-                    for m0 in range(0, P, P // 2):
-                        source = wd_raw[:, b, :, PACK * m0 : PACK * (m0 + P // 2)]
-                        source = source.rearrange("p t (m pg) -> p m t pg", pg=PACK)
-                        nc.scalar.copy(
-                            grouped[:, pair, b, :, m0 : m0 + P // 2, :].rearrange("p side m t -> p m t side"),
-                            source[:, :, :, 2 * pair : 2 * pair + 2],
-                        )
-            return grouped[:].rearrange("p pair b side m t -> p pair (b side m t)")
-
-        def projection(pg, half, tag, bufs):
+        def projection(pg, half, slow):
             wd_codes, wd_plane = wd_mx[pg // 2]
             h_codes, h_plane = h_mx[half]
-            bank = psum.tile([P, HALF], F32, name="bank_y", tag=tag, bufs=bufs)
+            bank = new_bank([P, HALF], "bank_y", slow)
             for b in range(PASSES):
                 w_cols = slice((2 * b + pg % 2) * P, (2 * b + pg % 2 + 1) * P)
                 j_cols = slice(b * HALF, (b + 1) * HALF)
@@ -392,75 +409,78 @@ def tile_list_motet_voice_completion_kernel(
                 )
             return bank
 
+        y_tags = ["wc_raw0", "wc_raw1", "tab_bytes", "raw_scales"]
+
         def copied_projection(pg, half):
-            y = keep.tile([P, HALF], F32, name="y%d_%d" % (pg, half), tag="y%d" % pg, align_bytes=64)
-            nc.scalar.copy(y[:], projection(pg, half, "scalar_bank", SCALAR_BANKS)[:])
+            y = kept([P, HALF], F32, "y%d_%d" % (pg, half), tag=y_tags[pg])
+            nc.scalar.copy(y[:], projection(pg, half, False)[:])
             return y
 
         def weighted_by_vector(pg, tag):
-            weighted = keep.tile([P, HALF], F32, name="weighted%d" % pg, tag=tag, align_bytes=64)
-            bank = projection(pg, 0, "slow_bank", SLOW_BANKS)
+            weighted = kept([P, HALF], F32, "weighted%d" % pg, tag=tag)
+            bank = projection(pg, 0, True)
             nc.vector.tensor_tensor(weighted[:], bank[:], wgo_sb[:, :HALF], ALU.mult)
             return weighted
 
         def window(pg, half):
             return pages[pg][:].indirect(offs2_sb[:, half * HALF // LIST_ROWS : (half + 1) * HALF // LIST_ROWS])
 
-        fetch_gains()
-        for n in range(2):
-            gate_of(n)
-            tanh_of(n)
-        tanh_of(2)
-        gate_of(2)
-        for n, step in ((0, 0), (1, 0), (2, 0), (2, 1)):
-            linear_of(n, step)
-        second_pass_weights(product_tag(0))
-        for n in range(2):
-            difference(n, 0, range(PACK))
-            product(n, product_tag(n))
-        difference(2, 0, range(PACK))
-        interpolate(0)
+        both(gate_of, 0)
+        gate_of(1, 0)
+        gate_of(1, 1, slow=True)
+        for pair in PAIRS:
+            tanh_of(0, pair, slow=True)
+        both(linear_of, 0)
+        both(tanh_of, 1)
+        both(linear_of, 1)
+        both(difference, 0)
+        multiply(0, from_c[0], gate[0], product_tag(0), [slice(2 * pair, 2 * pair + 2) for pair in PAIRS])
+        both(difference, 1)
+        both(tanh_of, 2)
+        wide_linear_of(2, 0)
+        both(gate_of, 2)
+        wide_difference(2, 0)
 
-        for n in range(3, LAST_OF_HALF + 1):
-            tanh_of(n)
+        grouped = round_wb(1, product_tag(1))
+        for pair in PAIRS:
+            quantise_wb(1, grouped, pair)
+        product(1)
+        interpolate(0)
+        wide_linear_of(2, 1)
+
+        for n in range(FIRST_OF_PASS_1, LAST_OF_HALF + 1):
+            if n == FIRST_OF_PASS_1:
+                both(gate_of, n)
+            both(tanh_of, n)
             wide_linear_of(n, 0)
-            gate_of(n)
-            if n == 3:
-                difference(n - 1, 1, range(PACK))
-            else:
-                wide_difference(n - 1, 1)
-            product(n - 1, product_tag(n - 1))
+            if n != FIRST_OF_PASS_1:
+                both(gate_of, n)
+            wide_difference(n - 1, 1)
+            product(n - 1)
             wide_difference(n, 0)
             if n == LAST_OF_HALF:
-                for step in range(2):
-                    linear_of(n - 2, step)
+                both(linear_of, n - 2)
             interpolate(n - 2)
             wide_linear_of(n, 1)
 
-        gate_of(LATE_A)
-        gate_of(LATE_B)
-        tanh_of(LATE_A)
-        wd_grouped = round_wd(tanh_tag(3, 0))
+        both(gate_of, LATE_A)
+        both(gate_of, LATE_B)
+        both(tanh_of, LATE_A)
+        wd_grouped = [round_wd(b, tanh_tag(2, b)) for b in range(PASSES)]
         wide_difference(LAST_OF_HALF, 1)
-        product(LAST_OF_HALF, product_tag(LAST_OF_HALF))
+        product(LAST_OF_HALF)
         for n in (LAST_OF_HALF - 1, LAST_OF_HALF):
-            for step in range(2):
-                linear_of(n, step)
+            both(linear_of, n)
         interpolate(LAST_OF_HALF - 1)
-        for step in range(2):
-            linear_of(LATE_A, step)
-        for step in range(2):
-            linear_share(LATE_A, step)
+        both(linear_of, LATE_A)
+        both(linear_share, LATE_A)
         linear_of(LATE_B, 0)
         linear_share(LATE_B, 0)
-        scaled = scaled_tanh(LATE_A, negated_gains, 2)
+        scaled = scaled_tanh(LATE_A)
         interpolate(LAST_OF_HALF)
 
-        codes = placed.tile([P, PASS], U32, name="wd0_codes", offset=HALF_DIFFERENCE_AT, align_bytes=64)
-        plane = keep.tile([P, PASS], U8, name="wd0_plane", align_bytes=64)
-        nc.vector.quantize_mx(out=codes[:].bitcast(FP8X4), scales=plane[:], in_=wd_grouped[:, 0])
-        wd_mx[0] = codes, plane
-        codes = keep.tile([P, PASSES * HALF], U32, name="h0_codes", align_bytes=64)
+        quantise_wd(0, placed.tile([P, PASS], U32, name="wd0_codes", offset=HALF_DIFFERENCE_AT, align_bytes=64))
+        codes = kept([P, PASSES * HALF], U32, "h0_codes")
         plane = placed.tile([P, PASSES * HALF], U8, name="h0_plane", offset=HALF_DIFFERENCE_AT + 4 * PASS, align_bytes=64)
         for b in range(PASSES):
             cols = slice(b * HALF, (b + 1) * HALF)
@@ -468,44 +488,42 @@ def tile_list_motet_voice_completion_kernel(
                 out=codes[:, cols].bitcast(FP8X4), scales=plane[:, cols], in_=h_bf[0][:, b].rearrange("p j t -> p (j t)")
             )
         h_mx[0] = codes, plane
-        wd_mx[1] = quantise(wd_grouped[:, 1], "wd1", product_tag(LAST_OF_HALF))
+        quantise_wd(1, kept([P, PASS], U32, "wd1_codes", tag=product_tag(LAST_OF_HALF)))
 
-        multiply(LATE_A, gate[LATE_A], scaled, tanh_tag(3, 0))
-        tanh_of(LATE_B)
+        multiply(LATE_A, gate[LATE_A], scaled, tanh_tag(2, 1))
+        both(tanh_of, LATE_B)
         linear_of(LATE_B, 1)
         linear_share(LATE_B, 1)
-        weighted = weighted_by_vector(0, "weighted0")
-        scaled = scaled_tanh(LATE_B, negated_gains)
+        weighted = weighted_by_vector(0, "wb_grouped0")
+        scaled = scaled_tanh(LATE_B)
         multiply(LATE_B, gate[LATE_B], scaled, product_tag(LATE_B))
         nc.vector.tensor_copy(window(0, 0), weighted[:])
 
-        gate_of(LAST)
+        both(gate_of, LAST)
         y = copied_projection(1, 0)
-        weighted_by_gpsimd = keep.tile([P, HALF], F32, name="weighted1")
+        weighted_by_gpsimd = kept([P, HALF], F32, "weighted1")
         nc.gpsimd.tensor_tensor(weighted_by_gpsimd[:], y[:], wgo_sb[:, :HALF], ALU.mult)
-        for step in range(2):
-            linear_of(LAST, step)
-        for step in range(2):
-            linear_share(LAST, step)
-        tanh_of(LAST)
-        weighted = weighted_by_vector(2, "wb1_codes")
+        both(linear_of, LAST)
+        both(linear_share, LAST)
+        both(tanh_of, LAST)
+        weighted = weighted_by_vector(2, "wb_codes1")
         nc.vector.tensor_copy(window(2, 0), weighted[:])
-        scaled = scaled_tanh(LAST, gains)
+        scaled = scaled_tanh(LAST)
         last_share = placed.tile([P, PACK, QUARTER], F32, name="last_share", offset=LAST_SHARE_AT)
         nc.gpsimd.tensor_tensor(last_share[:], gate[LAST][:], scaled[:], ALU.mult)
         nc.vector.tensor_copy(window(1, 0), weighted_by_gpsimd[:])
 
-        sum_on_tensor(LATE_A, "slow_bank", SLOW_BANKS)
-        sum_on_tensor(LATE_B, "scalar_bank", SCALAR_BANKS)
+        sum_on_tensor(LATE_A, True)
+        sum_on_tensor(LATE_B, False)
         for n in (LATE_A, LATE_B):
             turn_back(n)
         nc.gpsimd.tensor_tensor(
-            woven(h_cols(LAST, 0, QUARTER)), by_pairs(last_share[:]), by_pairs(from_c[LAST][:]), ALU.subtract
+            woven(h_cols(LAST, 0, QUARTER)), by_twos(last_share[:]), by_twos(from_c[LAST][:]), ALU.subtract
         )
 
         y = placed.tile([P, GROUP_BYTES // 4], F32, name="y3_0", offset=LAST_Y_AT)[:, :HALF]
-        nc.scalar.copy(y, projection(PACK - 1, 0, "slow_bank", SLOW_BANKS)[:])
-        h_mx[1] = quantise(h_bf[1][:].rearrange("p b j t -> p (b j t)"), "h1", "h1_codes")
+        nc.scalar.copy(y, projection(PACK - 1, 0, True)[:])
+        h_mx[1] = quantise(h_bf[1][:].rearrange("p b j t -> p (b j t)"), "h1", "tab")
         nc.vector.tensor_tensor(window(PACK - 1, 0), y, wgo_sb[:, :HALF], ALU.mult)
 
         out_rows = out.rearrange("(p pg) c -> p pg c", pg=PACK)

@@ -99,22 +99,8 @@ def tile_list_motet_voice_completion_kernel(
             repeated = gain_blocks[b].unsqueeze(1).broadcast_to([BLOCKS, RUN, PACK * RUN])
             nc.scalar.dma_start(block_gains[:, b, :], repeated)
 
-        zeros = kept([P, P], F32, "zeros", tag="page1")
-        nc.gpsimd.memset(zeros[:], 0.0)
-        identity_tile = kept([P, P], F32, "identity")
-        identity = identity_tile[:]
-        nc.gpsimd.affine_select(
-            out=identity, in_=zeros[:], compare_op=ALU.not_equal, fill=1.0, base=0,
-            pattern=[[-1, P]], channel_multiplier=1,
-        )
-
-        own = kept([P, RUN], F32, "own")
-        nc.vector.tensor_reduce(own[:], identity.rearrange("p (q i) -> p i q", i=RUN), mybir.AxisListType.X, ALU.add)
-        masked = kept([P, PASSES * PACK, RUN], F32, "masked")
-        nc.gpsimd.tensor_tensor(
-            masked[:], block_gains[:].rearrange("p b (t i) -> p (b t) i", i=RUN),
-            own[:].unsqueeze(1).broadcast_to([P, PASSES * PACK, RUN]), ALU.mult,
-        )
+        distance = kept([P, RUN], I32, "distance")
+        nc.gpsimd.iota(distance[:], pattern=[[-1, RUN]], base=0, channel_multiplier=1)
 
         pages = [kept([P, T2], F32, "page%d" % pg) for pg in range(PACK - 1)]
         zero_on_vector(pages[0])
@@ -162,9 +148,6 @@ def tile_list_motet_voice_completion_kernel(
         wgo_sb = load([P, S], F32, "wgo_sb", wgo)
 
 
-        gains = kept([P, PASSES * PACK], F32, "gains", tag="v_bytes")
-        nc.vector.tensor_reduce(gains[:], masked[:], mybir.AxisListType.X, ALU.add)
-
         v_words = []
         for half in range(2):
             words = kept([P, HALF], U32, "v_words%d" % half)
@@ -195,6 +178,27 @@ def tile_list_motet_voice_completion_kernel(
         for pair in PAIRS:
             quantise_wb(0, grouped, pair)
             wc_codes[pair] = reorder(wc_raw[pair], "wc_codes%d" % pair)
+
+        remainder = kept([P, RUN], I32, "remainder", tag="wb_raw0")
+        nc.vector.tensor_single_scalar(remainder[:], distance[:], RUN - 1, ALU.bitwise_and)
+        own = kept([P, RUN], F32, "own")
+        nc.vector.tensor_single_scalar(own[:], remainder[:], 0.0, ALU.is_equal)
+        masked = kept([P, PASSES * PACK, RUN], F32, "masked")
+        nc.vector.tensor_tensor(
+            masked[:], block_gains[:].rearrange("p b (t i) -> p (b t) i", i=RUN),
+            own[:].unsqueeze(1).broadcast_to([P, PASSES * PACK, RUN]), ALU.mult,
+        )
+        gains = kept([P, PASSES * PACK], F32, "gains")
+        nc.vector.tensor_reduce(gains[:], masked[:], mybir.AxisListType.X, ALU.add)
+
+        zeros = kept([P, P], F32, "zeros", tag="wc_raw1")
+        nc.gpsimd.memset(zeros[:], 0.0)
+        identity_tile = kept([P, P], F32, "identity")
+        identity = identity_tile[:]
+        nc.gpsimd.affine_select(
+            out=identity, in_=zeros[:], compare_op=ALU.not_equal, fill=1.0, base=0,
+            pattern=[[-1, P]], channel_multiplier=1,
+        )
 
         h_bf = [
             kept([P, PASSES, HALF, PACK], BF16, "h_bf0"),

@@ -45,9 +45,6 @@ LAST_SHARE_AT = 0
 LAST_ROWS_AT = {LATE_A: GROUP_BYTES, LATE_B: GROUP_BYTES + ROW_BYTES}
 LAST_Y_AT = GROUP_BYTES // 2
 HALF_DIFFERENCE_AT = GROUP_BYTES + 2 * ROW_BYTES
-WA_SECOND_AT = HALF_DIFFERENCE_AT + GROUP_BYTES
-LAST_PAGE_AT = WA_SECOND_AT + 2 * PASS
-WA_FIRST_AT = LAST_PAGE_AT - PASS
 
 
 def tile_list_motet_voice_completion_kernel(
@@ -87,8 +84,7 @@ def tile_list_motet_voice_completion_kernel(
         wa_rows = wa_words[0].bitcast(I32)
         wb_rows = wb.rearrange("(p row) c -> p row c", row=PACK)
         wc_rows = wc_words[0].rearrange("p e i -> p (e i)").bitcast(I32)
-        wa_raw = {0: placed.tile([P, PASS // 2], I32, name="wa_raw0", offset=WA_FIRST_AT, align_bytes=64)}
-        nc.sync.dma_start(wa_raw[0][:], wa_rows[:, : PASS // 2])
+        wa_raw = {0: load([P, PASS // 2], I32, "wa_raw0", wa_rows[:, : PASS // 2])}
         tab = kept([P, T], U32, "tab")
         nc.sync.dma_start(tab[:].bitcast(I32), tab_words[0].rearrange("p t i -> p (t i)").bitcast(I32))
         wb_raw = {0: load([P, PACK, PASS], F32, "wb_raw0", wb_rows[:, :, :PASS])}
@@ -128,15 +124,15 @@ def tile_list_motet_voice_completion_kernel(
         )
         nc.vector.tensor_copy(v_plane.bitcast(I32), v_bytes[:].bitcast(I32))
         for x in range(1, PACK):
-            nc.scalar.dma_start(planes[x:P:QUADRANT, :].bitcast(I32), planes[RUN * x : P : QUADRANT, :].bitcast(I32))
+            nc.sync.dma_start(planes[x:P:QUADRANT, :].bitcast(I32), planes[RUN * x : P : QUADRANT, :].bitcast(I32))
 
         wa_codes = {0: reorder(wa_raw[0], "wa_codes0")}
-        pages.append(placed.tile([P, T2], F32, name="page3", offset=LAST_PAGE_AT, align_bytes=64))
+        pages.append(kept([P, T2], F32, "page3", tag="wa_raw0"))
         nc.gpsimd.memset(pages[-1][:], 0.0)
 
-        wa_raw[1] = placed.tile([P, PASS // 2], I32, name="wa_raw1", offset=WA_SECOND_AT, align_bytes=64)
-        nc.sync.dma_start(wa_raw[1][:], wa_rows[:, PASS // 2 :])
-        wc_raw = [load([P, PASS], I32, "wc_raw%d" % b, wc_rows[:, b * PASS : (b + 1) * PASS]) for b in range(PASSES)]
+        wc_raw = {0: load([P, PASS], I32, "wc_raw0", wc_rows[:, :PASS])}
+        wa_raw[1] = load([P, PASS // 2], I32, "wa_raw1", wa_rows[:, PASS // 2 :])
+        wc_raw[1] = load([P, PASS], I32, "wc_raw1", wc_rows[:, PASS:])
         wb_raw[1] = load([P, PACK, PASS], F32, "wb_raw1", wb_rows[:, :, PASS:])
         offs2_sb = keep.tile([P, S // LIST_ROWS], U16, name="offs2_sb")
         nc.sync.dma_start(offs2_sb[:], offs2)
@@ -162,22 +158,23 @@ def tile_list_motet_voice_completion_kernel(
             blocks = wb_raw[b][:].rearrange("p row (q t i) -> p t q i row", t=PACK, i=RUN)
             for pair in PAIRS:
                 nc.vector.tensor_copy(grouped[:, 2 * pair : 2 * pair + 2], blocks[:, 2 * pair : 2 * pair + 2])
-            wb_mx[b] = kept([P, PASS], U32, "wb_codes%d" % b), kept([P, PASS], U8, "wb_plane%d" % b)
             return grouped
 
-        def quantise_wb(b, grouped, pair):
-            codes, plane = wb_mx[b]
-            cols = slice(2 * pair * P, (2 * pair + 2) * P)
+        def quantise_wb(b, grouped, pair, tag=None):
+            codes = kept([P, 2 * P], U32, "wb_codes%d_%d" % (b, pair), tag=tag)
+            plane = kept([P, 2 * P], U8, "wb_plane%d_%d" % (b, pair))
             nc.vector.quantize_mx(
-                out=codes[:, cols].bitcast(FP8X4), scales=plane[:, cols],
+                out=codes[:].bitcast(FP8X4), scales=plane[:],
                 in_=grouped[:, 2 * pair : 2 * pair + 2].rearrange("p t q i row -> p (t q i row)"),
             )
+            wb_mx[b, pair] = codes, plane
 
         grouped = round_wb(0, "wb_grouped0")
+        quantise_wb(0, grouped, 0)
+        wc_codes[0] = reorder(wc_raw[0], "wc_codes0")
+        quantise_wb(0, grouped, 1, tag="wc_raw0")
         wa_codes[1] = reorder(wa_raw[1], "wa_codes1")
-        for pair in PAIRS:
-            quantise_wb(0, grouped, pair)
-            wc_codes[pair] = reorder(wc_raw[pair], "wc_codes%d" % pair)
+        wc_codes[1] = reorder(wc_raw[1], "wc_codes1")
 
         remainder = kept([P, RUN], I32, "remainder", tag="wb_raw0")
         nc.vector.tensor_single_scalar(remainder[:], distance[:], RUN - 1, ALU.bitwise_and)
@@ -235,10 +232,10 @@ def tile_list_motet_voice_completion_kernel(
 
         def tanh_of(n, pair, slow=False):
             b, j0 = GROUPS[n]
-            codes, plane = wb_mx[b]
+            codes, plane = wb_mx[b, pair]
             bank = new_bank([P, 2, QUARTER], "bank_b", slow)
             for t in slices(pair):
-                cols = slice(t * P, (t + 1) * P)
+                cols = slice(t % 2 * P, (t % 2 + 1) * P)
                 first_stage(bank[:, t % 2, :], codes[:, cols].bitcast(FP8X4), plane[:, cols], j0, QUARTER)
             part = kept([P, 2, QUARTER], F32, "tanh", tag=tanh_tag(n, pair))
             nc.scalar.activation(part[:], bank[:], ACT.Tanh, scale=-1.0 if n in (LATE_A, LATE_B) else 1.0)
@@ -431,10 +428,10 @@ def tile_list_motet_voice_completion_kernel(
 
         both(gate_of, 0)
         gate_of(1, 0)
-        gate_of(1, 1, slow=True)
-        for pair in PAIRS:
-            tanh_of(0, pair, slow=True)
+        tanh_of(0, 0, slow=True)
         both(linear_of, 0)
+        tanh_of(0, 1, slow=True)
+        gate_of(1, 1, slow=True)
         both(tanh_of, 1)
         both(linear_of, 1)
         both(difference, 0)
@@ -510,7 +507,7 @@ def tile_list_motet_voice_completion_kernel(
         both(linear_of, LAST)
         both(linear_share, LAST)
         both(tanh_of, LAST)
-        weighted = weighted_by_vector(2, "wb_codes1")
+        weighted = weighted_by_vector(2, "wb_codes1_1")
         nc.vector.tensor_copy(window(2, 0), weighted[:])
         scaled = scaled_tanh(LAST)
         last_share = placed.tile([P, PACK, QUARTER], F32, name="last_share", offset=LAST_SHARE_AT)

@@ -45,6 +45,8 @@ LAST_SHARE_AT = 0
 LAST_ROWS_AT = {LATE_A: GROUP_BYTES, LATE_B: GROUP_BYTES + ROW_BYTES}
 LAST_Y_AT = GROUP_BYTES // 2
 HALF_DIFFERENCE_AT = GROUP_BYTES + 2 * ROW_BYTES
+SECOND_PRODUCT_AT = HALF_DIFFERENCE_AT + GROUP_BYTES
+FIRST_DIFFERENCE_AT = SECOND_PRODUCT_AT + GROUP_BYTES // 2
 
 
 def tile_list_motet_voice_completion_kernel(
@@ -72,11 +74,11 @@ def tile_list_motet_voice_completion_kernel(
 
         offs_sb = keep.tile([P, S // LIST_ROWS], U16, name="offs_sb")
         nc.sync.dma_start(offs_sb[:], offs)
+        offs2_sb = keep.tile([P, S // LIST_ROWS], U16, name="offs2_sb")
+        nc.sync.dma_start(offs2_sb[:], offs2)
         tab_bytes = kept([P, T], U8, "tab_bytes")
-        nc.sync.dma_start(
-            tab_bytes[:].bitcast(I32),
-            tab_scales[0].bitcast(I32).unsqueeze(1).broadcast_to([BLOCKS, RUN, T // 4]),
-        )
+        nc.gpsimd.memset(tab_bytes[:].bitcast(I32), 0)
+        nc.sync.dma_start(tab_bytes[0:P:RUN, :].bitcast(I32), tab_scales[0].bitcast(I32))
         raw_scales = kept([P, 2, H], U8, "raw_scales")
         for which, scales in enumerate((wa_scales, wc_scales)):
             repeated = scales[0].bitcast(I32).unsqueeze(1).broadcast_to([BLOCKS, RUN, H // 4])
@@ -88,12 +90,6 @@ def tile_list_motet_voice_completion_kernel(
         tab = kept([P, T], U32, "tab")
         nc.sync.dma_start(tab[:].bitcast(I32), tab_words[0].rearrange("p t i -> p (t i)").bitcast(I32))
         wb_raw = {0: load([P, PACK, PASS], F32, "wb_raw0", wb_rows[:, :, :PASS])}
-
-        block_gains = kept([P, PASSES, PACK * RUN], F32, "block_gains")
-        gain_blocks = gain.rearrange("(b q c) -> b q c", b=PASSES, q=BLOCKS)
-        for b in range(PASSES):
-            repeated = gain_blocks[b].unsqueeze(1).broadcast_to([BLOCKS, RUN, PACK * RUN])
-            nc.scalar.dma_start(block_gains[:, b, :], repeated)
 
         distance = kept([P, RUN], I32, "distance")
         nc.gpsimd.iota(distance[:], pattern=[[-1, RUN]], base=0, channel_multiplier=1)
@@ -131,11 +127,14 @@ def tile_list_motet_voice_completion_kernel(
         nc.gpsimd.memset(pages[-1][:], 0.0)
 
         wc_raw = {0: load([P, PASS], I32, "wc_raw0", wc_rows[:, :PASS])}
+        block_gains = kept([P, PASSES, PACK * RUN], F32, "block_gains")
+        gain_blocks = gain.rearrange("(b q c) -> b q c", b=PASSES, q=BLOCKS)
+        for b in range(PASSES):
+            repeated = gain_blocks[b].unsqueeze(1).broadcast_to([BLOCKS, RUN, PACK * RUN])
+            nc.sync.dma_start(block_gains[:, b, :], repeated)
         wa_raw[1] = load([P, PASS // 2], I32, "wa_raw1", wa_rows[:, PASS // 2 :])
         wc_raw[1] = load([P, PASS], I32, "wc_raw1", wc_rows[:, PASS:])
         wb_raw[1] = load([P, PACK, PASS], F32, "wb_raw1", wb_rows[:, :, PASS:])
-        offs2_sb = keep.tile([P, S // LIST_ROWS], U16, name="offs2_sb")
-        nc.sync.dma_start(offs2_sb[:], offs2)
         wd_rows = wd.rearrange("(b q t i) n -> b t q i n", b=PASSES, t=PACK, i=RUN)
         wd_raw = [kept([P, PACK, N], F32, "wd_raw%d" % b) for b in range(PASSES)]
         for b in range(PASSES):
@@ -153,26 +152,26 @@ def tile_list_motet_voice_completion_kernel(
 
         wb_mx, wc_codes = {}, {}
 
-        def round_wb(b, tag):
-            grouped = kept([P, PACK, BLOCKS, RUN, PACK], BF16, "wb_grouped%d" % b, tag=tag)
-            blocks = wb_raw[b][:].rearrange("p row (q t i) -> p t q i row", t=PACK, i=RUN)
-            for pair in PAIRS:
-                nc.vector.tensor_copy(grouped[:, 2 * pair : 2 * pair + 2], blocks[:, 2 * pair : 2 * pair + 2])
+        wb_pair_shape = [P, 2, BLOCKS, RUN, PACK]
+
+        def round_wb(b, pair, grouped, copy, walk):
+            blocks = wb_raw[b][:].rearrange("p row (q t i) -> " + walk, t=PACK, i=RUN)
+            copy(grouped[:].rearrange("p t q i row -> " + walk), blocks[:, 2 * pair : 2 * pair + 2])
             return grouped
 
-        def quantise_wb(b, grouped, pair, tag=None):
-            codes = kept([P, 2 * P], U32, "wb_codes%d_%d" % (b, pair), tag=tag)
+        def quantise_wb(b, pair, grouped, codes):
             plane = kept([P, 2 * P], U8, "wb_plane%d_%d" % (b, pair))
             nc.vector.quantize_mx(
-                out=codes[:].bitcast(FP8X4), scales=plane[:],
-                in_=grouped[:, 2 * pair : 2 * pair + 2].rearrange("p t q i row -> p (t q i row)"),
+                out=codes[:].bitcast(FP8X4), scales=plane[:], in_=grouped[:].rearrange("p t q i row -> p (t q i row)")
             )
             wb_mx[b, pair] = codes, plane
 
-        grouped = round_wb(0, "wb_grouped0")
-        quantise_wb(0, grouped, 0)
+        on_vector = (nc.vector.tensor_copy, "p t q i row")
+        on_scalar = (nc.scalar.copy, "p t q row i")
+        grouped = [round_wb(0, pair, kept(wb_pair_shape, BF16, "wb_grouped0_%d" % pair), *on_vector) for pair in PAIRS]
+        quantise_wb(0, 0, grouped[0], kept([P, 2 * P], U32, "wb_codes0_0"))
         wc_codes[0] = reorder(wc_raw[0], "wc_codes0")
-        quantise_wb(0, grouped, 1, tag="wc_raw0")
+        quantise_wb(0, 1, grouped[1], kept([P, 2 * P], U32, "wb_codes0_1", tag="wc_raw0"))
         wa_codes[1] = reorder(wa_raw[1], "wa_codes1")
         wc_codes[1] = reorder(wc_raw[1], "wc_codes1")
 
@@ -211,6 +210,7 @@ def tile_list_motet_voice_completion_kernel(
 
         tanh, gate, c_banks, from_c, from_gate, h_rows = {}, {}, {}, {}, {}, {}
         wd_mx, h_mx, wide_banks = {}, {}, {}
+        group_shape = [P, PACK, QUARTER]
 
         def slices(pair):
             return range(2 * pair, 2 * pair + 2)
@@ -228,6 +228,8 @@ def tile_list_motet_voice_completion_kernel(
             )
 
         def tanh_tag(n, pair):
+            if n == LATE_A:
+                return "wd_raw%d" % (1 - pair)
             return "tanh%d_%d" % (n - (LAST - LAST_OF_HALF) if n > LATE_A else n, pair)
 
         def tanh_of(n, pair, slow=False):
@@ -279,12 +281,16 @@ def tile_list_motet_voice_completion_kernel(
             column = GROUPS[n][0] * PACK + t
             return gains[:, column : column + 1]
 
-        def product_tag(n):
-            return "product%d" % (n % 3)
+        def product_tile(n, shape, dtype):
+            if n % 3 == 1:
+                return placed.tile(shape, dtype, name="product%d" % n, offset=SECOND_PRODUCT_AT, align_bytes=64)
+            return kept(shape, dtype, "product", tag="product%d" % (n % 3))
 
         def from_c_tile(n):
             if n not in from_c and n == 0:
-                from_c[n] = kept([P, PACK, QUARTER], F32, "from_c_first", tag=product_tag(1))
+                from_c[n] = placed.tile(
+                    [P, PACK, QUARTER], F32, name="from_c_first", offset=FIRST_DIFFERENCE_AT, align_bytes=64
+                )
             if n not in from_c and n == LAST_OF_HALF:
                 from_c[n] = placed.tile(
                     [P, PACK, QUARTER], F32, name="from_c_half", offset=HALF_DIFFERENCE_AT, align_bytes=64
@@ -318,13 +324,13 @@ def tile_list_motet_voice_completion_kernel(
                     wide_banks[n, pair][:, t % 2, :], ALU.mult, ALU.subtract,
                 )
 
-        def multiply(n, left, right, tag, parts=(slice(0, PACK),)):
-            from_gate[n] = kept([P, PACK, QUARTER], F32, "from_gate", tag=tag)
+        def multiply(n, left, right, tile, parts=(slice(0, PACK),)):
+            from_gate[n] = tile
             for part in parts:
                 nc.gpsimd.tensor_tensor(from_gate[n][:, part], left[:, part], right[:, part], ALU.mult)
 
         def product(n):
-            multiply(n, from_c[n], gate[n], product_tag(n))
+            multiply(n, from_c[n], gate[n], product_tile(n, group_shape, F32))
 
         def interpolate(n):
             for step, cols in enumerate(STEPS):
@@ -435,16 +441,20 @@ def tile_list_motet_voice_completion_kernel(
         both(tanh_of, 1)
         both(linear_of, 1)
         both(difference, 0)
-        multiply(0, from_c[0], gate[0], product_tag(0), [slice(2 * pair, 2 * pair + 2) for pair in PAIRS])
+        multiply(0, from_c[0], gate[0], product_tile(0, group_shape, F32), [slice(2 * pair, 2 * pair + 2) for pair in PAIRS])
         both(difference, 1)
         both(tanh_of, 2)
         wide_linear_of(2, 0)
         both(gate_of, 2)
         wide_difference(2, 0)
 
-        grouped = round_wb(1, product_tag(1))
-        for pair in PAIRS:
-            quantise_wb(1, grouped, pair)
+        grouped = {}
+        for pair in reversed(PAIRS):
+            offset = FIRST_DIFFERENCE_AT + pair * GROUP_BYTES // 2
+            tile = placed.tile(wb_pair_shape, BF16, name="wb_grouped1_%d" % pair, offset=offset, align_bytes=64)
+            grouped[pair] = round_wb(1, pair, tile, *on_vector)
+        for pair in reversed(PAIRS):
+            quantise_wb(1, pair, grouped[pair], kept([P, 2 * P], U32, "wb_codes1_%d" % pair))
         product(1)
         interpolate(0)
         wide_linear_of(2, 1)
@@ -466,8 +476,8 @@ def tile_list_motet_voice_completion_kernel(
 
         both(gate_of, LATE_A)
         both(gate_of, LATE_B)
-        both(tanh_of, LATE_A)
         wd_grouped = [round_wd(b, tanh_tag(2, b)) for b in range(PASSES)]
+        both(tanh_of, LATE_A)
         wide_difference(LAST_OF_HALF, 1)
         product(LAST_OF_HALF)
         for n in (LAST_OF_HALF - 1, LAST_OF_HALF):
@@ -489,15 +499,15 @@ def tile_list_motet_voice_completion_kernel(
                 out=codes[:, cols].bitcast(FP8X4), scales=plane[:, cols], in_=h_bf[0][:, b].rearrange("p j t -> p (j t)")
             )
         h_mx[0] = codes, plane
-        quantise_wd(1, kept([P, PASS], U32, "wd1_codes", tag=product_tag(LAST_OF_HALF)))
+        quantise_wd(1, product_tile(LAST_OF_HALF, [P, PASS], U32))
 
-        multiply(LATE_A, gate[LATE_A], scaled, tanh_tag(2, 1))
+        multiply(LATE_A, gate[LATE_A], scaled, kept(group_shape, F32, "product_late", tag=tanh_tag(2, 1)))
         both(tanh_of, LATE_B)
         linear_of(LATE_B, 1)
         linear_share(LATE_B, 1)
-        weighted = weighted_by_vector(0, "wb_grouped0")
+        weighted = weighted_by_vector(0, "wb_grouped0_0")
         scaled = scaled_tanh(LATE_B)
-        multiply(LATE_B, gate[LATE_B], scaled, product_tag(LATE_B))
+        multiply(LATE_B, gate[LATE_B], scaled, product_tile(LATE_B, group_shape, F32))
         nc.vector.tensor_copy(window(0, 0), weighted[:])
 
         both(gate_of, LAST)

@@ -32,6 +32,7 @@ STEPS = [slice(j, j + STEP) for j in range(0, QUARTER, STEP)]
 PAIRS = range(2)
 SLOW_BANKS = 5
 SCALAR_BANKS = 8 - SLOW_BANKS
+VECTOR_ZEROED = 256
 
 GROUPS = [(0, 0), (0, QUARTER), (0, 2 * QUARTER), (1, 0), (1, QUARTER)]
 FIRST_OF_PASS_1 = 3
@@ -47,6 +48,8 @@ LAST_Y_AT = GROUP_BYTES // 2
 HALF_DIFFERENCE_AT = GROUP_BYTES + 2 * ROW_BYTES
 SECOND_PRODUCT_AT = HALF_DIFFERENCE_AT + GROUP_BYTES
 FIRST_DIFFERENCE_AT = SECOND_PRODUCT_AT + GROUP_BYTES // 2
+WA_FIRST_AT = FIRST_DIFFERENCE_AT + GROUP_BYTES
+LAST_PAGE_AT = WA_FIRST_AT + PASS
 
 
 def tile_list_motet_voice_completion_kernel(
@@ -79,25 +82,24 @@ def tile_list_motet_voice_completion_kernel(
         tab_bytes = kept([P, T], U8, "tab_bytes")
         nc.gpsimd.memset(tab_bytes[:].bitcast(I32), 0)
         nc.sync.dma_start(tab_bytes[0:P:RUN, :].bitcast(I32), tab_scales[0].bitcast(I32))
-        raw_scales = kept([P, 2, H], U8, "raw_scales")
-        for which, scales in enumerate((wa_scales, wc_scales)):
-            repeated = scales[0].bitcast(I32).unsqueeze(1).broadcast_to([BLOCKS, RUN, H // 4])
-            nc.sync.dma_start(raw_scales[:, which, :].bitcast(I32), repeated)
         wa_rows = wa_words[0].bitcast(I32)
         wb_rows = wb.rearrange("(p row) c -> p row c", row=PACK)
         wc_rows = wc_words[0].rearrange("p e i -> p (e i)").bitcast(I32)
-        wa_raw = {0: load([P, PASS // 2], I32, "wa_raw0", wa_rows[:, : PASS // 2])}
+        wa_raw = {0: placed.tile([P, PASS // 2], I32, name="wa_raw0", offset=WA_FIRST_AT, align_bytes=64)}
+        nc.sync.dma_start(wa_raw[0][:], wa_rows[:, : PASS // 2])
+        raw_scales = kept([P, 2, H], U8, "raw_scales")
+        nc.gpsimd.memset(raw_scales[:].rearrange("p s c -> p (s c)").bitcast(I32), 0)
+        for which, scales in enumerate((wa_scales, wc_scales)):
+            nc.sync.dma_start(raw_scales[0:P:RUN, which, :].bitcast(I32), scales[0].bitcast(I32))
         tab = kept([P, T], U32, "tab")
         nc.sync.dma_start(tab[:].bitcast(I32), tab_words[0].rearrange("p t i -> p (t i)").bitcast(I32))
         wb_raw = {0: load([P, PACK, PASS], F32, "wb_raw0", wb_rows[:, :, :PASS])}
 
-        distance = kept([P, RUN], I32, "distance")
-        nc.gpsimd.iota(distance[:], pattern=[[-1, RUN]], base=0, channel_multiplier=1)
-
         pages = [kept([P, T2], F32, "page%d" % pg) for pg in range(PACK - 1)]
         zero_on_vector(pages[0])
-        for page in pages[1:]:
-            nc.gpsimd.memset(page[:], 0.0)
+        nc.gpsimd.memset(pages[1][:], 0.0)
+        zero_on_vector(pages[2][:, :VECTOR_ZEROED])
+        nc.gpsimd.memset(pages[2][:, VECTOR_ZEROED:], 0.0)
 
         def reorder(raw, name):
             codes = kept(list(raw.shape), I32, name)
@@ -123,7 +125,9 @@ def tile_list_motet_voice_completion_kernel(
             nc.sync.dma_start(planes[x:P:QUADRANT, :].bitcast(I32), planes[RUN * x : P : QUADRANT, :].bitcast(I32))
 
         wa_codes = {0: reorder(wa_raw[0], "wa_codes0")}
-        pages.append(kept([P, T2], F32, "page3", tag="wa_raw0"))
+        distance = placed.tile([P, RUN], I32, name="distance", offset=WA_FIRST_AT, align_bytes=64)
+        nc.gpsimd.iota(distance[:], pattern=[[-1, RUN]], base=0, channel_multiplier=1)
+        pages.append(placed.tile([P, T2], F32, name="page3", offset=LAST_PAGE_AT, align_bytes=64))
         nc.gpsimd.memset(pages[-1][:], 0.0)
 
         wc_raw = {0: load([P, PASS], I32, "wc_raw0", wc_rows[:, :PASS])}

@@ -32,7 +32,7 @@ STEPS = [slice(j, j + STEP) for j in range(0, QUARTER, STEP)]
 PAIRS = range(2)
 SLOW_BANKS = 5
 SCALAR_BANKS = 8 - SLOW_BANKS
-VECTOR_ZEROED = 256
+VECTOR_ZEROED = 448
 
 GROUPS = [(0, 0), (0, QUARTER), (0, 2 * QUARTER), (1, 0), (1, QUARTER)]
 FIRST_OF_PASS_1 = 3
@@ -48,8 +48,6 @@ LAST_Y_AT = GROUP_BYTES // 2
 HALF_DIFFERENCE_AT = GROUP_BYTES + 2 * ROW_BYTES
 SECOND_PRODUCT_AT = HALF_DIFFERENCE_AT + GROUP_BYTES
 FIRST_DIFFERENCE_AT = SECOND_PRODUCT_AT + GROUP_BYTES // 2
-WA_FIRST_AT = FIRST_DIFFERENCE_AT + GROUP_BYTES
-LAST_PAGE_AT = WA_FIRST_AT + PASS
 
 
 def tile_list_motet_voice_completion_kernel(
@@ -85,8 +83,7 @@ def tile_list_motet_voice_completion_kernel(
         wa_rows = wa_words[0].bitcast(I32)
         wb_rows = wb.rearrange("(p row) c -> p row c", row=PACK)
         wc_rows = wc_words[0].rearrange("p e i -> p (e i)").bitcast(I32)
-        wa_raw = {0: placed.tile([P, PASS // 2], I32, name="wa_raw0", offset=WA_FIRST_AT, align_bytes=64)}
-        nc.sync.dma_start(wa_raw[0][:], wa_rows[:, : PASS // 2])
+        wa_raw = {0: load([P, PASS // 2], I32, "wa_raw0", wa_rows[:, : PASS // 2])}
         raw_scales = kept([P, 2, H], U8, "raw_scales")
         nc.gpsimd.memset(raw_scales[:].rearrange("p s c -> p (s c)").bitcast(I32), 0)
         for which, scales in enumerate((wa_scales, wc_scales)):
@@ -94,6 +91,9 @@ def tile_list_motet_voice_completion_kernel(
         tab = kept([P, T], U32, "tab")
         nc.sync.dma_start(tab[:].bitcast(I32), tab_words[0].rearrange("p t i -> p (t i)").bitcast(I32))
         wb_raw = {0: load([P, PACK, PASS], F32, "wb_raw0", wb_rows[:, :, :PASS])}
+
+        distance = kept([P, RUN], I32, "distance")
+        nc.gpsimd.iota(distance[:], pattern=[[-1, RUN]], base=0, channel_multiplier=1)
 
         pages = [kept([P, T2], F32, "page%d" % pg) for pg in range(PACK - 1)]
         zero_on_vector(pages[0])
@@ -125,9 +125,7 @@ def tile_list_motet_voice_completion_kernel(
             nc.sync.dma_start(planes[x:P:QUADRANT, :].bitcast(I32), planes[RUN * x : P : QUADRANT, :].bitcast(I32))
 
         wa_codes = {0: reorder(wa_raw[0], "wa_codes0")}
-        distance = placed.tile([P, RUN], I32, name="distance", offset=WA_FIRST_AT, align_bytes=64)
-        nc.gpsimd.iota(distance[:], pattern=[[-1, RUN]], base=0, channel_multiplier=1)
-        pages.append(placed.tile([P, T2], F32, name="page3", offset=LAST_PAGE_AT, align_bytes=64))
+        pages.append(kept([P, T2], F32, "page3", tag="raw_scales"))
         nc.gpsimd.memset(pages[-1][:], 0.0)
 
         wc_raw = {0: load([P, PASS], I32, "wc_raw0", wc_rows[:, :PASS])}
@@ -420,7 +418,7 @@ def tile_list_motet_voice_completion_kernel(
                 )
             return bank
 
-        y_tags = ["wc_raw0", "wc_raw1", "tab_bytes", "raw_scales"]
+        y_tags = ["wc_raw0", "wc_raw1", "tab_bytes", "wa_raw0"]
 
         def copied_projection(pg, half):
             y = kept([P, HALF], F32, "y%d_%d" % (pg, half), tag=y_tags[pg])

@@ -101,11 +101,11 @@ def tile_list_motet_voice_completion_kernel(
         zero_on_vector(pages[2][:, :VECTOR_ZEROED])
         nc.gpsimd.memset(pages[2][:, VECTOR_ZEROED:], 0.0)
 
-        def reorder(raw, name):
+        def reorder(raw, name, copy=nc.vector.tensor_copy, dtype=I32):
             codes = kept(list(raw.shape), I32, name)
-            nc.vector.tensor_copy(
-                codes[:].rearrange("p (t q w) -> p t q w", t=PACK, q=BLOCKS),
-                raw[:].rearrange("p (q t w) -> p t q w", t=PACK, q=BLOCKS),
+            copy(
+                codes[:].bitcast(dtype).rearrange("p (t q w) -> p t q w", t=PACK, q=BLOCKS),
+                raw[:].bitcast(dtype).rearrange("p (q t w) -> p t q w", t=PACK, q=BLOCKS),
             )
             return codes
 
@@ -114,9 +114,9 @@ def tile_list_motet_voice_completion_kernel(
         v_plane = planes[:, 2 * H :]
         v_bytes = kept([P, S], U8, "v_bytes")
         nc.vector.tensor_copy(v_bytes[:], tab_bytes[:].indirect(offs_sb[:]))
-        nc.vector.tensor_copy(
-            planes[:, : 2 * H].bitcast(I32).rearrange("p (g t q w) -> p g t q w", t=PACK, q=BLOCKS, w=RUN // 4),
-            raw_scales[:].rearrange("p s c -> p (s c)").bitcast(I32).rearrange(
+        nc.scalar.copy(
+            planes[:, : 2 * H].bitcast(U32).rearrange("p (g t q w) -> p g t q w", t=PACK, q=BLOCKS, w=RUN // 4),
+            raw_scales[:].rearrange("p s c -> p (s c)").bitcast(U32).rearrange(
                 "p (g q t w) -> p g t q w", t=PACK, q=BLOCKS, w=RUN // 4
             ),
         )
@@ -124,8 +124,8 @@ def tile_list_motet_voice_completion_kernel(
         for x in range(1, PACK):
             nc.sync.dma_start(planes[x:P:QUADRANT, :].bitcast(I32), planes[RUN * x : P : QUADRANT, :].bitcast(I32))
 
-        wa_codes = {0: reorder(wa_raw[0], "wa_codes0")}
-        pages.append(kept([P, T2], F32, "page3", tag="raw_scales"))
+        wa_codes = {0: reorder(wa_raw[0], "wa_codes0", nc.scalar.copy, U32)}
+        pages.append(kept([P, T2], F32, "page3", tag="v_bytes"))
         nc.gpsimd.memset(pages[-1][:], 0.0)
 
         wc_raw = {0: load([P, PASS], I32, "wc_raw0", wc_rows[:, :PASS])}

@@ -27,6 +27,7 @@ QUADRANT = 32
 BANK = 512
 HALF = S // 2
 QUARTER = S // 4
+AHEAD_OF_MOVES = 12
 STEP = BANK // PACK
 STEPS = [slice(j, j + STEP) for j in range(0, QUARTER, STEP)]
 PAIRS = range(2)
@@ -75,22 +76,22 @@ def tile_list_motet_voice_completion_kernel(
 
         offs_sb = keep.tile([P, S // LIST_ROWS], U16, name="offs_sb")
         nc.sync.dma_start(offs_sb[:], offs)
-        offs2_sb = keep.tile([P, S // LIST_ROWS], U16, name="offs2_sb")
-        nc.sync.dma_start(offs2_sb[:], offs2)
+        wa_rows = wa_words[0].bitcast(I32)
+        wa_raw = {0: load([P, PASS // 2], I32, "wa_raw0", wa_rows[:, : PASS // 2])}
         tab_bytes = kept([P, T], U8, "tab_bytes")
         nc.gpsimd.memset(tab_bytes[:].bitcast(I32), 0)
         nc.sync.dma_start(tab_bytes[0:P:RUN, :].bitcast(I32), tab_scales[0].bitcast(I32))
-        wa_rows = wa_words[0].bitcast(I32)
         wb_rows = wb.rearrange("(p row) c -> p row c", row=PACK)
         wc_rows = wc_words[0].rearrange("p e i -> p (e i)").bitcast(I32)
-        wa_raw = {0: load([P, PASS // 2], I32, "wa_raw0", wa_rows[:, : PASS // 2])}
         raw_scales = kept([P, 2, H], U8, "raw_scales")
         nc.gpsimd.memset(raw_scales[:].rearrange("p s c -> p (s c)").bitcast(I32), 0)
         for which, scales in enumerate((wa_scales, wc_scales)):
             nc.sync.dma_start(raw_scales[0:P:RUN, which, :].bitcast(I32), scales[0].bitcast(I32))
         tab = kept([P, T], U32, "tab")
         nc.sync.dma_start(tab[:].bitcast(I32), tab_words[0].rearrange("p t i -> p (t i)").bitcast(I32))
-        wb_raw = {0: load([P, PACK, PASS], F32, "wb_raw0", wb_rows[:, :, :PASS])}
+        wb_raw = {0: kept([P, PACK, PASS], F32, "wb_raw0")}
+        ahead = AHEAD_OF_MOVES * PASS // BLOCKS
+        nc.sync.dma_start(wb_raw[0][:, :, :ahead], wb_rows[:, :, :ahead])
 
         distance = kept([P, RUN], I32, "distance")
         nc.gpsimd.iota(distance[:], pattern=[[-1, RUN]], base=0, channel_multiplier=1)
@@ -128,14 +129,15 @@ def tile_list_motet_voice_completion_kernel(
         pages.append(kept([P, T2], F32, "page3", tag="v_bytes"))
         nc.gpsimd.memset(pages[-1][:], 0.0)
 
+        nc.sync.dma_start(wb_raw[0][:, :, ahead:], wb_rows[:, :, ahead:PASS])
         wc_raw = {0: load([P, PASS], I32, "wc_raw0", wc_rows[:, :PASS])}
+        wa_raw[1] = load([P, PASS // 2], I32, "wa_raw1", wa_rows[:, PASS // 2 :])
+        wc_raw[1] = load([P, PASS], I32, "wc_raw1", wc_rows[:, PASS:])
         block_gains = kept([P, PASSES, PACK * RUN], F32, "block_gains")
         gain_blocks = gain.rearrange("(b q c) -> b q c", b=PASSES, q=BLOCKS)
         for b in range(PASSES):
             repeated = gain_blocks[b].unsqueeze(1).broadcast_to([BLOCKS, RUN, PACK * RUN])
             nc.sync.dma_start(block_gains[:, b, :], repeated)
-        wa_raw[1] = load([P, PASS // 2], I32, "wa_raw1", wa_rows[:, PASS // 2 :])
-        wc_raw[1] = load([P, PASS], I32, "wc_raw1", wc_rows[:, PASS:])
         wb_raw[1] = load([P, PACK, PASS], F32, "wb_raw1", wb_rows[:, :, PASS:])
         wd_rows = wd.rearrange("(b q t i) n -> b t q i n", b=PASSES, t=PACK, i=RUN)
         wd_raw = [kept([P, PACK, N], F32, "wd_raw%d" % b) for b in range(PASSES)]
@@ -143,6 +145,8 @@ def tile_list_motet_voice_completion_kernel(
             for t in range(PACK):
                 nc.sync.dma_start(wd_raw[b][:, t, :], wd_rows[b, t])
         wgo_sb = load([P, S], F32, "wgo_sb", wgo)
+        offs2_sb = keep.tile([P, S // LIST_ROWS], U16, name="offs2_sb")
+        nc.sync.dma_start(offs2_sb[:], offs2)
 
 
         v_words = []
@@ -156,9 +160,9 @@ def tile_list_motet_voice_completion_kernel(
 
         wb_pair_shape = [P, 2, BLOCKS, RUN, PACK]
 
-        def round_wb(b, pair, grouped, copy, walk):
+        def round_wb(b, pair, grouped, copy, walk, qs=slice(0, BLOCKS)):
             blocks = wb_raw[b][:].rearrange("p row (q t i) -> " + walk, t=PACK, i=RUN)
-            copy(grouped[:].rearrange("p t q i row -> " + walk), blocks[:, 2 * pair : 2 * pair + 2])
+            copy(grouped[:].rearrange("p t q i row -> " + walk)[:, :, qs], blocks[:, 2 * pair : 2 * pair + 2, qs])
             return grouped
 
         def quantise_wb(b, pair, grouped, codes):
@@ -170,7 +174,10 @@ def tile_list_motet_voice_completion_kernel(
 
         on_vector = (nc.vector.tensor_copy, "p t q i row")
         on_scalar = (nc.scalar.copy, "p t q row i")
-        grouped = [round_wb(0, pair, kept(wb_pair_shape, BF16, "wb_grouped0_%d" % pair), *on_vector) for pair in PAIRS]
+        grouped = [kept(wb_pair_shape, BF16, "wb_grouped0_%d" % pair) for pair in PAIRS]
+        for qs in (slice(0, AHEAD_OF_MOVES), slice(AHEAD_OF_MOVES, BLOCKS)):
+            for pair in PAIRS:
+                round_wb(0, pair, grouped[pair], *on_vector, qs)
         quantise_wb(0, 0, grouped[0], kept([P, 2 * P], U32, "wb_codes0_0"))
         wc_codes[0] = reorder(wc_raw[0], "wc_codes0")
         quantise_wb(0, 1, grouped[1], kept([P, 2 * P], U32, "wb_codes0_1", tag="wc_raw0"))

from contextlib import ExitStack

import concourse.mybir as mybir

K, H, N, T, S, T2 = 512, 1024, 512, 2048, 1024, 2048
FLOPS = 2 * S * (3 * K * H + H * N)

F32 = mybir.dt.float32
BF16 = mybir.dt.bfloat16
I32 = mybir.dt.int32
U32 = mybir.dt.uint32
U16 = mybir.dt.uint16
U8 = mybir.dt.uint8
FP8X4 = mybir.dt.float8_e4m3fn_x4
FP4X4 = mybir.dt.float4_e2m1fn_x4
ALU = mybir.AluOpType
ACT = mybir.ActivationFunctionType

P = 128
PACK = 4
RUN = 8
BLOCKS = P // RUN
PASS = P * PACK
PASSES = H // PASS
LIST_ROWS = 16
QUADRANT = 32
BANK = 512
HALF = S // 2
QUARTER = S // 4
AHEAD_OF_MOVES = 12
STEP = BANK // PACK
STEPS = [slice(j, j + STEP) for j in range(0, QUARTER, STEP)]
PAIRS = range(2)
SLOW_BANKS = 5
SCALAR_BANKS = 8 - SLOW_BANKS
VECTOR_ZEROED = 448

GROUPS = [(0, 0), (0, QUARTER), (0, 2 * QUARTER), (1, 0), (1, QUARTER)]
FIRST_OF_PASS_1 = 3
LAST_OF_HALF = len(GROUPS) - 1
GROUPS = GROUPS + [(0, 3 * QUARTER), (1, 2 * QUARTER), (1, 3 * QUARTER)]
LATE_A, LATE_B, LAST = range(LAST_OF_HALF + 1, len(GROUPS))

GROUP_BYTES = PACK * QUARTER * 4
ROW_BYTES = P * PACK * 2
LAST_SHARE_AT = 0
LAST_ROWS_AT = {LATE_A: GROUP_BYTES, LATE_B: GROUP_BYTES + ROW_BYTES}
LAST_Y_AT = GROUP_BYTES // 2
HALF_DIFFERENCE_AT = GROUP_BYTES + 2 * ROW_BYTES
SECOND_PRODUCT_AT = HALF_DIFFERENCE_AT + GROUP_BYTES
FIRST_DIFFERENCE_AT = SECOND_PRODUCT_AT + GROUP_BYTES // 2


def tile_list_motet_voice_completion_kernel(
    tc, tab_words, tab_scales, offs, wa_words, wa_scales, wb, wc_words, wc_scales, gain, wd, wgo, offs2, out
):
    nc = tc.nc
    with ExitStack() as ctx:
        keep = ctx.enter_context(tc.tile_pool(name="keep", bufs=1))
        ring = ctx.enter_context(tc.tile_pool(name="ring", bufs=2))
        psum = ctx.enter_context(tc.psum_pool(name="psum", bufs=SCALAR_BANKS))
        placed = ctx.enter_context(tc.tile_pool(name="placed", bufs=1))

        def kept(shape, dtype, name, tag=None):
            return keep.tile(shape, dtype, name=name, tag=tag or name, align_bytes=64)

        def load(shape, dtype, name, source):
            tile = kept(shape, dtype, name)
            nc.sync.dma_start(tile[:], source)
            return tile

        def zero_on_vector(tile):
            width = tile.shape[1]
            for cols in (slice(0, width // 2 - 1), slice(width // 2 - 1, width)):
                nc.vector.memset(tile[:, cols], 0.0)

        offs_sb = keep.tile([P, S // LIST_ROWS], U16, name="offs_sb")
        nc.sync.dma_start(offs_sb[:], offs)
        wa_rows = wa_words[0].bitcast(I32)
        wa_raw = {0: load([P, PASS // 2], I32, "wa_raw0", wa_rows[:, : PASS // 2])}
        tab_bytes = kept([P, T], U8, "tab_bytes")
        nc.gpsimd.memset(tab_bytes[:].bitcast(I32), 0)
        nc.sync.dma_start(tab_bytes[0:P:RUN, :].bitcast(I32), tab_scales[0].bitcast(I32))
        wb_rows = wb.rearrange("(p row) c -> p row c", row=PACK)
        wc_rows = wc_words[0].rearrange("p e i -> p (e i)").bitcast(I32)
        raw_scales = kept([P, 2, H], U8, "raw_scales")
        nc.gpsimd.memset(raw_scales[:].rearrange("p s c -> p (s c)").bitcast(I32), 0)
        for which, scales in enumerate((wa_scales, wc_scales)):
            nc.sync.dma_start(raw_scales[0:P:RUN, which, :].bitcast(I32), scales[0].bitcast(I32))
        tab = kept([P, T], U32, "tab")
        nc.sync.dma_start(tab[:].bitcast(I32), tab_words[0].rearrange("p t i -> p (t i)").bitcast(I32))
        wb_raw = {0: kept([P, PACK, PASS], F32, "wb_raw0")}
        ahead = AHEAD_OF_MOVES * PASS // BLOCKS
        nc.sync.dma_start(wb_raw[0][:, :, :ahead], wb_rows[:, :, :ahead])

        distance = kept([P, RUN], I32, "distance")
        nc.gpsimd.iota(distance[:], pattern=[[-1, RUN]], base=0, channel_multiplier=1)

        pages = [kept([P, T2], F32, "page%d" % pg) for pg in range(PACK - 1)]
        zero_on_vector(pages[0])
        nc.gpsimd.memset(pages[1][:], 0.0)
        zero_on_vector(pages[2][:, :VECTOR_ZEROED])
        nc.gpsimd.memset(pages[2][:, VECTOR_ZEROED:], 0.0)

        def reorder(raw, name, copy=nc.vector.tensor_copy, dtype=I32):
            codes = kept(list(raw.shape), I32, name)
            copy(
                codes[:].bitcast(dtype).rearrange("p (t q w) -> p t q w", t=PACK, q=BLOCKS),
                raw[:].bitcast(dtype).rearrange("p (q t w) -> p t q w", t=PACK, q=BLOCKS),
            )
            return codes

        planes = kept([P, 2 * H + S], U8, "planes")
        w_scales = planes[:, : 2 * H].rearrange("p (s c) -> p s c", s=2)
        v_plane = planes[:, 2 * H :]
        v_bytes = kept([P, S], U8, "v_bytes")
        nc.vector.tensor_copy(v_bytes[:], tab_bytes[:].indirect(offs_sb[:]))
        nc.scalar.copy(
            planes[:, : 2 * H].bitcast(U32).rearrange("p (g t q w) -> p g t q w", t=PACK, q=BLOCKS, w=RUN // 4),
            raw_scales[:].rearrange("p s c -> p (s c)").bitcast(U32).rearrange(
                "p (g q t w) -> p g t q w", t=PACK, q=BLOCKS, w=RUN // 4
            ),
        )
        nc.vector.tensor_copy(v_plane.bitcast(I32), v_bytes[:].bitcast(I32))
        for x in range(1, PACK):
            nc.sync.dma_start(planes[x:P:QUADRANT, :].bitcast(I32), planes[RUN * x : P : QUADRANT, :].bitcast(I32))

        wa_codes = {0: reorder(wa_raw[0], "wa_codes0", nc.scalar.copy, U32)}
        pages.append(kept([P, T2], F32, "page3", tag="v_bytes"))
        nc.gpsimd.memset(pages[-1][:], 0.0)

        nc.sync.dma_start(wb_raw[0][:, :, ahead:], wb_rows[:, :, ahead:PASS])
        wc_raw = {0: load([P, PASS], I32, "wc_raw0", wc_rows[:, :PASS])}
        wa_raw[1] = load([P, PASS // 2], I32, "wa_raw1", wa_rows[:, PASS // 2 :])
        wc_raw[1] = load([P, PASS], I32, "wc_raw1", wc_rows[:, PASS:])
        block_gains = kept([P, PASSES, PACK * RUN], F32, "block_gains")
        gain_blocks = gain.rearrange("(b q c) -> b q c", b=PASSES, q=BLOCKS)
        for b in range(PASSES):
            repeated = gain_blocks[b].unsqueeze(1).broadcast_to([BLOCKS, RUN, PACK * RUN])
            nc.sync.dma_start(block_gains[:, b, :], repeated)
        wb_raw[1] = load([P, PACK, PASS], F32, "wb_raw1", wb_rows[:, :, PASS:])
        wd_rows = wd.rearrange("(b q t i) n -> b t q i n", b=PASSES, t=PACK, i=RUN)
        wd_raw = [kept([P, PACK, N], F32, "wd_raw%d" % b) for b in range(PASSES)]
        for b in range(PASSES):
            for t in range(PACK):
                nc.sync.dma_start(wd_raw[b][:, t, :], wd_rows[b, t])
        wgo_sb = load([P, S], F32, "wgo_sb", wgo)
        offs2_sb = keep.tile([P, S // LIST_ROWS], U16, name="offs2_sb")
        nc.sync.dma_start(offs2_sb[:], offs2)


        v_words = []
        for half in range(2):
            words = kept([P, HALF], U32, "v_words%d" % half)
            entries = offs_sb[:, half * HALF // LIST_ROWS : (half + 1) * HALF // LIST_ROWS]
            nc.vector.tensor_copy(words[:], tab[:].indirect(entries))
            v_words.append(words)

        wb_mx, wc_codes = {}, {}

        wb_pair_shape = [P, 2, BLOCKS, RUN, PACK]

        def round_wb(b, pair, grouped, copy, walk, qs=slice(0, BLOCKS)):
            blocks = wb_raw[b][:].rearrange("p row (q t i) -> " + walk, t=PACK, i=RUN)
            copy(grouped[:].rearrange("p t q i row -> " + walk)[:, :, qs], blocks[:, 2 * pair : 2 * pair + 2, qs])
            return grouped

        def quantise_wb(b, pair, grouped, codes):
            plane = kept([P, 2 * P], U8, "wb_plane%d_%d" % (b, pair))
            nc.vector.quantize_mx(
                out=codes[:].bitcast(FP8X4), scales=plane[:], in_=grouped[:].rearrange("p t q i row -> p (t q i row)")
            )
            wb_mx[b, pair] = codes, plane

        on_vector = (nc.vector.tensor_copy, "p t q i row")
        on_scalar = (nc.scalar.copy, "p t q row i")
        grouped = [kept(wb_pair_shape, BF16, "wb_grouped0_%d" % pair) for pair in PAIRS]
        for qs in (slice(0, AHEAD_OF_MOVES), slice(AHEAD_OF_MOVES, BLOCKS)):
            for pair in PAIRS:
                round_wb(0, pair, grouped[pair], *on_vector, qs)
        quantise_wb(0, 0, grouped[0], kept([P, 2 * P], U32, "wb_codes0_0"))
        wc_codes[0] = reorder(wc_raw[0], "wc_codes0")
        quantise_wb(0, 1, grouped[1], kept([P, 2 * P], U32, "wb_codes0_1", tag="wc_raw0"))
        wa_codes[1] = reorder(wa_raw[1], "wa_codes1")
        wc_codes[1] = reorder(wc_raw[1], "wc_codes1")

        remainder = kept([P, RUN], I32, "remainder", tag="wb_raw0")
        nc.vector.tensor_single_scalar(remainder[:], distance[:], RUN - 1, ALU.bitwise_and)
        own = kept([P, RUN], F32, "own")
        nc.vector.tensor_single_scalar(own[:], remainder[:], 0.0, ALU.is_equal)
        masked = kept([P, PASSES * PACK, RUN], F32, "masked")
        nc.vector.tensor_tensor(
            masked[:], block_gains[:].rearrange("p b (t i) -> p (b t) i", i=RUN),
            own[:].unsqueeze(1).broadcast_to([P, PASSES * PACK, RUN]), ALU.mult,
        )
        gains = kept([P, PASSES * PACK], F32, "gains")
        nc.vector.tensor_reduce(gains[:], masked[:], mybir.AxisListType.X, ALU.add)

        zeros = kept([P, P], F32, "zeros", tag="wc_raw1")
        nc.gpsimd.memset(zeros[:], 0.0)
        identity_tile = kept([P, P], F32, "identity")
        identity = identity_tile[:]
        nc.gpsimd.affine_select(
            out=identity, in_=zeros[:], compare_op=ALU.not_equal, fill=1.0, base=0,
            pattern=[[-1, P]], channel_multiplier=1,
        )

        h_bf = [
            kept([P, PASSES, HALF, PACK], BF16, "h_bf0"),
            kept([P, PASSES, HALF, PACK], BF16, "h_bf1", tag="wb_raw0"),
        ]

        def quantise(grouped, name, tag):
            width = grouped.shape[1] // PACK
            codes = kept([P, width], U32, name + "_codes", tag=tag)
            plane = kept([P, width], U8, name + "_plane")
            nc.vector.quantize_mx(out=codes[:].bitcast(FP8X4), scales=plane[:], in_=grouped)
            return codes, plane

        tanh, gate, c_banks, from_c, from_gate, h_rows = {}, {}, {}, {}, {}, {}
        wd_mx, h_mx, wide_banks = {}, {}, {}
        group_shape = [P, PACK, QUARTER]

        def slices(pair):
            return range(2 * pair, 2 * pair + 2)

        def new_bank(shape, name, slow):
            if slow:
                return psum.tile(shape, F32, name=name, tag="slow_bank", bufs=SLOW_BANKS)
            return psum.tile(shape, F32, name=name, tag="scalar_bank")

        def first_stage(bank, codes, plane, j0, width):
            words = v_words[j0 // HALF][:, j0 % HALF : j0 % HALF + width]
            nc.tensor.matmul_mx(
                out=bank, lhsT=codes, lhsT_scale=plane,
                rhs=words.bitcast(FP8X4), rhs_scale=v_plane[:, j0 : j0 + width], start=True, stop=True,
            )

        def tanh_tag(n, pair):
            if n == LATE_A:
                return "wd_raw%d" % (1 - pair)
            return "tanh%d_%d" % (n - (LAST - LAST_OF_HALF) if n > LATE_A else n, pair)

        def tanh_of(n, pair, slow=False):
            b, j0 = GROUPS[n]
            codes, plane = wb_mx[b, pair]
            bank = new_bank([P, 2, QUARTER], "bank_b", slow)
            for t in slices(pair):
                cols = slice(t % 2 * P, (t % 2 + 1) * P)
                first_stage(bank[:, t % 2, :], codes[:, cols].bitcast(FP8X4), plane[:, cols], j0, QUARTER)
            part = kept([P, 2, QUARTER], F32, "tanh", tag=tanh_tag(n, pair))
            nc.scalar.activation(part[:], bank[:], ACT.Tanh, scale=-1.0 if n in (LATE_A, LATE_B) else 1.0)
            for t in slices(pair):
                tanh[n, t] = part[:, t % 2, :]

        def gate_of(n, pair, slow=False):
            b, j0 = GROUPS[n]
            if pair == 0:
                gate[n] = ring.tile([P, PACK, QUARTER], F32, name="gate", bufs=4)
            bank = new_bank([P, 2, QUARTER], "bank_a", slow)
            for t in slices(pair):
                codes = wa_codes[b][:].bitcast(U8)[:, 2 * t * P : 2 * (t + 1) * P].bitcast(FP4X4)
                c0 = b * PASS + t * P
                first_stage(bank[:, t % 2, :], codes, w_scales[:, 0, c0 : c0 + P], j0, QUARTER)
            nc.scalar.activation(gate[n][:, 2 * pair : 2 * pair + 2, :], bank[:], ACT.Sigmoid)

        def both(function, n):
            for pair in PAIRS:
                function(n, pair)

        def linear_slice(target, n, t, j, width):
            b, j0 = GROUPS[n]
            c0 = b * PASS + t * P
            codes = wc_codes[b][:, t * P : (t + 1) * P].bitcast(FP8X4)
            first_stage(target, codes, w_scales[:, 1, c0 : c0 + P], j0 + j, width)

        def linear_of(n, step):
            bank = new_bank([P, PACK, STEP], "bank_c", True)
            for t in range(PACK):
                linear_slice(bank[:, t, :], n, t, step * STEP, STEP)
            c_banks[n, step] = bank

        def wide_linear_of(n, pair):
            bank = new_bank([P, 2, QUARTER], "bank_wide", True)
            for t in slices(pair):
                linear_slice(bank[:, t % 2, :], n, t, 0, QUARTER)
            wide_banks[n, pair] = bank

        def gain_of(n, t):
            column = GROUPS[n][0] * PACK + t
            return gains[:, column : column + 1]

        def product_tile(n, shape, dtype):
            if n % 3 == 1:
                return placed.tile(shape, dtype, name="product%d" % n, offset=SECOND_PRODUCT_AT, align_bytes=64)
            return kept(shape, dtype, "product", tag="product%d" % (n % 3))

        def from_c_tile(n):
            if n not in from_c and n == 0:
                from_c[n] = placed.tile(
                    [P, PACK, QUARTER], F32, name="from_c_first", offset=FIRST_DIFFERENCE_AT, align_bytes=64
                )
            if n not in from_c and n == LAST_OF_HALF:
                from_c[n] = placed.tile(
                    [P, PACK, QUARTER], F32, name="from_c_half", offset=HALF_DIFFERENCE_AT, align_bytes=64
                )
            if n not in from_c:
                from_c[n] = ring.tile([P, PACK, QUARTER], F32, name="from_c", bufs=3)
            return from_c[n]

        def h_cols(n, j, width):
            b, j0 = GROUPS[n]
            return h_bf[j0 // HALF][:, b, j0 % HALF + j : j0 % HALF + j + width, :]

        def by_twos(tile):
            return tile.rearrange("p t (c two) -> p c t two", two=2)

        def woven(h_part):
            return h_part.rearrange("p (c two) t -> p c t two", two=2)

        def difference(n, pair):
            for step, cols in enumerate(STEPS):
                for t in slices(pair):
                    nc.vector.scalar_tensor_tensor(
                        from_c_tile(n)[:, t, cols], tanh[n, t][:, cols], gain_of(n, t),
                        c_banks[n, step][:, t, :], ALU.mult, ALU.subtract,
                    )

        def wide_difference(n, pair):
            for t in slices(pair):
                nc.vector.scalar_tensor_tensor(
                    from_c_tile(n)[:, t, :], tanh[n, t], gain_of(n, t),
                    wide_banks[n, pair][:, t % 2, :], ALU.mult, ALU.subtract,
                )

        def multiply(n, left, right, tile, parts=(slice(0, PACK),)):
            from_gate[n] = tile
            for part in parts:
                nc.gpsimd.tensor_tensor(from_gate[n][:, part], left[:, part], right[:, part], ALU.mult)

        def product(n):
            multiply(n, from_c[n], gate[n], product_tile(n, group_shape, F32))

        def interpolate(n):
            for step, cols in enumerate(STEPS):
                nc.vector.tensor_tensor(
                    woven(h_cols(n, cols.start, STEP)),
                    by_twos(from_gate[n][:, :, cols]), by_twos(c_banks[n, step][:]), ALU.add,
                )

        def linear_share(n, step):
            cols = STEPS[step]
            nc.vector.scalar_tensor_tensor(
                from_c_tile(n)[:, :, cols], gate[n][:, :, cols], 1.0, c_banks[n, step][:], ALU.subtract, ALU.mult
            )

        def scaled_tanh(n):
            scaled = ring.tile([P, PACK, QUARTER], F32, name="scaled")
            for t in range(PACK):
                nc.scalar.activation(scaled[:, t, :], tanh[n, t], ACT.Copy, scale=gain_of(n, t))
            return scaled

        def sum_on_tensor(n, slow):
            h_rows[n] = []
            for cols in STEPS:
                turned = new_bank([P, PACK, P], "bank_turned", slow)
                for t in range(PACK):
                    for term, share in enumerate((from_gate[n], from_c[n])):
                        nc.tensor.matmul(
                            out=turned[:, t, :], lhsT=share[:, t, cols], rhs=identity,
                            is_transpose=True, start=(term == 0), stop=(term == 1),
                        )
                if cols.start == 0:
                    rows = ring.tile([P, 2, P, 2], BF16, name="h_rows")
                else:
                    rows = placed.tile([P, 2, P, 2], BF16, name="last_rows%d" % n, offset=LAST_ROWS_AT[n])
                nc.scalar.activation(rows[:], turned[:].rearrange("j (u e) p -> j u p e", e=2), ACT.Copy, scale=-1.0)
                h_rows[n].append(rows)

        def turn_back(n):
            words = new_bank([P, 2, 2, STEP], "bank_words", True)
            for step, rows in enumerate(h_rows[n]):
                row_words = rows[:].rearrange("j u p e -> j u (p e)").bitcast(F32)
                for u in range(2):
                    nc.tensor.transpose(words[:, step, u, :], row_words[:, u, :], identity)
            h_words = h_cols(n, 0, QUARTER).rearrange("p j t -> p (j t)").bitcast(F32)
            nc.scalar.copy(
                h_words.rearrange("p (step j u) -> p step j u", step=2, u=2),
                words[:].rearrange("p step u j -> p step j u"),
            )

        def round_wd(b, tag):
            grouped = kept([P, 2, 2, P, PACK], BF16, "wd_grouped%d" % b, tag=tag)
            for pair in PAIRS:
                for m0 in range(0, P, P // 2):
                    source = wd_raw[b][:, :, PACK * m0 : PACK * (m0 + P // 2)]
                    source = source.rearrange("p t (m pg) -> p m t pg", pg=PACK)
                    nc.scalar.copy(
                        grouped[:, pair, :, m0 : m0 + P // 2, :].rearrange("p side m t -> p m t side"),
                        source[:, :, :, 2 * pair : 2 * pair + 2],
                    )
            return grouped[:].rearrange("p pair side m t -> p pair (side m t)")

        def quantise_wd(pair, codes):
            plane = kept([P, PASS], U8, "wd_plane%d" % pair)
            for b in range(PASSES):
                cols = slice(2 * b * P, 2 * (b + 1) * P)
                nc.vector.quantize_mx(
                    out=codes[:, cols].bitcast(FP8X4), scales=plane[:, cols], in_=wd_grouped[b][:, pair]
                )
            wd_mx[pair] = codes, plane

        def projection(pg, half, slow):
            wd_codes, wd_plane = wd_mx[pg // 2]
            h_codes, h_plane = h_mx[half]
            bank = new_bank([P, HALF], "bank_y", slow)
            for b in range(PASSES):
                w_cols = slice((2 * b + pg % 2) * P, (2 * b + pg % 2 + 1) * P)
                j_cols = slice(b * HALF, (b + 1) * HALF)
                nc.tensor.matmul_mx(
                    out=bank[:],
                    lhsT=wd_codes[:, w_cols].bitcast(FP8X4), lhsT_scale=wd_plane[:, w_cols],
                    rhs=h_codes[:, j_cols].bitcast(FP8X4), rhs_scale=h_plane[:, j_cols],
                    start=(b == 0), stop=(b == PASSES - 1),
                )
            return bank

        y_tags = ["wc_raw0", "wc_raw1", "tab_bytes", "wa_raw0"]

        def copied_projection(pg, half):
            y = kept([P, HALF], F32, "y%d_%d" % (pg, half), tag=y_tags[pg])
            nc.scalar.copy(y[:], projection(pg, half, False)[:])
            return y

        def weighted_by_vector(pg, tag):
            weighted = kept([P, HALF], F32, "weighted%d" % pg, tag=tag)
            bank = projection(pg, 0, True)
            nc.vector.tensor_tensor(weighted[:], bank[:], wgo_sb[:, :HALF], ALU.mult)
            return weighted

        def window(pg, half):
            return pages[pg][:].indirect(offs2_sb[:, half * HALF // LIST_ROWS : (half + 1) * HALF // LIST_ROWS])

        both(gate_of, 0)
        gate_of(1, 0)
        tanh_of(0, 0, slow=True)
        both(linear_of, 0)
        tanh_of(0, 1, slow=True)
        gate_of(1, 1, slow=True)
        both(tanh_of, 1)
        both(linear_of, 1)
        both(difference, 0)
        multiply(0, from_c[0], gate[0], product_tile(0, group_shape, F32), [slice(2 * pair, 2 * pair + 2) for pair in PAIRS])
        both(difference, 1)
        both(tanh_of, 2)
        wide_linear_of(2, 0)
        both(gate_of, 2)
        wide_difference(2, 0)

        grouped = {}
        for pair in reversed(PAIRS):
            offset = FIRST_DIFFERENCE_AT + pair * GROUP_BYTES // 2
            tile = placed.tile(wb_pair_shape, BF16, name="wb_grouped1_%d" % pair, offset=offset, align_bytes=64)
            grouped[pair] = round_wb(1, pair, tile, *on_vector)
        for pair in reversed(PAIRS):
            quantise_wb(1, pair, grouped[pair], kept([P, 2 * P], U32, "wb_codes1_%d" % pair))
        product(1)
        interpolate(0)
        wide_linear_of(2, 1)

        for n in range(FIRST_OF_PASS_1, LAST_OF_HALF + 1):
            if n == FIRST_OF_PASS_1:
                both(gate_of, n)
            both(tanh_of, n)
            wide_linear_of(n, 0)
            if n != FIRST_OF_PASS_1:
                both(gate_of, n)
            wide_difference(n - 1, 1)
            product(n - 1)
            wide_difference(n, 0)
            if n == LAST_OF_HALF:
                both(linear_of, n - 2)
            interpolate(n - 2)
            wide_linear_of(n, 1)

        both(gate_of, LATE_A)
        both(gate_of, LATE_B)
        wd_grouped = [round_wd(b, tanh_tag(2, b)) for b in range(PASSES)]
        both(tanh_of, LATE_A)
        wide_difference(LAST_OF_HALF, 1)
        product(LAST_OF_HALF)
        for n in (LAST_OF_HALF - 1, LAST_OF_HALF):
            both(linear_of, n)
        interpolate(LAST_OF_HALF - 1)
        both(linear_of, LATE_A)
        both(linear_share, LATE_A)
        linear_of(LATE_B, 0)
        linear_share(LATE_B, 0)
        scaled = scaled_tanh(LATE_A)
        interpolate(LAST_OF_HALF)

        quantise_wd(0, placed.tile([P, PASS], U32, name="wd0_codes", offset=HALF_DIFFERENCE_AT, align_bytes=64))
        codes = kept([P, PASSES * HALF], U32, "h0_codes")
        plane = placed.tile([P, PASSES * HALF], U8, name="h0_plane", offset=HALF_DIFFERENCE_AT + 4 * PASS, align_bytes=64)
        for b in range(PASSES):
            cols = slice(b * HALF, (b + 1) * HALF)
            nc.vector.quantize_mx(
                out=codes[:, cols].bitcast(FP8X4), scales=plane[:, cols], in_=h_bf[0][:, b].rearrange("p j t -> p (j t)")
            )
        h_mx[0] = codes, plane
        quantise_wd(1, product_tile(LAST_OF_HALF, [P, PASS], U32))

        multiply(LATE_A, gate[LATE_A], scaled, kept(group_shape, F32, "product_late", tag=tanh_tag(2, 1)))
        both(tanh_of, LATE_B)
        linear_of(LATE_B, 1)
        linear_share(LATE_B, 1)
        weighted = weighted_by_vector(0, "wb_grouped0_0")
        scaled = scaled_tanh(LATE_B)
        multiply(LATE_B, gate[LATE_B], scaled, product_tile(LATE_B, group_shape, F32))
        nc.vector.tensor_copy(window(0, 0), weighted[:])

        both(gate_of, LAST)
        y = copied_projection(1, 0)
        weighted_by_gpsimd = kept([P, HALF], F32, "weighted1")
        nc.gpsimd.tensor_tensor(weighted_by_gpsimd[:], y[:], wgo_sb[:, :HALF], ALU.mult)
        both(linear_of, LAST)
        both(linear_share, LAST)
        both(tanh_of, LAST)
        weighted = weighted_by_vector(2, "wb_codes1_1")
        nc.vector.tensor_copy(window(2, 0), weighted[:])
        scaled = scaled_tanh(LAST)
        last_share = placed.tile([P, PACK, QUARTER], F32, name="last_share", offset=LAST_SHARE_AT)
        nc.gpsimd.tensor_tensor(last_share[:], gate[LAST][:], scaled[:], ALU.mult)
        nc.vector.tensor_copy(window(1, 0), weighted_by_gpsimd[:])

        sum_on_tensor(LATE_A, True)
        sum_on_tensor(LATE_B, False)
        for n in (LATE_A, LATE_B):
            turn_back(n)
        nc.gpsimd.tensor_tensor(
            woven(h_cols(LAST, 0, QUARTER)), by_twos(last_share[:]), by_twos(from_c[LAST][:]), ALU.subtract
        )

        y = placed.tile([P, GROUP_BYTES // 4], F32, name="y3_0", offset=LAST_Y_AT)[:, :HALF]
        nc.scalar.copy(y, projection(PACK - 1, 0, True)[:])
        h_mx[1] = quantise(h_bf[1][:].rearrange("p b j t -> p (b j t)"), "h1", "tab")
        nc.vector.tensor_tensor(window(PACK - 1, 0), y, wgo_sb[:, :HALF], ALU.mult)

        out_rows = out.rearrange("(p pg) c -> p pg c", pg=PACK)
        for pg in range(PACK):
            y = copied_projection(pg, 1)
            nc.vector.tensor_tensor(window(pg, 1), y[:], wgo_sb[:, HALF:], ALU.mult)
            nc.sync.dma_start(out_rows[:, pg, :], pages[pg][:])
